import numpy as np, ml_dtypes
CORES = [2,6,10,14,18,22,26,30]
N = 8
BF = ml_dtypes.bfloat16
def f(rng, *shape):
    return (rng.standard_normal(shape, dtype=np.float32) * np.exp2(rng.integers(-2, 3, shape[:-1] + (1,)))).astype(BF)
def wide(rng, *shape):
    v = f(rng, *shape).astype(np.float32); k = shape[:-2] + (1, shape[-1])
    return (v * np.exp2(rng.integers(-6, 7, k)) * (rng.random(k) > 0.0625)).astype(BF)
S, U, HB, M, CAP, TH, RO = 4096, 4096, 512, 256, 16, 8, 2
def stand(rng):
    birth = np.arange(U)[None, :] // HB; pw = rng.choice(np.array([0.7, 1.0, 1.4]), (8, 1))
    any_ = np.minimum((N * rng.random((8, U)) ** pw).astype(np.int64), N - 1)
    w = np.where(rng.random((8, U)) < 0.4, (birth + rng.integers(0, N, (8, 1))) % N, any_)
    return np.where(rng.random((8, U)) < 0.04, -1, w)
def fair(rng):
    w = np.zeros((8, U), np.int64)
    for g in range(8):
        for e in range(2): w[g, e + 2 * rng.permutation(U // 2)] = np.arange(U // 2) // (HB // 2)
    return w
def lay(rng, w):
    b = np.full((N, 8, S), U, np.int64)
    for g in range(8):
        for r in range(N):
            u = np.flatnonzero(w[g] == r); b[r, g, rng.permutation(S)[:len(u)]] = u
    return b
def squares(b):
    at = np.full((8, U), -1, np.int64)
    for g in range(8):
        for r in range(N):
            s = np.flatnonzero(b[r, g] < U); at[g, b[r, g, s]] = s
    return at
def homes(rng):
    return np.array(np.argsort(rng.random((8, N, S)), axis=-1)[..., :HB]).reshape(8, U)
def trade(c, i, s):
    x, y = int(c[i]), int(c[s]); c[i] = y; c[s] = x
def put(c, u, s):
    trade(c, int(np.flatnonzero(c == u)[0]), s)
def rehome(hm, g, u, s):
    lo = u // HB * HB; i = np.flatnonzero(hm[g, lo:lo + HB] == s)
    if len(i): hm[g, lo + int(i[0])] = hm[g, u]
    hm[g, u] = s
def ranks(v):
    return np.array(np.broadcast_to(np.asarray(v).reshape(-1, 128, U), (N, 128, U)))
def pack(b, xs, ds, hm):
    h = np.asarray(hm).astype(np.int32)
    return {"board": b.astype(np.int32), "xs": ranks(xs).astype(BF), "ds": ranks(ds).astype(np.int32), "hm": np.stack([h] * N)}
def setup_inputs(rng):
    b = lay(rng, stand(rng))
    return pack(b, f(rng, N, 128, U), rng.integers(0, S, (N, 128, U)), homes(rng))
def setup_inputs_spread(rng):
    b = lay(rng, stand(rng)); v = np.minimum(np.exp2(np.log2(S) * rng.random((N, 128, U))).astype(np.int64), S - 1)
    return pack(b, wide(rng, N, 128, U), np.where(rng.random((N, 128, U)) < 0.5, v, S - v), homes(rng))
def setup_inputs_ends(rng):
    w = fair(rng); b = np.full((N, 8, S), U, np.int64); top = np.zeros(8, np.int64)
    ds = (S - 1) * rng.integers(0, 2, (8, 16, U)) * (rng.random((8, 1, U)) > 0.125); kind = rng.choice(np.array([0, 1, 2, 3]), (8, U), p=np.array([0.3, 0.35, 0.2, 0.15]))
    for g in range(8):
        for u, r in ((0, g % N), (U - 1, (N + g - 8) % N)):
            v = int(np.flatnonzero((w[g] == r) & (np.arange(U) % 2 == u % 2))[0]); w[g, v] = w[g, u]; w[g, u] = r
        for r in range(N):
            u = np.flatnonzero(w[g] == r); e = int(np.max(u[u % 2 == 0])); o = int(np.max(u[u % 2 == 1]))
            c = np.concatenate([np.array([0, S // 8 - 1]), 1 + rng.permutation(S // 8 - 2)[:HB // 6 - 1]])
            cells = (8 * c[:, None] + np.arange(8)[None, :]).reshape(-1); cells = cells[(cells > 0) & (cells < S - 2)]
            rest = rng.permutation(u[(u != e) & (u != o)])
            b[r, g, rng.permutation(cells)[:len(rest)]] = rest; b[r, g, 0] = e; b[r, g, S - 1] = o
            kind[g, e] = 0; kind[g, o] = 1
            if r == g % N: top[g] = e
            for v in (e, o): ds[g, :, v] = 0; ds[g, 15, v] = S - 1
    order = np.argsort(np.argsort(rng.random((8, 16, U)), axis=1), axis=1)
    xs = np.where(order < np.array([16, 0, TH, TH - 1])[kind][:, None, :], 2.0 ** 20, -2.0 ** 20)
    pool = np.concatenate([np.arange(HB // 2), S - HB // 2 + np.arange(HB // 2)])
    hm = np.stack([np.concatenate([rng.permutation(pool) for p in range(N)]) for g in range(8)])
    for g in range(8):
        e = int(top[g]); lo = e // HB * HB; i = lo + int(np.flatnonzero(hm[g, lo:lo + HB] == S - 1)[0])
        hm[g, i] = hm[g, e]; hm[g, e] = S - 1
    return pack(b, xs, ds, hm)
def setup_inputs_corners(rng):
    xs = f(rng, 128, U).astype(np.float32).reshape(8, 16, U); ds = rng.integers(0, S, (8, 16, U)); hm = homes(rng); w = fair(rng)
    ds = np.where(rng.random(ds.shape) < 0.1, rng.choice(np.array([0, 1, S - 1, S // 2]), ds.shape), ds)
    gp = rng.permutation(8); off = int(rng.integers(0, 6)); ev = 2 * np.arange(U // 2); K = M // N
    pats = ([0, M + 1, M - 1], [1, M, M + 1], [0, M, M - 1], [M + 1, 1, M])
    for i in range(8):
        g = int(gp[i]); w[g, ev] = -1
        if i < 4:
            for p in range(N):
                u = p * HB + 2 * rng.permutation(HB // 2); w[g, u[:N * K]] = np.repeat(np.arange(N), K)
        else:
            c = list(pats[i - 4]); c = c + [(U // 2 - sum(c)) // (N - 3)] * (N - 3)
            w[g, rng.permutation(ev)[:sum(c)]] = np.repeat(rng.permutation(N), c)
    b = lay(rng, w); at = squares(b)
    for i in range(8):
        g = int(gp[i])
        if i < 4:
            for r in range(N):
                vic = rng.permutation(np.flatnonzero((w[g] == r) & (np.arange(U) % 2 == 1))); used = 0
                e = ev[w[g, ev] == r]; xs[g][:, e] = -64.0
                for p in range(N):
                    n = (0, 1, CAP - 1, CAP, CAP + 1, K)[(r + 2 * p + i + off) % 6]
                    a = rng.permutation(e[e // HB == p])[:n]; v = vic[used:used + n]; used += n
                    xs[g][:, a] = 64.0; ds[g, 0, a] = (at[g, v] - at[g, a]) & (S - 1)
        else:
            for p in range(N):
                u = np.arange(p * HB, (p + 1) * HB); own = u[w[g, u] == p]; oth = u[w[g, u] != p]
                left = rng.permutation(np.setdiff1d(np.arange(S), at[g, own]))
                hm[g, own] = at[g, own]; hm[g, oth] = left[:len(oth)]
    return pack(b, xs, ds, hm)
def setup_inputs_crowd(rng):
    xs = f(rng, 128, U).astype(np.float32).reshape(8, 16, U); ds = rng.integers(0, S, (8, 16, U)); hm = homes(rng); w = fair(rng)
    gp = rng.permutation(8); off = int(rng.integers(0, 6)); ev = 2 * np.arange(U // 2); od = ev + 1; K = M // N
    ga, gb, gc = int(gp[0]), int(gp[1]), int(gp[2]); o = [int(v) for v in rng.permutation(N)]; r0, r1, rd = o[0], o[1], o[2]
    w[ga, ev] = -1
    for i in (0, 2):
        w[ga, ev[ev // HB == o[i + 1]]] = o[i]; w[ga, od[w[ga, od] == o[i + 1]]] = o[i]
    w[ga, U - 1] = o[0]
    w[gb, ev] = -1
    for p in range(N):
        u = p * HB + 2 * rng.permutation(HB // 2)[:N * K]; w[gb, u] = np.repeat(np.arange(N), K)
    w[gc, od[w[gc, od] == r0]] = r1; w[gc, ev[w[gc, ev] == r1]] = r0
    z = rd * HB + 1 + 2 * int(rng.integers(0, HB // 2)); w[gc, z] = rd; w[gc, 0] = rd
    b = lay(rng, w); put(b[rd, gc], z, 0); put(b[rd, gc], 0, S - 1)
    for i in range(3, 8):
        for r in range(N):
            c = b[r, int(gp[i])]; mode = (i + r + off) % 6; place = (0, S - 1, S - 1, 0, S - 1, 0)[mode]
            u = rng.permutation(c[c < U]); e = u[u % 2 == 0]; v = u[u % 2 == 1]
            if mode < 2: put(c, int(v[0]), place)
            else: trade(c, int(rng.choice(np.flatnonzero(c == U))), place)
            if place > 0: put(c, int(e[0]), 0); put(c, int(e[1]), 1)
    at = squares(b)
    for i in range(3, 8):
        g = int(gp[i])
        for r in range(N):
            c = b[r, g]; mode = (i + r + off) % 6; place = (0, S - 1, S - 1, 0, S - 1, 0)[mode]
            u = c[c < U]; e = u[u % 2 == 0]; vic = rng.permutation(u[u % 2 == 1]); emp = rng.permutation(np.flatnonzero(c == U))
            if mode < 2: vic = np.concatenate([c[place:place + 1], vic[vic != c[place]]])
            else: emp = np.concatenate([np.array([place]), emp[emp != place]])
            j = int(rng.integers(2, M))
            if mode < 2:
                xs[g][:, e] = 64.0; to = np.full(len(e), at[g, vic[0]])
                if mode == 1: to[j] = at[g, vic[1]]
            elif mode < 4:
                xs[g][:, e] = -64.0; to = np.full(len(e), emp[0])
                if mode == 3: to[j] = emp[1]
            else:
                xs[g][:, e] = 64.0; v = vic[:len(e)]; to = at[g, v]; back = np.full(len(e), emp[0])
                if mode == 5: back[j] = emp[1]
                ds[g, 0, v] = (back - to) & (S - 1)
            ds[g, 0, e] = (to - at[g, e]) & (S - 1)
    for i in (0, 2):
        c = b[o[i], ga]; u = c[c < U]; e = u[u % 2 == 0]; v = rng.permutation(u[u % 2 == 1])
        if i == 0: v = np.concatenate([np.array([U - 1]), v[v != U - 1]]); rehome(hm, ga, int(e[0]), S - 2)
        v = v[:len(e)]; xs[ga][:, e] = 64.0; ds[ga, 0, e] = (at[ga, v] - at[ga, e]) & (S - 1)
        if i == 2: xs[ga][:, int(e[int(rng.integers(0, M))])] = -64.0
    for r in range(N):
        c = b[r, gb]; s = np.flatnonzero((c < U) & (c % 2 == 0)); e = c[s]; v = rng.permutation(c[(c < U) & (c % 2 == 1)])[:len(e)]
        xs[gb][:, e] = 64.0; ds[gb, 0, e] = (at[gb, v] - s) & (S - 1)
        u = np.arange(r * HB, (r + 1) * HB); m = (u % 2 == 0) & (w[gb, u] >= 0)
        hm[gb, u[m]] = rng.permutation(s); hm[gb, u[~m]] = rng.permutation(np.setdiff1d(np.arange(S), s))[:HB - len(s)]
    c = b[r0, gc]; e = c[c < U]; xs[gc][:, ev] = -64.0
    ds[gc, 0, e] = (int(rng.choice(np.flatnonzero(c == U))) - at[gc, e]) & (S - 1)
    xs[gc][:, 0] = 64.0; xs[gc][:, z] = 128.0; ds[gc, :, 0] = 0; ds[gc, :, z] = S - 1; rehome(hm, gc, z, 0)
    return pack(b, xs, ds, hm)
def setup_inputs_heap(rng):
    w = np.tile(((np.arange(8) + int(rng.integers(0, N))) % N)[:, None], (1, U))
    xs = rng.integers(-2, 3, (N, 128, U)).astype(np.float32) * rng.choice(np.array([-1.0, 1.0], np.float32), (N, 128, U))
    return pack(lay(rng, w), xs, rng.integers(0, S, (N, 128, U)), homes(rng))
def check_inputs(d):
    bad = []
    for k, lo, hi in (("board", 0, U), ("ds", 0, S - 1), ("hm", 0, S - 1)):
        if np.min(d[k]) < lo or np.max(d[k]) > hi: bad.append("range of " + k)
    v = np.abs(np.asarray(d["xs"]).astype(np.float32))
    if not np.all((v == 0) | ((v >= 2.0 ** -100) & (v <= 2.0 ** 20))): bad.append("range of xs")
    b = np.asarray(d["board"]).astype(np.int64); h = np.asarray(d["hm"]).astype(np.int64)
    if not np.all(h == h[:1]): bad.append("ranks alike in hm")
    for g in range(8):
        v = b[:, g].reshape(-1); v = v[v != U]
        if len(np.unique(v)) != len(v): bad.append("units of board stand once (group " + str(g) + ")")
    for q in range(h.shape[0]):
        v = np.sort(h[q].reshape(8, N, HB), axis=-1)
        if np.any(v[..., 1:] == v[..., :-1]): bad.append("distinct homes in hm (rank " + str(q) + ")")
    return bad
def first_of(keys, ok):
    w = np.zeros(len(keys), bool); i = np.flatnonzero(ok); u, at = np.unique(keys[i], return_index=True); w[i[at]] = True
    return w
def reference(board, xs, ds, hm):
    bd = np.array(board).astype(np.int64)
    x = np.asarray(xs).astype(np.float32).reshape(N, 8, 16, U); d = np.asarray(ds).astype(np.int64).reshape(N, 8, 16, U); home = np.asarray(hm).astype(np.int64)
    for t in range(RO):
        new = np.array(bd); born = []
        for r in range(N):
            for g in range(8):
                c = bd[r, g]; X = x[r, g]; D = d[r, g]
                s = np.flatnonzero((c < U) & ((c & 1) == (t & 1)))[:M]; a = c[s]; n = len(a); j = np.arange(n)
                if n == 0: continue
                q = (s[None, :] + D[:, a]) & (S - 1)
                v = c[q]; more = np.add.reduce((X[:, a][:, None, :] > X[:, np.minimum(v, U - 1)]).astype(np.int64), axis=0)
                can = (v < U) & ((v & 1) != (t & 1)) & (more >= TH)
                claim = np.any(can, axis=0); sq = q[np.argmax(can, axis=0), j]
                won = first_of(sq, claim)
                at = np.where(won, sq, s); who = np.where(won, c[sq], a)
                w = (at[None, :] + D[:, np.minimum(who, U - 1)]) & (S - 1)
                free = c[w] == U; to = w[np.argmax(free, axis=0), j]
                go = first_of(to, np.any(free, axis=0) & (won | ~claim))
                new[r, g, s] = U; new[r, g, sq[won]] = U; new[r, g, np.where(go, to, at)] = a
                for p in range(N):
                    i = np.flatnonzero(won & (a // HB == p))[:CAP]
                    born.append((p, g, home[r, g, a[i]], c[sq[i]]))
        for p, g, h, b in born:
            e = new[p, g, h] == U; new[p, g, h[e]] = b[e]
        bd = new
    return {"y": bd.astype(np.float32)}

@@ -1,0 +1,683 @@
+import math
+import numpy as np
+from concourse.bass import DstId, RemoteDMATransfer
+from concourse.mybir import AluOpType as A
+from concourse.mybir import ActivationFunctionType as F
+
+N = 8
+S = 4096
+RO = 2
+BW = 4608
+PWW = 2304
+PARTS = [(0, 128), (128, 256)]
+PARTS2 = [(0, 256)]
+CH = 32
+DLAT, WAKE = 2000.0, 100.0
+MODELS = [dict(far=5000.0, pe=0.55, cy=1.04, ga=1.55, sc=3.8, wake=100.0, bpn=250.0),
+          dict(far=3000.0, pe=0.45, cy=0.85, ga=1.1, sc=2.0, wake=50.0, bpn=350.0),
+          dict(far=8000.0, pe=1.1, cy=1.2, ga=2.0, sc=5.5, wake=150.0, bpn=200.0),
+          dict(far=5000.0, pe=1.0, cy=1.0, ga=1.2, sc=5.0, wake=40.0, bpn=300.0),
+          dict(far=5000.0, pe=0.5, cy=1.0, ga=2.0, sc=2.0, wake=200.0, bpn=250.0)]
+
+
+def _sb(n, d):
+    return ("sbuf", [128, n], d)
+
+
+SCRATCH = {
+    "dsb": _sb(4104, "int32"), "xsb": _sb(4112, "bfloat16"), "hmb": _sb(512, "int32"),
+    "bufi": ("sbuf", [128, 2, 128], "int32"), "buff": ("sbuf", [128, 2, 128], "float32"),
+    "bd": _sb(BW, "float32"), "XB": _sb(S, "bfloat16"), "xv": _sb(S, "bfloat16"), "cmp": _sb(S, "bfloat16"),
+    "fr": _sb(S, "bfloat16"), "E": _sb(4352, "bfloat16"),
+    "PW0": _sb(PWW, "float32"), "PW1": _sb(PWW, "float32"), "land0": _sb(128, "float32"), "land1": _sb(128, "float32"),
+    "WR": _sb(2048, "bfloat16"), "TR": _sb(2048, "bfloat16"), "LL": _sb(2048, "bfloat16"),
+    "BLK": _sb(128, "bfloat16"), "K0": _sb(128, "bfloat16"), "TRI": _sb(128, "bfloat16"), "UP": _sb(128, "bfloat16"),
+    "DW": _sb(128, "bfloat16"), "B16": _sb(128, "bfloat16"), "NI": _sb(128, "bfloat16"), "tm": _sb(128, "bfloat16"),
+    "HB": _sb(128, "bfloat16"), "neg": _sb(256, "float32"),
+    "grp": _sb(128, "float32"), "lo1": _sb(128, "float32"), "pci": _sb(8, "int32"), "col": _sb(16, "float32"),
+    "clt": _sb(16, "float32"), "dwr": _sb(16, "float32"), "i16": _sb(16, "float32"),
+    "M16f": _sb(256, "float32"), "M1": _sb(256, "float32"), "MW": _sb(256, "float32"), "j16": _sb(256, "bfloat16"),
+    "keep": _sb(256, "bfloat16"), "MK": _sb(256, "bfloat16"), "sg": _sb(256, "bfloat16"), "C1": _sb(256, "bfloat16"),
+    "c256": _sb(272, "bfloat16"), "ones": _sb(256, "bfloat16"), "c4096": _sb(256, "float32"),
+    "Bw": _sb(256, "float32"), "Bi": _sb(256, "int32"), "X": _sb(256, "int32"), "f": _sb(272, "bfloat16"),
+    "ox": _sb(256, "float32"), "xo": _sb(256, "uint16"), "Bo": _sb(272, "float32"),
+    "cum": _sb(288, "bfloat16"), "G": _sb(272, "float32"), "L2": _sb(24, "float32"),
+    "T1": _sb(256, "bfloat16"), "T2": _sb(256, "bfloat16"), "OH": _sb(256, "bfloat16"),
+    "Zu": _sb(512, "float16"), "Z": _sb(512, "float16"), "Zp": _sb(512, "float16"),
+    "u16": _sb(256, "uint16"), "w32": _sb(256, "float32"), "wi": _sb(32, "int32"),
+    "srep": _sb(256, "float32"), "arep": _sb(256, "float32"), "absb": _sb(256, "float32"), "atrep": _sb(256, "float32"),
+    "t": _sb(512, "int32"), "q": _sb(512, "int32"), "q16": _sb(512, "uint16"), "qo": _sb(512, "float16"),
+    "so": _sb(256, "float16"), "A1": _sb(256, "bfloat16"), "hmf": _sb(512, "float32"), "NB": _sb(128, "bfloat16"),
+    "ID": _sb(128, "bfloat16"), "dm": _sb(256, "bfloat16"), "xa": _sb(256, "bfloat16"),
+    "good": _sb(256, "bfloat16"), "who": _sb(256, "float16"), "whom": _sb(256, "float32"), "hg": _sb(256, "float32"),
+    "key": _sb(512, "float16"), "fl": _sb(256, "bfloat16"),
+    "h16": _sb(128, "float16"), "em": _sb(128, "float32"), "old": _sb(128, "float32"), "dd": _sb(128, "float32"),
+}
+for _b in range(8):
+    SCRATCH["p%d" % _b] = ("psum", [128, 512], "float32")
+SEMAPHORES = ["V", "S", "P", "G", "arr0", "arr1", "snt0", "snt1", "dB", "dX", "dD", "dR", "dH", "dF", "dY0", "dY1"]
+
+
+def masks_from(src, cores, topo):
+    peers = [c for c in cores if c != src]
+    off = [c for c in peers if topo.chip(c) != topo.chip(src)]
+    on = [c for c in peers if topo.chip(c) == topo.chip(src)]
+    near = lambda c: topo.mates(topo.chip(c), topo.chip(src)) or topo.same_plane(topo.chip(c), topo.chip(src))
+    off = sorted(off, key=near)
+    eng = list(topo.engines(src, off[0]))
+    out = {}
+    spare = len(eng) - len(off)
+    at = 0
+    for i, c in enumerate(off):
+        n = 2 if i < spare else 1
+        out[c] = eng[at:at + n]
+        at += n
+    for i, c in enumerate(on):
+        rest = [e for e in topo.engines(src, c) if e not in eng]
+        out[c] = rest[i:i + 1]
+    return out
+
+
+def psum(name):
+    return name in SCRATCH and SCRATCH[name][0] == "psum"
+
+
+def schedule(ops):
+    n = len(ops)
+    pred = [dict() for _ in range(n)]
+    hist, lastq = {}, {}
+    for j, o in enumerate(ops):
+        q = o["alts"][0][0]
+        for regs, writes in ((o["rd"], False), (o["wr"], True)):
+            for (name, lo, hi) in regs:
+                for (i, l2, h2, w2) in hist.get(name, []):
+                    if l2 < hi and lo < h2 and (w2 or writes) and not (o["sem"] and ops[i]["sem"] == o["sem"]):
+                        pred[j][i] = True
+                if q == "P" and psum(name) and writes:
+                    if name in lastq:
+                        pred[j].setdefault(lastq[name], False)
+                    lastq[name] = j
+        if o["keep"]:
+            if q in lastq:
+                pred[j].setdefault(lastq[q], False)
+            lastq[q] = j
+        for regs, writes in ((o["rd"], False), (o["wr"], True)):
+            for (name, lo, hi) in regs:
+                h = hist.setdefault(name, [])
+                if writes:
+                    h[:] = [e for e in h if not (lo <= e[1] and e[2] <= hi and ops[e[0]]["sem"] != o["sem"] or
+                                                 lo <= e[1] and e[2] <= hi and not o["sem"])]
+                h.append((j, lo, hi, writes))
+    succ = [[] for _ in range(n)]
+    for j in range(n):
+        for i in pred[j]:
+            succ[i].append(j)
+    tail = [0.0] * n
+    nxt = {}
+    for j in range(n - 1, -1, -1):
+        pe = ops[j]["alts"][0][0] == "P"
+        tail[j] = ops[j]["alts"][0][2] + ops[j]["lat"] + max(
+            [0.0] + [tail[i] + (0.0 if pe and ops[i]["alts"][0][0] == "P" else WAKE) for i in succ[j]])
+        name = ops[j]["wr"][0][0] if ops[j]["wr"] else None
+        if name in CHAIN:
+            if name in nxt:
+                tail[j] = max(tail[j], CHAIN[name] * ops[j]["alts"][0][2] + tail[nxt[name]])
+            nxt[name] = j
+    kinds = {}
+    seen = {}
+    for j, o in enumerate(ops):
+        name, lo = o["wr"][0][:2] if o["wr"] else ("", 0)
+        lo = lo % 256 if name == "cmp" else 0 if name in ("E", "WR", "TR", "LL", "Bw") else lo
+        k = (name, lo, o["rd"][-1][0] if o["rd"] else "")
+        seen[j] = kinds.setdefault(k, len(kinds))
+    for j in range(n):
+        pred[j] = [(i, raw) for i, raw in pred[j].items()
+                   if not (ops[i]["keep"] and ops[j]["keep"] and not raw and ops[i]["sem"]
+                           and ops[i]["alts"][0][0] == ops[j]["alts"][0][0])] , len(pred[j])
+    return pred, succ, tail, seen, len(kinds)
+
+
+def replay(ops, pred, order, m):
+    wake = m["wake"]
+    free, done, on, bank, df = {}, [0.0] * len(ops), [None] * len(ops), {}, 0.0
+    for j, a in order:
+        o = ops[j]
+        q, call, c = o["alts"][a]
+        s = free.get(q, 0.0)
+        for i, raw in pred[j][0]:
+            d = done[i] + (0.0 if on[i] == q and not ops[i]["sem"] and (q == "P" or not raw) else wake)
+            if d > s:
+                s = d
+        for b in o["banks"]:
+            if b in bank and bank[b][0] != q and bank[b][1] + wake > s:
+                s = bank[b][1] + wake
+        on[j] = q
+        free[q] = s + c
+        done[j] = s + c + o["lat"]
+        if o["bytes"]:
+            df = max(df, s + c + 0.6 * DLAT) + o["bytes"] / m["bpn"]
+            done[j] = df + 0.4 * DLAT
+        for b in o["banks"]:
+            bank[b] = (q, done[j])
+    return max(done)
+
+
+def plan(builds):
+    ops = builds[0]
+    pred, succ, tail, kind, kinds = schedule(ops)
+    rng = np.random.default_rng(SEED)
+
+    def trial(bias):
+        order = greedy(ops, pred, succ, [tail[j] + bias[kind[j]] for j in range(len(ops))])
+        t = [replay(b, pred, order, m) for b, m in zip(builds, MODELS)]
+        return sum(math.log(x) for x in t) + math.log(t[0]), order, t
+    bias = [0.0] * kinds
+    best = trial(bias)
+    for _ in range(ROUNDS):
+        c = list(bias)
+        for _i in range(int(rng.choice([1, 2, 3, 5, 8]))):
+            c[int(rng.integers(kinds))] += float(rng.choice([-1, 1]) * rng.choice([200, 500, 1000, 2000, 4000]))
+        r = trial(c)
+        if r[0] <= best[0]:
+            best, bias = r, c
+    SPAN[:] = best[2]
+    return best[1]
+
+
+def greedy(ops, pred, succ, tail):
+    n = len(ops)
+    WAKE, BPN = MODELS[0]["wake"], MODELS[0]["bpn"]
+    left = [p[1] for p in pred]
+    ready = [j for j in range(n) if left[j] == 0]
+    free, done, on, bank = {}, [0.0] * n, [None] * n, {}
+    dmafree = [0.0]
+    order = []
+    base = {}
+
+    def start(j, q):
+        if (j, q) not in base:
+            s = 0.0
+            for i, raw in pred[j][0]:
+                s = max(s, done[i] + (0.0 if on[i] == q and not ops[i]["sem"] and (q == "P" or not raw) else WAKE))
+            base[(j, q)] = s
+        s = max(base[(j, q)], free.get(q, 0.0))
+        for b in ops[j]["banks"]:
+            if b in bank and bank[b][0] != q:
+                s = max(s, bank[b][1] + WAKE)
+        return s
+    while ready:
+        best = None
+        byq = {}
+        for j in ready:
+            for alt, (q, call, cost) in enumerate(ops[j]["alts"]):
+                byq.setdefault(q, []).append((j, start(j, q), cost, alt))
+        for q, c in byq.items():
+            c.sort(key=lambda e: -tail[e[0]])
+            top = c[0]
+            for e in c[1:]:
+                if e[1] < top[1]:
+                    a = max(top[1] + tail[top[0]], top[1] + top[2] + tail[e[0]])
+                    b = max(e[1] + tail[e[0]], max(top[1], e[1] + e[2]) + tail[top[0]])
+                    if b <= a + SLACK:
+                        top = e
+                        break
+            if best is None or top[1] < best[1][1]:
+                best = (q, top)
+        q, (j, s, cost, call) = best
+        on[j] = q
+        free[q] = s + cost
+        done[j] = s + cost + ops[j]["lat"]
+        if ops[j]["bytes"]:
+            dmafree[0] = max(dmafree[0], s + cost + 0.6 * DLAT) + ops[j]["bytes"] / BPN
+            done[j] = dmafree[0] + 0.4 * DLAT
+        for b in ops[j]["banks"]:
+            bank[b] = (q, done[j])
+        order.append((j, call))
+        ready.remove(j)
+        for i in succ[j]:
+            left[i] -= 1
+            if left[i] == 0:
+                ready.append(i)
+    return order
+
+
+SLACK = 150.0
+SPAN = []
+ORDER = []
+SEED = 1
+ROUNDS = 1200
+CHAIN = {"xv": 0.5, "cmp": 1.0, "fr": 0.6, "E": 1.0, "XB": 0.7, "WR": 1.0, "TR": 1.0, "LL": 1.0}
+
+
+def build(g, core, T, topo, m):
+    rank = T.rank_of(core)
+    cores = list(T.cores)
+    ops = []
+    CY, PEC, GA, SC, FAR, BPN = m["cy"], m["pe"], m["ga"], m["sc"], m["far"], m["bpn"]
+
+    def R(name, lo=0, hi=None, step=1, at=None):
+        if hi is None:
+            hi = SCRATCH[name][1][1]
+        a = lo if at is None else at
+        ap = T[name][:, a:hi] if step == 1 else T[name][:, a:hi:step]
+        return (ap, [(name, lo, hi)], [], len(range(a, hi, step)), name, False)
+
+    def W(name, ap, n=256):
+        return (ap, [(name, 0, 1 << 20)], [], n, name, False)
+
+    def IND(win, off):
+        return (win[0].indirect(off[0]), win[1], off[1], 16 * off[3], win[4], True)
+
+    def put(alts, outs, ins, sem=None, cnt=1, lat=0.0, nbytes=0, keep=False):
+        rd, wr = [], []
+        for x in ins:
+            if isinstance(x, tuple):
+                rd += x[1] + x[2]
+        for x in outs:
+            wr += x[1]
+            rd += x[2]
+        ops.append({"alts": alts, "rd": rd, "wr": wr, "sem": sem, "cnt": cnt, "lat": lat, "bytes": nbytes, "keep": keep,
+                    "banks": set(r[0] for r in rd + wr if psum(r[0]))})
+
+    def ap(x):
+        return x[0] if isinstance(x, tuple) else x
+
+    def cost(o, i, per, fix=50.0):
+        if o[5]:
+            return fix + o[3] * SC * CY
+        if i[5]:
+            return fix + i[3] * GA * CY
+        return max(64.0, i[3] * per) * CY
+
+    def half(*xs):
+        return 0.5 if all(SCRATCH[x[4]][2] in ("bfloat16", "float16", "uint16") for x in xs) else 1.0
+
+    def a_cp(o, i):
+        return ("V", lambda: g.vector.tensor_copy(o[0], i[0]), cost(o, i, half(o, i)))
+
+    def a_ts(o, a, s1, op0, s2=None, op1=None):
+        if op1 is None:
+            return ("V", lambda: g.vector.tensor_scalar(o[0], a[0], ap(s1), None, op0), cost(o, a, half(o, a)))
+        return ("V", lambda: g.vector.tensor_scalar(o[0], a[0], ap(s1), ap(s2), op0, op1), cost(o, a, half(o, a)))
+
+    def a_act(o, i, func, bias=0.0, scale=1.0):
+        if o[5]:
+            return ("S", lambda: g.scalar.activation(o[0], i[0], func), cost(o, i, 1.0, 65.0))
+        return ("S", lambda: g.scalar.activation(o[0], i[0], func, bias=ap(bias), scale=ap(scale)), cost(o, i, 1.0, 65.0))
+
+    def cp(o, i):
+        put([a_cp(o, i)], [o], [i])
+
+    def tt(o, a, b, op):
+        put([("V", lambda: g.vector.tensor_tensor(o[0], a[0], b[0], op),
+              cost(o, a, 1.0 if psum(a[4]) or psum(b[4]) else 2.0))], [o], [a, b])
+
+    def ts(o, a, s1, op0, s2=None, op1=None):
+        put([a_ts(o, a, s1, op0, s2, op1)], [o], [a, s1, s2])
+
+    def scan(o, a, b, init, op0, op1):
+        put([("V", lambda: g.vector.tensor_tensor_scan(o[0], a[0], b[0], ap(init), op0, op1), cost(o, a, 1.0))],
+            [o], [a, b, init])
+
+    def ms(o, c):
+        put([("V", lambda: g.vector.memset(o[0], c), cost(o, o, half(o)))], [o], [])
+
+    def act(o, i, func, bias=0.0, scale=1.0):
+        put([a_act(o, i, func, bias, scale)], [o], [i, bias, scale])
+
+    def lin(o, i, scale, bias):
+        put([a_act(o, i, F.Identity, bias, scale), a_ts(o, i, scale, A.mult, bias, A.add)], [o], [i, scale, bias])
+
+    def gather(o, i):
+        put([a_act(o, i, F.Copy), a_cp(o, i)], [o], [i])
+
+    def mm(o, l, r, start, stop):
+        put([("P", lambda: g.tensor.matmul(o[0], l[0], r[0], start, stop), max(64, r[3]) * PEC)], [o], [l, r])
+
+    def iota(o, pat, base, ch, flt=True):
+        if flt:
+            call = lambda: g.iota(o[0], pat, base, ch, allow_small_or_imprecise_dtypes=True)
+        else:
+            call = lambda: g.iota(o[0], pat, base, ch)
+        put([("G", call, 130.0 + 2 * o[3] * CY)], [o], [], keep=True)
+
+    def dma(o, i, q, sem, nbytes):
+        eng = g.sync if q == "Y" else g.scalar
+        put([(q, lambda: eng.dma_start(o[0], i[0]), 60.0)], [o], [i], sem, 16, DLAT + nbytes / BPN, nbytes, q == "Y")
+
+    def mat(name, r):
+        return R(name, 128 * r, 128 * r + 128)
+
+    def wrap(o, name, lo, hi):
+        for r in range(16):
+            mm(o, mat("WR", r), R(name, lo, hi, 16, lo + r), r == 0, r == 15)
+
+    def col(j):
+        return R("col", j, j + 1)
+
+    def ext(t, name="hbm"):
+        return (t, [] if name == "hbm" else [(name, 0, S)], [], 0, name, False)
+
+    PG, PI, PI1, M0, MH, AB, ZI = 0, 1, 2, 3, 4, 5, 6
+    U_C1, U_C, U_A, U_A9, U_S, U_AT, U_W, U_P, U_FB, U_E, U_H, U_L = [16 * i for i in range(12)]
+    W_C1, W_C, W_X, W_S, W_AT, W_D, W_FB, W_K, W_Y, W_E, W_P, W_C16, W_X2, W_D2, W_Y2 = [16 * i for i in range(15)]
+
+    def u(c, lo=0, hi=256):
+        return R("u16", c + lo // 16, c + hi // 16)
+
+    def w(c, lo=0, hi=256):
+        return R("w32", c + lo // 16, c + hi // 16)
+
+    for y in range(2):
+        dma(W("bufi", T.bufi[:, y, :]), ext(T.board[y:8:2, :]), "Y", "dB", 65536)
+    dma(R("xsb", 0, S), ext(T.xs[:, :]), "Y", "dX", 1 << 20)
+    dma(R("dsb", 0, S), ext(T.ds[:, :]), "Y", "dD", 1 << 21)
+    iota(R("pci", 0, 1), [[0, 1]], 0, 1, False)
+    iota(R("grp"), [[1, 8], [0, 16]], 0, 0)
+    iota(R("lo1"), [[0, 8], [1, 16]], 1, 0)
+    iota(R("i16"), [[1, 16]], 0, 0)
+    iota(R("MW"), [[16, 16], [0, 16]], 0, 0)
+    iota(R("j16"), [[0, 16], [1, 16]], 0, 0)
+    iota(R("M16f"), [[16, 256]], 0, 0)
+    iota(R("M1"), [[1, 256]], 512, 0)
+    iota(R("bd"), [[0, BW]], 0, 0)
+    iota(R("hmb"), [[0, 512]], 0, 0, False)
+    for t in range(RO):
+        for p in range(N):
+            z = 256 * (p if p < 4 else p + 1)
+            iota(R("PW%d" % t, z, z + 16), [[2, 16]], 4352 + 32 * rank, 0)
+    ms(R("c256"), 256.0)
+    ms(R("cum", 0, 16), 0.0)
+    ms(R("f", 256, 272), 1.0)
+    ms(R("Bo", 256, 272), 0.0)
+    ms(R("xsb", S, S + 16), 1e29)
+    ms(R("dsb", S, S + 8), 0)
+    ms(R("L2", 16, 24), 0.0)
+    ms(R("ones"), 1.0)
+    ts(R("pci", 2, 3), R("pci", 0, 1), 4, A.arith_shift_right)
+    ts(R("pci", 4, 5), R("pci", 0, 1), 15, A.bitwise_and)
+    cp(col(PG), R("pci", 2, 3))
+    cp(col(PI), R("pci", 4, 5))
+    ts(R("BLK"), R("grp"), col(PG), A.is_equal)
+    ts(col(PI1), col(PI), 1.0, A.add)
+    tt(R("K0"), R("BLK"), R("lo1"), A.mult)
+    ts(col(M0), col(PI), 0.0, A.is_equal)
+    ts(R("NI"), R("K0"), col(PI1), A.is_equal, -1.0, A.mult)
+    ts(R("tm"), R("K0"), col(PI1), A.is_gt)
+    ts(R("clt"), R("i16"), col(PI), A.is_gt)
+    ts(R("UP"), R("NI"), -512.0, A.mult)
+    ts(col(AB), col(PI), -512.0, A.mult, 2048.0 - 255.5, A.add)
+    tt(R("UP"), R("UP"), R("tm"), A.add)
+    ts(col(8), col(PI), 16.0, A.mult, 15.0, A.add)
+    ts(u(U_L), R("i16"), 0.0, A.mult, col(8), A.add)
+    lin(R("MW"), R("MW"), 1.0, col(PI))
+    ts(R("keep"), R("j16"), 1.0, A.min)
+    ts(R("MK"), R("j16"), col(PI), A.is_equal, 1.0, A.subtract)
+    lin(R("DW"), R("BLK"), col(PI), 0.0)
+    lin(R("B16"), R("BLK"), 16.0, 0.0)
+    lin(R("NB"), R("BLK"), -1.0, 0.0)
+    lin(R("ID"), R("NI"), -1.0, 0.0)
+    lin(R("HB"), R("BLK"), 1.0 / 32, 0.0)
+    for r in range(1, 16):
+        lin(mat("LL", r), R("BLK"), R("clt", r, r + 1), 0.0)
+    for k in range(16):
+        act(mat("TR", k), R("K0"), F.Relu, bias=-0.5 * k, scale=0.5)
+    for r in range(16):
+        ts(mat("WR", r), R("K0"), float(r + 1), A.is_equal)
+    ts(R("TRI"), R("K0"), col(PI), A.subtract, 0.0, A.max)
+    ts(col(MH), col(PI), float(2 * rank + 1), A.is_equal)
+    ts(col(ZI), col(PI), 3.5, A.is_gt, 256.0, A.mult)
+    ts(R("dwr"), R("i16"), 16.0, A.mult, col(PI), A.add)
+    ts(col(ZI + 1), col(PI), 256.0, A.mult, -1024.0, A.add)
+    ts(R("dwr"), R("dwr"), 1024.0, A.add)
+    tt(col(ZI), col(ZI), col(ZI + 1), A.add)
+    lin(R("c4096"), R("M16f"), 0.0, float(S))
+    lin(R("neg"), R("M16f"), 0.0, -200.0)
+    put([("G", lambda: g.dma_start(T.y[:, :], T.c4096[:, :]), 500.0)], [ext(None, "y")], [R("c4096")], "dY0", 16, DLAT,
+        keep=True)
+    ts(W("buff", T.buff[:, :, :]), W("bufi", T.bufi[:, :, :]), float(S), A.subtract)
+    for y in range(2):
+        dma(ext(T.bd[16 * y:128:32, 0:S], "bd"), W("buff", T.buff[:, y, :]), "Y", "dR", 65536)
+    dma(ext(T.hmb[1:128:2, :], "hmb"), ext(T.hm[:, :]), "Y", "dH", 131072)
+    cp(R("hmf"), R("hmb"))
+
+    bdw = R("bd")
+
+    def targets(lst, base, lo, hi, o):
+        tt(R("t", o + lo, o + hi), IND(R("dsb"), u(lst, lo, hi)), R(base, lo, hi), A.add)
+        ts(R("q", o + lo, o + hi), R("t", o + lo, o + hi), S - 1, A.bitwise_and)
+        cp(R("q16", o + lo, o + hi), R("q", o + lo, o + hi))
+        ts(R("qo", o + lo, o + hi), R("q16", o + lo, o + hi), 2048.0, A.subtract)
+
+    def pick(base, lo, hi, o, wb, wx, wk):
+        n = hi - lo
+        z1, z2 = R("Z", 2 * lo, 2 * lo + n), R("Z", 2 * lo + n, 2 * hi)
+        tt(z1, R("p2", 256 + lo, 256 + hi), R("qo", o + lo, o + hi), A.mult)
+        tt(z2, R("p2", 256 + lo, 256 + hi), R(base, lo, hi), A.mult)
+        wrap(R("p3", lo // 8, hi // 8), "Z", 2 * lo, 2 * hi)
+        mm(R("p5", lo, hi), R("ID"), R(base, lo, hi), True, False)
+        mm(R("p5", lo, hi), R("BLK"), z1, False, False)
+        mm(R("p5", lo, hi), R("NB"), z2, False, True)
+        if o == 0:
+            mm(R("p6", lo, hi), R("BLK"), z1, True, False)
+            mm(R("p6", lo, hi), R("NB"), z2, False, True)
+        tt(w(wx, lo, hi), R("p3", lo // 8, lo // 8 + n // 16), w(wb, lo, hi), A.add)
+        tt(w(wk, lo, hi), w(wx, lo, hi), R("p3", lo // 8 + n // 16, hi // 8), A.subtract)
+        cp(R("key", o + lo, o + hi), R("p5", lo, hi))
+
+    def dedupe(kw, o):
+        mm(R("p7", 0, 256), R("BLK"), R("dm"), True, False)
+        for c in range(16):
+            ts(R("E", 272 * c, 256 * c + 256), R("key", o + 16 * c, o + 256), 2048.0, A.add, R("w32", kw + c, kw + c + 1), A.is_equal)
+            if c < 15:
+                mm(R("p7", 16 * c + 16, 256), R("BLK"), R("E", 272 * c + 16, 256 * c + 256), False, False)
+        for r in range(1, 16):
+            mm(R("p7", r, 256, 16), mat("LL", r), R("E", 0, 4352, 272, r), False, r == 15)
+
+    for t in range(RO):
+        PW = "PW%d" % t
+        land = "land%d" % t
+        for b in range(8):
+            put([("V", (lambda b: lambda: g.vector.transpose(T.Bw[:, b:256:8], T.buff[:, :, 16 * b:16 * b + 16]))(b), 64 * CY)],
+                [R("Bw", 32 * b, 32 * b + 32)], [W("buff", None)])
+        ts(R("Bi"), R("Bw"), float(S), A.add)
+        lin(R("Bo", 0, 256), R("Bw"), 1.0, 2048.0)
+        ts(R("X"), R("Bi"), 4097, A.bitwise_and)
+        ts(R("f", 0, 256), R("X"), float(t), A.is_equal)
+        mm(R("p0", 0, 272), R("BLK"), R("f"), True, True)
+        mm(R("p1", 0, 272), R("UP"), R("f"), True, False)
+        ts(R("p2", 256, 512), R("X"), float(1 - t), A.not_equal, float(S), A.mult)
+        scan(R("cum", 16, 288), R("p0", 0, 272), R("c256"), 0.0, A.add, A.min)
+        wrap(R("p4", 0, 17), "cum", 16, 288)
+        tt(R("ox"), R("p2", 256, 512), R("Bw"), A.add)
+        ts(R("xo"), R("ox"), 0.0, A.min, float(S), A.add)
+        for c in range(0, 256, CH):
+            gather(R("XB", 16 * c, 16 * (c + CH)), IND(R("xsb"), R("xo", c, c + CH)))
+        tt(R("T1"), IND(R("cum", 16, 288), u(U_L)), R("MW"), A.is_le)
+        scan(R("sg"), R("keep"), R("T1"), 0.0, A.mult, A.add)
+        lin(R("L2", 0, 17), R("p4", 0, 17), 1.0, 0.0)
+        mm(R("p1", 0, 272), R("ID"), R("cum", 15, 287), False, True)
+        lin(R("G"), R("p1", 0, 272), 1.0, 0.0)
+        cp(u(U_C1), R("sg", 0, 256, 16, 15))
+        ts(w(W_C1), R("sg", 0, 256, 16, 15), 16.0, A.mult)
+        tt(R("T2"), IND(R("L2"), u(U_C1)), R("M16f"), A.is_le)
+        gather(R("C1"), IND(R("M16f", 0, 24), u(U_C1)))
+        wrap(R("p4", 32, 48), "T2", 0, 256)
+        mm(R("p5", 0, 256), R("B16"), R("T2"), True, False)
+        mm(R("p5", 0, 256), R("BLK"), R("C1"), False, False)
+        tt(w(W_C), R("p4", 32, 48), w(W_C1), A.add)
+        cp(u(U_C), w(W_C))
+        tt(R("OH"), IND(R("G"), u(U_C)), R("M1"), A.is_equal)
+        mm(R("p5", 0, 256), R("DW"), R("OH"), False, True)
+        ts(R("Zu", 256, 512), R("OH"), col(PI), A.mult)
+        tt(R("Zu", 0, 256), IND(R("Bo"), u(U_C)), R("OH"), A.mult)
+        wrap(R("p3", 32, 64), "Zu", 0, 512)
+        mm(R("p6", 0, 256), R("BLK"), R("Zu", 0, 256), True, True)
+        lin(R("srep"), R("p5", 0, 256), 1.0, 0.0)
+        ts(u(U_A), R("p3", 32, 48), 2048.0, A.add)
+        ts(w(W_C16), w(W_C), 16.0, A.mult)
+        ts(R("wi", 0, 16), R("p3", 32, 48), 2048.0, A.add)
+        tt(w(W_S), R("p3", 48, 64), w(W_C16), A.add)
+        cp(u(U_S), w(W_S))
+        ts(R("so"), R("srep"), 2048.0, A.subtract)
+        act(R("dm"), R("srep"), F.Relu, bias=-4095.0)
+        lin(R("arep"), R("p6", 0, 256), 1.0, -2048.0)
+        act(R("absb"), R("p6", 0, 256), F.Abs, bias=col(AB))
+        act(R("absb"), R("absb"), F.Relu, bias=-255.5 * 8192, scale=8192.0)
+        ts(R("wi", 16, 32), R("wi", 0, 16), 511, A.bitwise_and)
+        cp(u(U_A9), R("wi", 16, 32))
+        gather(R("hg"), IND(R("hmf"), u(U_A9)))
+        gather(R("xa"), IND(R("xsb"), u(U_A)))
+        lin(R("p2", 0, 256), R("xa"), 1.0, 0.0)
+        for (lo, hi) in PARTS:
+            targets(U_A, "srep", lo, hi, 0)
+            for c in range(lo, hi, CH):
+                gather(R("xv", 16 * c, 16 * (c + CH)), IND(R("XB"), R("q16", c, c + CH)))
+        for c in range(0, 256, 64):
+            for k in range(16):
+                tt(R("cmp", 256 * k + c, 256 * k + c + 64), R("xv", 16 * c, 16 * c + 1024, 16, 16 * c + k),
+                   R("p2", c, c + 64), A.is_lt)
+                mm(R("p0", c, c + 64) if c < PARTS[0][1] else R("p7", 256 + c, 320 + c), mat("WR", k), R("cmp", 256 * k + c, 256 * k + c + 64), k == 0, k == 15)
+        for (lo, hi) in PARTS:
+            ts(R("good", lo, hi), R("p0", lo, hi) if lo == 0 else R("p7", 256 + lo, 256 + hi), 8.0, A.is_ge)
+            mm(R("p1", lo, hi), R("TRI"), R("good", lo, hi), True, True)
+            ts(R("p2", 256 + lo, 256 + hi), R("p1", lo, hi), 1.0, A.is_equal)
+            pick("so", lo, hi, 0, W_S, W_X, W_AT)
+            cp(u(U_AT, lo, hi), w(W_AT, lo, hi))
+            lin(R("atrep", lo, hi), R("p5", lo, hi), 1.0, 2048.0)
+            ts(R("who", lo, hi), IND(bdw, u(U_AT, lo, hi)), 2048.0, A.add, col(M0), A.mult)
+            wrap(R("p4", lo // 16, hi // 16), "who", lo, hi)
+            ts(u(U_W, lo, hi), R("p4", lo // 16, hi // 16), 2048.0, A.add)
+            targets(U_W, "atrep", lo, hi, 256)
+            for c in range(lo, hi, CH):
+                o, i = R("fr", 16 * c, 16 * (c + CH)), IND(bdw, R("q16", 256 + c, 256 + c + CH))
+                put([a_act(o, i, F.Relu, col(M0), col(M0)), a_ts(o, i, 0.0, A.is_equal, col(M0), A.mult)], [o], [i, col(M0)])
+        lin(R("whom"), IND(bdw, u(U_AT)), col(M0), 0.0)
+        tt(w(W_D), w(W_AT), w(W_S), A.subtract)
+        for c in range(0, 256, 64):
+            pb = "p1" if c < 128 else "p0"
+            mm(R(pb, c, c + 64), R("HB"), R("ones", c, c + 64), True, False)
+            for k in range(16):
+                mm(R(pb, c, c + 64), mat("TR", k), R("fr", 16 * c, 16 * c + 1024, 16, 16 * c + k), False, k == 15)
+        act(R("p6", 256, 512), R("p6", 0, 256), F.Abs)
+        tt(R("A1"), R("absb"), R("p6", 256, 512), A.is_lt)
+        dedupe(W_AT, 0)
+        ts(R("Zp", 256, 512), R("p7", 0, 256), 0.0, A.is_equal)
+        tt(R("fl"), R("p7", 0, 256), R("A1"), A.is_lt)
+        ts(w(W_D), w(W_D), 1.0 / 16, A.mult)
+        scan(R("p6", 0, 256), R("fl"), R("ones"), col(ZI), A.add, A.subtract)
+        tt(R("Zp", 0, 256), R("p6", 0, 256), R("fl"), A.mult)
+        wrap(R("p4", 32, 64), "Zp", 0, 512)
+        tt(w(W_Y), R("p4", 48, 64), w(W_D), A.mult)
+        tt(w(W_FB), w(W_Y), w(W_S), A.add)
+        cp(u(U_FB), w(W_FB))
+        tt(w(W_P), R("p4", 32, 48), R("dwr"), A.add)
+        cp(u(U_P), w(W_P))
+        tt(IND(R(PW), u(U_P)), R("whom"), R("hg"), A.add)
+        mine = masks_from(core, cores, topo)
+        trs = []
+        for p in range(N):
+            z = 256 * (p if p < 4 else p + 1)
+            if p == rank:
+                lin(R(land, 16 * rank, 16 * rank + 16), R(PW, z, z + 16), 1.0, 0.0)
+                continue
+            rid, pid, _e = topo.addr(cores[p])
+            trs.append(RemoteDMATransfer(dst_ids=[DstId(rid=rid, pnc=pid)], dma_engine_mask=sum(1 << e for e in mine[cores[p]]),
+                                         remote_sem=T.sem["arr%d" % t], src=T[PW][:, z:z + 16],
+                                         dst=T[land][:, 16 * rank:16 * rank + 16]))
+        sent = ext(None, "sent%d" % t)
+        put([("G", (lambda trs, t: lambda: g.remote_dma_fused(trs, local_sem=T.sem["snt%d" % t]))(trs, t), 500.0)],
+            [sent], [R(PW)], "snt%d" % t, -sum(len(v) for v in mine.values()), FAR, keep=True)
+        arrivals = sum(len(masks_from(c, cores, topo)[core]) for c in cores if c != core)
+        put([("X", None, 0.0)], [(None, [(land, 16 * p, 16 * p + 16) for p in range(N) if p != rank], [])], [sent],
+            "arr%d" % t, -arrivals)
+        tt(R("p2", 256, 384), R("p1", 0, 128), R("Zp", 256, 384), A.is_equal)
+        tt(R("p2", 384, 512), R("p0", 128, 256), R("Zp", 384, 512), A.is_equal)
+        for (lo, hi) in PARTS2:
+            pick("key", lo, hi, 256, W_AT, W_X2, W_K)
+        act(IND(bdw, u(U_S)), R("neg"), F.Sigmoid)
+        act(IND(bdw, u(U_FB)), R("neg"), F.Sigmoid)
+        ts(R("h16"), R(land), 2048.0, A.subtract, col(MH), A.mult)
+        wrap(R("p4", 0, 8), "h16", 0, 128)
+        ts(u(U_H, 0, 128), R("p4", 0, 8), 2048.0, A.add)
+        dedupe(W_K, 256)
+        tt(R("T1"), R("p7", 0, 256), R("MK"), A.is_equal)
+        scan(R("sg"), R("keep"), R("T1"), 0.0, A.mult, A.add)
+        tt(w(W_D2), w(W_K), w(W_AT), A.subtract)
+        tt(w(W_Y2), R("sg", 0, 256, 16, 15), w(W_D2), A.mult)
+        tt(w(W_E), w(W_Y2), w(W_FB), A.add)
+        cp(u(U_E), w(W_E))
+        cp(IND(bdw, u(U_E)), R("arep"))
+        ts(R("em"), IND(bdw, u(U_H, 0, 128)), 0.0, A.is_equal)
+        gather(R("old"), IND(bdw, u(U_H, 0, 128)))
+        tt(R("dd"), R("em"), R(land), A.mult)
+        tt(IND(bdw, u(U_H, 0, 128)), R("old"), R("dd"), A.add)
+        if t + 1 < RO:
+            dma(W("buff", T.buff[:, 0, :]), ext(T.bd[0:128:32, 0:S], "bd"), "Y", "dF", 65536)
+            dma(W("buff", T.buff[:, 1, :]), ext(T.bd[16:128:32, 0:S], "bd"), "S", "dF", 65536)
+        else:
+            put([("G", lambda: g.dma_start(T.y[:, :], T.bd[0:128:16, 0:S], accum_op=A.add, max_dma_last_dim=8192), 500.0)],
+                [ext(None, "y")], [R("bd", 0, S)], "dY1", 16, DLAT, keep=True)
+
+    return ops
+
+
+def rank_program(g, core, T, topo):
+    if T.rank_of(core) is None:
+        return
+    if not ORDER:
+        ORDER.extend(plan([build(g, core, T, topo, m) for m in MODELS]))
+    calls = build(g, core, T, topo, MODELS[0])
+    ops = [calls[j]["alts"][a][:2] + (calls[j]["rd"], calls[j]["wr"], calls[j]["sem"], calls[j]["cnt"]) for j, a in ORDER]
+    queue = {"V": g.vector, "S": g.scalar, "P": g.tensor, "G": g, "Y": g.sync}
+    hist = {}
+    known = {q: {} for q in queue}
+    waits = []
+    marked = set()
+    for j, (q, call, rd, wr, sem, cnt) in enumerate(ops):
+        need = {}
+        for regs, writes in ((rd, False), (wr, True)):
+            for (name, lo, hi) in regs:
+                bank = psum(name)
+                for (i, l2, h2, w2) in hist.get(name, []):
+                    qi, semi = ops[i][0], ops[i][4]
+                    meet = l2 < hi and lo < h2
+                    if semi is None and sem is None and qi == q:
+                        hit = meet and (w2 or writes) and q != "P"
+                    else:
+                        hit = (meet and (w2 or writes)) or bank
+                    if hit and not (sem is not None and semi == sem):
+                        k = semi if semi is not None else qi
+                        need[k] = max(need.get(k, -1), i)
+        mine_w = []
+        if q != "X":
+            for k, i in need.items():
+                if known[q].get(k, -1) < i:
+                    known[q][k] = i
+                    mine_w.append((k, i))
+                    marked.add(i)
+        waits.append(mine_w)
+        for regs, writes in ((rd, False), (wr, True)):
+            for (name, lo, hi) in regs:
+                hist.setdefault(name, []).append((j, lo, hi, writes))
+    count = {}
+    value = {}
+    for j, (q, call, rd, wr, sem, cnt) in enumerate(ops):
+        if sem is not None:
+            count[sem] = count.get(sem, 0) + abs(cnt)
+        elif j in marked:
+            count[q] = count.get(q, 0) + 1
+            value[j] = count[q]
+    for j, (q, call, rd, wr, sem, cnt) in enumerate(ops):
+        for (k, i) in waits[j]:
+            queue[q].wait_ge(T.sem[k], value[i] if i in value else count[k])
+        if call is None:
+            continue
+        ins = call()
+        if sem is not None:
+            if cnt > 0:
+                ins.then_inc(T.sem[sem], cnt)
+        elif j in marked:
+            ins.then_inc(T.sem[q], 1)
+    for k, v in count.items():
+        g.wait_ge(T.sem[k], v)

@@ -7,55 +7,58 @@ from concourse.mybir import ActivationFunctionType as F
 N = 8
 S = 4096
 RO = 2
+REB0 = 4352
 BW = 4608
 PWW = 2304
-PARTS = [(0, 128), (128, 256)]
-PARTS2 = [(0, 256)]
+LIFT = 8192.0
+ROUND = 1.5 * 2 ** 23
+HALVES = [(0, 128), (128, 256)]
+WHO = ["VVVV", "VVVV"]
+SCAN = "s"
 CH = 32
-DLAT, WAKE = 2000.0, 100.0
-MODELS = [dict(far=5000.0, pe=0.55, cy=1.04, ga=1.55, sc=3.8, wake=100.0, bpn=250.0),
-          dict(far=3000.0, pe=0.45, cy=0.85, ga=1.1, sc=2.0, wake=50.0, bpn=350.0),
-          dict(far=8000.0, pe=1.1, cy=1.2, ga=2.0, sc=5.5, wake=150.0, bpn=200.0),
-          dict(far=5000.0, pe=1.0, cy=1.0, ga=1.2, sc=5.0, wake=40.0, bpn=300.0),
-          dict(far=5000.0, pe=0.5, cy=1.0, ga=2.0, sc=2.0, wake=200.0, bpn=250.0)]
-
-
-def _sb(n, d):
-    return ("sbuf", [128, n], d)
-
+TINY = 2.0 ** -110
+BIG = 65536.0
+DLAT = 2000.0
+MODELS = [dict(far=4500.0, pe=0.54, cy=1.04, ga=1.56, sc=3.8, wake=60.0, bpn=310.0),
+          dict(far=3500.0, pe=0.47, cy=0.9, ga=1.3, sc=2.8, wake=90.0, bpn=260.0),
+          dict(far=6500.0, pe=0.62, cy=1.2, ga=1.9, sc=5.0, wake=80.0, bpn=380.0),
+          dict(far=5500.0, pe=0.6, cy=1.0, ga=1.4, sc=3.0, wake=120.0, bpn=340.0)]
+CALLS = 1
+SEED = 1
+HEAT = 0.002
+MIX = 3
+XV = "********"
+FR = "********"
+SPLIT = False
+LEAD = 3
+EARLY = [True, True]
+TRG = 10
+ROUNDS = 2200
+SPAN = []
+ORDER = []
 
 SCRATCH = {
-    "dsb": _sb(4104, "int32"), "xsb": _sb(4112, "bfloat16"), "hmb": _sb(512, "int32"),
     "bufi": ("sbuf", [128, 2, 128], "int32"), "buff": ("sbuf", [128, 2, 128], "float32"),
-    "bd": _sb(BW, "float32"), "XB": _sb(S, "bfloat16"), "xv": _sb(S, "bfloat16"), "cmp": _sb(S, "bfloat16"),
-    "fr": _sb(S, "bfloat16"), "E": _sb(4352, "bfloat16"),
-    "PW0": _sb(PWW, "float32"), "PW1": _sb(PWW, "float32"), "land0": _sb(128, "float32"), "land1": _sb(128, "float32"),
-    "WR": _sb(2048, "bfloat16"), "TR": _sb(2048, "bfloat16"), "LL": _sb(2048, "bfloat16"),
-    "BLK": _sb(128, "bfloat16"), "K0": _sb(128, "bfloat16"), "TRI": _sb(128, "bfloat16"), "UP": _sb(128, "bfloat16"),
-    "DW": _sb(128, "bfloat16"), "B16": _sb(128, "bfloat16"), "NI": _sb(128, "bfloat16"), "tm": _sb(128, "bfloat16"),
-    "HB": _sb(128, "bfloat16"), "neg": _sb(256, "float32"),
-    "grp": _sb(128, "float32"), "lo1": _sb(128, "float32"), "pci": _sb(8, "int32"), "col": _sb(16, "float32"),
-    "clt": _sb(16, "float32"), "dwr": _sb(16, "float32"), "i16": _sb(16, "float32"),
-    "M16f": _sb(256, "float32"), "M1": _sb(256, "float32"), "MW": _sb(256, "float32"), "j16": _sb(256, "bfloat16"),
-    "keep": _sb(256, "bfloat16"), "MK": _sb(256, "bfloat16"), "sg": _sb(256, "bfloat16"), "C1": _sb(256, "bfloat16"),
-    "c256": _sb(272, "bfloat16"), "ones": _sb(256, "bfloat16"), "c4096": _sb(256, "float32"),
-    "Bw": _sb(256, "float32"), "Bi": _sb(256, "int32"), "X": _sb(256, "int32"), "f": _sb(272, "bfloat16"),
-    "ox": _sb(256, "float32"), "xo": _sb(256, "uint16"), "Bo": _sb(272, "float32"),
-    "cum": _sb(288, "bfloat16"), "G": _sb(272, "float32"), "L2": _sb(24, "float32"),
-    "T1": _sb(256, "bfloat16"), "T2": _sb(256, "bfloat16"), "OH": _sb(256, "bfloat16"),
-    "Zu": _sb(512, "float16"), "Z": _sb(512, "float16"), "Zp": _sb(512, "float16"),
-    "u16": _sb(256, "uint16"), "w32": _sb(256, "float32"), "wi": _sb(32, "int32"),
-    "srep": _sb(256, "float32"), "arep": _sb(256, "float32"), "absb": _sb(256, "float32"), "atrep": _sb(256, "float32"),
-    "t": _sb(512, "int32"), "q": _sb(512, "int32"), "q16": _sb(512, "uint16"), "qo": _sb(512, "float16"),
-    "so": _sb(256, "float16"), "A1": _sb(256, "bfloat16"), "hmf": _sb(512, "float32"), "NB": _sb(128, "bfloat16"),
-    "ID": _sb(128, "bfloat16"), "dm": _sb(256, "bfloat16"), "xa": _sb(256, "bfloat16"),
-    "good": _sb(256, "bfloat16"), "who": _sb(256, "float16"), "whom": _sb(256, "float32"), "hg": _sb(256, "float32"),
-    "key": _sb(512, "float16"), "fl": _sb(256, "bfloat16"),
-    "h16": _sb(128, "float16"), "em": _sb(128, "float32"), "old": _sb(128, "float32"), "dd": _sb(128, "float32"),
+    "buf4": ("sbuf", [128, 2, 128], "float32"), "buf2": ("sbuf", [128, 2, 128], "float32"), "TB": ("sbuf", [128, 8, 32], "bfloat16"),
 }
+for _d, _names in (
+        ("int32", dict(dsb=4104, hmb=512, pci=8, Bi=256, X=256, wi=32, t=512, q=512)),
+        ("uint16", dict(xo=512, u16=256, q16=512)),
+        ("float16", dict(Zu=256, Z=512, Zp=512, qo=512, key=512, dwr=32)),
+        ("bfloat16", dict(xsb=4112, XB0=S, XB1=REB0, xv=S, cmp=S, fr=S, E=4352, LL=2048, TR=2048, WB=144, WB16=144, WBI=144,
+                          XP=144, grp=128, BLK=128, TRI=128, UP=128, B2K=128, B256=128, B16=128, DW=128, NI=128, tm=128,
+                          NB=128, ID=128, I16=128, I256=128, j16=256, keep=256, MK=256, SEL=256, M1b=256, c256=272,
+                          ones=256, f=272, cum=288, T1=256, T2=256, OH=256, C1=16, sg=256, nb=256, lose=256, A1=256,
+                          dm=256, xa=256, good=256)),
+        ("float32", dict(bd=BW, PW0=PWW, PW1=PWW, land0=128, land1=128, ID32=128, IO32=128, NI32=128, R0=128, RH=128, neg=256,
+                         col=24, clt=16, i16=16, M1=256, c4096=256, Bw=256, ox=256, Bo=272, G=272, L2=24, w32=160,
+                         srep=256, arep=256, absb=256, atrep=256, back=256, hmf=512, whom=256, hg=256, pay=256, s1=256,
+                         s2=256, rl=128, em=128, old=128, dd=128))):
+    for _n in _names:
+        SCRATCH[_n] = ("sbuf", [128, _names[_n]], _d)
 for _b in range(8):
     SCRATCH["p%d" % _b] = ("psum", [128, 512], "float32")
-SEMAPHORES = ["V", "S", "P", "G", "arr0", "arr1", "snt0", "snt1", "dB", "dX", "dD", "dR", "dH", "dF", "dY0", "dY1"]
+SEMAPHORES = ["V", "S", "P", "G", "arr0", "arr1", "snt0", "snt1", "dB", "dX", "dD", "dR", "dH", "dF", "dY"]
 
 
 def masks_from(src, cores, topo):
@@ -65,16 +68,16 @@ def masks_from(src, cores, topo):
     near = lambda c: topo.mates(topo.chip(c), topo.chip(src)) or topo.same_plane(topo.chip(c), topo.chip(src))
     off = sorted(off, key=near)
     eng = list(topo.engines(src, off[0]))
-    out = {}
-    spare = len(eng) - len(off)
-    at = 0
-    for i, c in enumerate(off):
-        n = 2 if i < spare else 1
-        out[c] = eng[at:at + n]
-        at += n
-    for i, c in enumerate(on):
-        rest = [e for e in topo.engines(src, c) if e not in eng]
-        out[c] = rest[i:i + 1]
+    rest = [e for e in topo.engines(src, on[0]) if e not in eng]
+    if CALLS == 1:
+        out = [{c: eng[i::len(off)] for i, c in enumerate(off)}]
+        out[0][on[0]] = rest[:1]
+        return out
+    first = len(eng) // 2
+    out = []
+    for part in (off[:first], off[first:]):
+        out.append({c: eng[i::len(part)] for i, c in enumerate(part)})
+    out[0][on[0]] = rest[0:4:2]
     return out
 
 
@@ -92,167 +95,207 @@ def schedule(ops):
             for (name, lo, hi) in regs:
                 for (i, l2, h2, w2) in hist.get(name, []):
                     if l2 < hi and lo < h2 and (w2 or writes) and not (o["sem"] and ops[i]["sem"] == o["sem"]):
-                        pred[j][i] = True
+                        pred[j][i] = 0
                 if q == "P" and psum(name) and writes:
                     if name in lastq:
-                        pred[j].setdefault(lastq[name], False)
+                        pred[j].setdefault(lastq[name], 2)
                     lastq[name] = j
         if o["keep"]:
-            if q in lastq:
-                pred[j].setdefault(lastq[q], False)
-            lastq[q] = j
+            row = (q, o["keep"])
+            if row in lastq:
+                pred[j].setdefault(lastq[row], 1 if ops[lastq[row]]["sem"] else 2)
+            lastq[row] = j
         for regs, writes in ((o["rd"], False), (o["wr"], True)):
             for (name, lo, hi) in regs:
                 h = hist.setdefault(name, [])
                 if writes:
-                    h[:] = [e for e in h if not (lo <= e[1] and e[2] <= hi and ops[e[0]]["sem"] != o["sem"] or
-                                                 lo <= e[1] and e[2] <= hi and not o["sem"])]
+                    h[:] = [e for e in h if not (lo <= e[1] and e[2] <= hi and (not o["sem"] or ops[e[0]]["sem"] != o["sem"]))]
                 h.append((j, lo, hi, writes))
-    succ = [[] for _ in range(n)]
-    for j in range(n):
-        for i in pred[j]:
-            succ[i].append(j)
-    tail = [0.0] * n
-    nxt = {}
-    for j in range(n - 1, -1, -1):
-        pe = ops[j]["alts"][0][0] == "P"
-        tail[j] = ops[j]["alts"][0][2] + ops[j]["lat"] + max(
-            [0.0] + [tail[i] + (0.0 if pe and ops[i]["alts"][0][0] == "P" else WAKE) for i in succ[j]])
-        name = ops[j]["wr"][0][0] if ops[j]["wr"] else None
-        if name in CHAIN:
-            if name in nxt:
-                tail[j] = max(tail[j], CHAIN[name] * ops[j]["alts"][0][2] + tail[nxt[name]])
-            nxt[name] = j
-    kinds = {}
-    seen = {}
-    for j, o in enumerate(ops):
-        name, lo = o["wr"][0][:2] if o["wr"] else ("", 0)
-        lo = lo % 256 if name == "cmp" else 0 if name in ("E", "WR", "TR", "LL", "Bw") else lo
-        k = (name, lo, o["rd"][-1][0] if o["rd"] else "")
-        seen[j] = kinds.setdefault(k, len(kinds))
-    for j in range(n):
-        pred[j] = [(i, raw) for i, raw in pred[j].items()
-                   if not (ops[i]["keep"] and ops[j]["keep"] and not raw and ops[i]["sem"]
-                           and ops[i]["alts"][0][0] == ops[j]["alts"][0][0])] , len(pred[j])
-    return pred, succ, tail, seen, len(kinds)
+    kinds, kind = {}, []
+    for o in ops:
+        name, lo = o["wr"][0][:2]
+        lo = lo // 1024 if name == "cmp" else 0 if name in ("E", "LL", "TR", "Bw") else lo
+        kind.append(kinds.setdefault((name, lo, o["rd"][-1][0] if o["rd"] else ""), len(kinds)))
+    return [list(p.items()) for p in pred], kind, len(kinds)
 
 
-def replay(ops, pred, order, m):
+def replay(ops, pred, order, m, log=None, held=None):
     wake = m["wake"]
     free, done, on, bank, df = {}, [0.0] * len(ops), [None] * len(ops), {}, 0.0
+    by, last, alt = {}, {}, {}
     for j, a in order:
         o = ops[j]
         q, call, c = o["alts"][a]
         s = free.get(q, 0.0)
-        for i, raw in pred[j][0]:
-            d = done[i] + (0.0 if on[i] == q and not ops[i]["sem"] and (q == "P" or not raw) else wake)
-            if d > s:
-                s = d
+        by[j] = last.get(q)
+        for i, link in pred[j]:
+            if not link:
+                d = done[i] + (0.0 if on[i] == q == "P" else wake)
+                if d > s:
+                    s, by[j] = d, i
         for b in o["banks"]:
             if b in bank and bank[b][0] != q and bank[b][1] + wake > s:
-                s = bank[b][1] + wake
-        on[j] = q
+                s, by[j] = bank[b][1] + wake, bank[b][2]
+        on[j], last[q], alt[j] = q, j, a
         free[q] = s + c
         done[j] = s + c + o["lat"]
         if o["bytes"]:
             df = max(df, s + c + 0.6 * DLAT) + o["bytes"] / m["bpn"]
             done[j] = df + 0.4 * DLAT
         for b in o["banks"]:
-            bank[b] = (q, done[j])
+            bank[b] = (q, done[j], j)
+        if log is not None:
+            log.append((s, q, c, o["wr"][0]))
+    if held is not None:
+        j = done.index(max(done))
+        while by[j] is not None:
+            if all(i != by[j] for i, link in pred[j]):
+                held.append((by[j], j, alt[by[j]]))
+            j = by[j]
     return max(done)
 
 
-def plan(builds):
-    ops = builds[0]
-    pred, succ, tail, kind, kinds = schedule(ops)
-    rng = np.random.default_rng(SEED)
+def slot(seq, e):
+    lo, hi = 0, len(seq)
+    while lo < hi:
+        mid = (lo + hi) // 2
+        if seq[mid] < e:
+            lo = mid + 1
+        else:
+            hi = mid
+    seq.insert(lo, e)
 
-    def trial(bias):
-        order = greedy(ops, pred, succ, [tail[j] + bias[kind[j]] for j in range(len(ops))])
-        t = [replay(b, pred, order, m) for b, m in zip(builds, MODELS)]
-        return sum(math.log(x) for x in t) + math.log(t[0]), order, t
-    bias = [0.0] * kinds
-    best = trial(bias)
-    for _ in range(ROUNDS):
-        c = list(bias)
-        for _i in range(int(rng.choice([1, 2, 3, 5, 8]))):
-            c[int(rng.integers(kinds))] += float(rng.choice([-1, 1]) * rng.choice([200, 500, 1000, 2000, 4000]))
-        r = trial(c)
-        if r[0] <= best[0]:
-            best, bias = r, c
+
+def place(ops, before, after, rank, spare, m, lat, forward):
+    n = len(ops)
+    wake = m["wake"]
+    left = [len(p) for p in before]
+    st, en, on, alt = [0.0] * n, [0.0] * n, [None] * n, [0] * n
+    busy, bank = {}, {}
+    df = 0.0
+    ready = sorted((rank[j], j) for j in range(n) if not left[j])
+    while ready:
+        j = ready.pop(0)[1]
+        o = ops[j]
+        best = None
+        for a, (q, call, c) in enumerate(o["alts"]):
+            s = 0.0
+            for i, link in before[j]:
+                d = st[i] if link == 1 and forward else en[i] + (0.0 if link or on[i] == q == "P" else wake)
+                if d > s:
+                    s = d
+            if not forward:
+                s += lat[j]
+            lists = [(busy.setdefault(q, []), 0.0)] + [(bank.setdefault(b, []), wake) for b in o["banks"]]
+            moved = True
+            while moved:
+                moved = False
+                for iv, gap in lists:
+                    lo, hi = 0, len(iv)
+                    while lo < hi:
+                        mid = (lo + hi) // 2
+                        if iv[mid][1] + gap <= s:
+                            lo = mid + 1
+                        else:
+                            hi = mid
+                    while lo < len(iv) and iv[lo][0] - gap < s + c:
+                        if (not gap or iv[lo][2] != q) and iv[lo][1] + gap > s:
+                            s = iv[lo][1] + gap
+                            moved = True
+                        lo += 1
+            v = s + c + (spare[j] if a else 0.0)
+            if best is None or v < best[0]:
+                best = (v, s, c, q, a, lists)
+        v, s, c, q, a, lists = best
+        for iv, gap in lists:
+            slot(iv, (s, s + c, q))
+        st[j], on[j], alt[j] = s, q, a
+        en[j] = s + c
+        if forward:
+            en[j] += o["lat"]
+            if o["bytes"]:
+                df = max(df, s + c + 0.6 * DLAT) + o["bytes"] / m["bpn"]
+                en[j] = df + 0.4 * DLAT
+            lat[j] = en[j] - s - c
+        for i, link in after[j]:
+            left[i] -= 1
+            if not left[i]:
+                slot(ready, (rank[i], i))
+    return st, en, alt
+
+
+def plan(builds):
+    ops, m = builds[0], MODELS[0]
+    n = len(ops)
+    before, kind, kinds = schedule(ops)
+    after = [[] for _ in range(n)]
+    for j in range(n):
+        for i, link in before[j]:
+            after[i].append((j, link))
+    rank = [0.0] * n
+    for j in range(n - 1, -1, -1):
+        rank[j] = min([0.0] + [rank[i] for i, link in after[j]]) - ops[j]["alts"][0][2] - ops[j]["lat"] - m["wake"]
+    rng = np.random.default_rng(SEED)
+    lat = [0.0] * n
+    either = sorted(set(kind[j] for j in range(n) if len(ops[j]["alts"]) > 1))
+    steps = sorted(set(o["step"][0] for o in ops))
+    best, cur, lean, held = None, 0.0, [300.0] * n, []
+    for r in range(ROUNDS):
+        now = list(rank)
+        spare = list(lean)
+        if r % MIX == 1:
+            for _ in range(1 + int(rng.integers(2))):
+                k, t = steps[int(rng.integers(len(steps)))], int(rng.integers(3))
+                d = float(rng.choice([-3000.0, -1500.0, -700.0, -300.0, 300.0, 700.0, 1500.0, 3000.0]))
+                now = [now[j] + d if ops[j]["step"][0] == k and t in (2, ops[j]["step"][1]) else now[j] for j in range(n)]
+        elif r % MIX == 0:
+            size = float(rng.choice([30.0, 100.0, 300.0, 1000.0]))
+            noise = rng.normal(0.0, 1.0, kinds) * size * (rng.random(kinds) < float(rng.choice([0.03, 0.1, 0.3])))
+            now = [rank[j] + float(noise[kind[j]]) for j in range(n)]
+            for _ in range(int(rng.integers(3))):
+                k, v = either[int(rng.integers(len(either)))], float(rng.choice([0.0, 200.0, 500.0, 1000.0, 2000.0, 5000.0]))
+                spare = [v if kind[j] == k else spare[j] for j in range(n)]
+        else:
+            for _ in range(1 + int(rng.integers(3))):
+                i, j, a = held[int(rng.integers(len(held)))]
+                if len(ops[i]["alts"]) > 1 and rng.random() < 0.4:
+                    spare[i] = 5000.0 if a else -5000.0
+                elif rng.random() < 0.5:
+                    now[i] = max(now[i], now[j]) + float(rng.choice([1.0, 300.0, 1500.0]))
+                else:
+                    top = now[i]
+                    stack = [j]
+                    while stack:
+                        x = stack.pop()
+                        if now[x] >= top:
+                            now[x] = top - 1.0
+                            stack += [y for y, link in before[x]]
+        new = spare
+        for again in range(1 + (r < 10 or r % 12 == 0)):
+            if again:
+                st, en, alt = place(ops, after, before, [-x for x in en], spare, m, lat, False)
+                now = [-x for x in en]
+            st, en, alt = place(ops, before, after, now, spare, m, lat, True)
+            if best is not None and max(en) > 1.02 * best[2][0]:
+                continue
+            order = [(j, alt[j]) for j in sorted(range(n), key=lambda j: (st[j], j))]
+            t = [replay(b, before, order, x) for b, x in zip(builds, MODELS)]
+            v = sum(math.log(x) for x in t)
+            if best is None or v <= cur + HEAT * (1.0 - r / ROUNDS) * float(rng.random()):
+                cur, rank, lean, held = v, now, new, []
+                for b, x in zip(builds, MODELS):
+                    replay(b, before, order, x, held=held)
+            if best is None or v <= best[0]:
+                best = (v, order, t)
     SPAN[:] = best[2]
     return best[1]
-
-
-def greedy(ops, pred, succ, tail):
-    n = len(ops)
-    WAKE, BPN = MODELS[0]["wake"], MODELS[0]["bpn"]
-    left = [p[1] for p in pred]
-    ready = [j for j in range(n) if left[j] == 0]
-    free, done, on, bank = {}, [0.0] * n, [None] * n, {}
-    dmafree = [0.0]
-    order = []
-    base = {}
-
-    def start(j, q):
-        if (j, q) not in base:
-            s = 0.0
-            for i, raw in pred[j][0]:
-                s = max(s, done[i] + (0.0 if on[i] == q and not ops[i]["sem"] and (q == "P" or not raw) else WAKE))
-            base[(j, q)] = s
-        s = max(base[(j, q)], free.get(q, 0.0))
-        for b in ops[j]["banks"]:
-            if b in bank and bank[b][0] != q:
-                s = max(s, bank[b][1] + WAKE)
-        return s
-    while ready:
-        best = None
-        byq = {}
-        for j in ready:
-            for alt, (q, call, cost) in enumerate(ops[j]["alts"]):
-                byq.setdefault(q, []).append((j, start(j, q), cost, alt))
-        for q, c in byq.items():
-            c.sort(key=lambda e: -tail[e[0]])
-            top = c[0]
-            for e in c[1:]:
-                if e[1] < top[1]:
-                    a = max(top[1] + tail[top[0]], top[1] + top[2] + tail[e[0]])
-                    b = max(e[1] + tail[e[0]], max(top[1], e[1] + e[2]) + tail[top[0]])
-                    if b <= a + SLACK:
-                        top = e
-                        break
-            if best is None or top[1] < best[1][1]:
-                best = (q, top)
-        q, (j, s, cost, call) = best
-        on[j] = q
-        free[q] = s + cost
-        done[j] = s + cost + ops[j]["lat"]
-        if ops[j]["bytes"]:
-            dmafree[0] = max(dmafree[0], s + cost + 0.6 * DLAT) + ops[j]["bytes"] / BPN
-            done[j] = dmafree[0] + 0.4 * DLAT
-        for b in ops[j]["banks"]:
-            bank[b] = (q, done[j])
-        order.append((j, call))
-        ready.remove(j)
-        for i in succ[j]:
-            left[i] -= 1
-            if left[i] == 0:
-                ready.append(i)
-    return order
-
-
-SLACK = 150.0
-SPAN = []
-ORDER = []
-SEED = 1
-ROUNDS = 1200
-CHAIN = {"xv": 0.5, "cmp": 1.0, "fr": 0.6, "E": 1.0, "XB": 0.7, "WR": 1.0, "TR": 1.0, "LL": 1.0}
 
 
 def build(g, core, T, topo, m):
     rank = T.rank_of(core)
     cores = list(T.cores)
     ops = []
+    step = ["constants", 0]
     CY, PEC, GA, SC, FAR, BPN = m["cy"], m["pe"], m["ga"], m["sc"], m["far"], m["bpn"]
 
     def R(name, lo=0, hi=None, step=1, at=None):
@@ -277,6 +320,7 @@ def build(g, core, T, topo, m):
             wr += x[1]
             rd += x[2]
         ops.append({"alts": alts, "rd": rd, "wr": wr, "sem": sem, "cnt": cnt, "lat": lat, "bytes": nbytes, "keep": keep,
+                    "step": tuple(step),
                     "banks": set(r[0] for r in rd + wr if psum(r[0]))})
 
     def ap(x):
@@ -286,7 +330,7 @@ def build(g, core, T, topo, m):
         if o[5]:
             return fix + o[3] * SC * CY
         if i[5]:
-            return fix + i[3] * GA * CY
+            return fix + i[3] * max(GA, per) * CY
         return max(64.0, i[3] * per) * CY
 
     def half(*xs):
@@ -316,7 +360,7 @@ def build(g, core, T, topo, m):
         put([a_ts(o, a, s1, op0, s2, op1)], [o], [a, s1, s2])
 
     def scan(o, a, b, init, op0, op1):
-        put([("V", lambda: g.vector.tensor_tensor_scan(o[0], a[0], b[0], ap(init), op0, op1), cost(o, a, 1.0))],
+        put([("V", lambda: g.vector.tensor_tensor_scan(o[0], a[0], b[0], ap(init), op0, op1), cost(o, a, half(o, a, b)))],
             [o], [a, b, init])
 
     def ms(o, c):
@@ -328,11 +372,23 @@ def build(g, core, T, topo, m):
     def lin(o, i, scale, bias):
         put([a_act(o, i, F.Identity, bias, scale), a_ts(o, i, scale, A.mult, bias, A.add)], [o], [i, scale, bias])
 
-    def gather(o, i):
-        put([a_act(o, i, F.Copy), a_cp(o, i)], [o], [i])
+    def either(alts, o, i, on):
+        put([a for a in alts if on in ("*", a[0])], [o], [i])
+        if on != "*":
+            row("large")
+
+    def row(name):
+        ops[-1]["keep"] = name
+
+    def gather(o, i, on="*"):
+        either([a_act(o, i, F.Copy), a_cp(o, i)], o, i, on)
+
+    def empty(o, i, on):
+        either([a_act(o, i, F.Relu, 1.0), a_ts(o, i, 0.0, A.is_equal)], o, i, on)
 
     def mm(o, l, r, start, stop):
-        put([("P", lambda: g.tensor.matmul(o[0], l[0], r[0], start, stop), max(64, r[3]) * PEC)], [o], [l, r])
+        slow = 4 if SCRATCH[r[4]][2] == "float32" else 1
+        put([("P", lambda: g.tensor.matmul(o[0], l[0], r[0], start, stop), max(64, r[3]) * slow * PEC)], [o], [l, r])
 
     def iota(o, pat, base, ch, flt=True):
         if flt:
@@ -341,26 +397,31 @@ def build(g, core, T, topo, m):
             call = lambda: g.iota(o[0], pat, base, ch)
         put([("G", call, 130.0 + 2 * o[3] * CY)], [o], [], keep=True)
 
+    def select(o, pat, op, fill, base, ch, i=None):
+        i = i or o
+        put([("G", lambda: g.affine_select(o[0], i[0], pat, op, fill, base, ch), 170.0 + 2 * o[3] * CY)], [o], [i], keep=True)
+
     def dma(o, i, q, sem, nbytes):
         eng = g.sync if q == "Y" else g.scalar
         put([(q, lambda: eng.dma_start(o[0], i[0]), 60.0)], [o], [i], sem, 16, DLAT + nbytes / BPN, nbytes, q == "Y")
 
-    def mat(name, r):
-        return R(name, 128 * r, 128 * r + 128)
-
-    def wrap(o, name, lo, hi):
+    def wrap(o, name, lo, hi, start=True, stop=True, base="WB"):
         for r in range(16):
-            mm(o, mat("WR", r), R(name, lo, hi, 16, lo + r), r == 0, r == 15)
+            mm(o, R(base, 15 - r, 143 - r), R(name, lo, hi, 16, lo + r), start and r == 0, stop and r == 15)
 
     def col(j):
         return R("col", j, j + 1)
 
+    def own(name, i, lo, hi):
+        scan(R(name, lo, hi), R("SEL", lo, hi), i, 0.0, A.add, A.min)
+        return R(name, lo, hi, 16, lo + 15)
+
     def ext(t, name="hbm"):
         return (t, [] if name == "hbm" else [(name, 0, S)], [], 0, name, False)
 
-    PG, PI, PI1, M0, MH, AB, ZI = 0, 1, 2, 3, 4, 5, 6
-    U_C1, U_C, U_A, U_A9, U_S, U_AT, U_W, U_P, U_FB, U_E, U_H, U_L = [16 * i for i in range(12)]
-    W_C1, W_C, W_X, W_S, W_AT, W_D, W_FB, W_K, W_Y, W_E, W_P, W_C16, W_X2, W_D2, W_Y2 = [16 * i for i in range(15)]
+    PG, PI, PW15, M0, MH, AB, ZI, ZJ, ZK, DW, AS, AO, M2, CB, C2K, C4K, CRAW, ODD, NONE, MO, NEG = range(21)
+    U_C1, U_C, U_A, U_A9, U_S, U_AT, U_W, U_P, U_FB, U_E, U_H = [16 * i for i in range(11)]
+    W_S, W_AT, W_D, W_Y, W_FB, W_K, W_NZ, W_D1, W_D2, W_E = [16 * i for i in range(10)]
 
     def u(c, lo=0, hi=256):
         return R("u16", c + lo // 16, c + hi // 16)
@@ -368,77 +429,99 @@ def build(g, core, T, topo, m):
     def w(c, lo=0, hi=256):
         return R("w32", c + lo // 16, c + hi // 16)
 
+    XS = R("xsb")
+    RAW = 7.0 * S
     for y in range(2):
         dma(W("bufi", T.bufi[:, y, :]), ext(T.board[y:8:2, :]), "Y", "dB", 65536)
     dma(R("xsb", 0, S), ext(T.xs[:, :]), "Y", "dX", 1 << 20)
     dma(R("dsb", 0, S), ext(T.ds[:, :]), "Y", "dD", 1 << 21)
+    for y in range(2):
+        dma(ext(T.hmb[y:128:2, :], "hmb"), ext(T.hm[:, :]), "Y", "dH", 131072)
+    TB = W("TB", T.TB[:, :, :])
     iota(R("pci", 0, 1), [[0, 1]], 0, 1, False)
     iota(R("grp"), [[1, 8], [0, 16]], 0, 0)
-    iota(R("lo1"), [[0, 8], [1, 16]], 1, 0)
     iota(R("i16"), [[1, 16]], 0, 0)
-    iota(R("MW"), [[16, 16], [0, 16]], 0, 0)
+    iota(R("XP"), [[1, 144]], 0, -1)
     iota(R("j16"), [[0, 16], [1, 16]], 0, 0)
-    iota(R("M16f"), [[16, 256]], 0, 0)
-    iota(R("M1"), [[1, 256]], 512, 0)
+    iota(R("M1b"), [[1, 256]], 0, 0)
+    iota(TB, [[0, 256]], 4096, 0)
+    select(TB, [[0, 8], [1, 32]], A.is_gt, -4096.0, -15, 0)
+    select(TB, [[0, 8], [1, 32]], A.is_ge, 0.0, -15, 0)
+    select(TB, [[-16, 8], [0, 32]], A.is_equal, 0.0, 0, 1)
     iota(R("bd"), [[0, BW]], 0, 0)
-    iota(R("hmb"), [[0, 512]], 0, 0, False)
-    for t in range(RO):
-        for p in range(N):
-            z = 256 * (p if p < 4 else p + 1)
-            iota(R("PW%d" % t, z, z + 16), [[2, 16]], 4352 + 32 * rank, 0)
+    for k in range(TRG):
+        select(R("TR", 128 * k, 128 * k + 128), [[0, 128]], A.is_ge, 0.0, 0, 0, W("TB", T.TB[:, :, 15 - k:31 - k], 128))
+    for k in range(TRG, 16):
+        lin(R("TR", 128 * k, 128 * k + 128), W("TB", T.TB[:, :, 15 - k:31 - k], 128), 1.0, 0.0)
     ms(R("c256"), 256.0)
     ms(R("cum", 0, 16), 0.0)
     ms(R("f", 256, 272), 1.0)
-    ms(R("Bo", 256, 272), 0.0)
+    ms(R("Bo", 256, 272), 2048.0)
     ms(R("xsb", S, S + 16), 1e29)
     ms(R("dsb", S, S + 8), 0)
-    ms(R("L2", 16, 24), 0.0)
-    ms(R("ones"), 1.0)
+    ms(R("dwr"), 0.0)
     ts(R("pci", 2, 3), R("pci", 0, 1), 4, A.arith_shift_right)
     ts(R("pci", 4, 5), R("pci", 0, 1), 15, A.bitwise_and)
     cp(col(PG), R("pci", 2, 3))
     cp(col(PI), R("pci", 4, 5))
     ts(R("BLK"), R("grp"), col(PG), A.is_equal)
-    ts(col(PI1), col(PI), 1.0, A.add)
-    tt(R("K0"), R("BLK"), R("lo1"), A.mult)
-    ts(col(M0), col(PI), 0.0, A.is_equal)
-    ts(R("NI"), R("K0"), col(PI1), A.is_equal, -1.0, A.mult)
-    ts(R("tm"), R("K0"), col(PI1), A.is_gt)
-    ts(R("clt"), R("i16"), col(PI), A.is_gt)
-    ts(R("UP"), R("NI"), -512.0, A.mult)
-    ts(col(AB), col(PI), -512.0, A.mult, 2048.0 - 255.5, A.add)
+    ts(R("ID"), R("XP", 0, 128), 0.0, A.is_equal)
+    ts(R("tm"), R("XP", 0, 128), 0.0, A.is_gt)
+    tt(R("tm"), R("tm"), R("BLK"), A.mult)
+    lin(R("UP"), R("ID"), 512.0, 0.0)
     tt(R("UP"), R("UP"), R("tm"), A.add)
-    ts(col(8), col(PI), 16.0, A.mult, 15.0, A.add)
-    ts(u(U_L), R("i16"), 0.0, A.mult, col(8), A.add)
-    lin(R("MW"), R("MW"), 1.0, col(PI))
+    lin(col(PW15), col(PI), -1.0, 15.0)
+    ts(R("WB"), R("XP"), col(PW15), A.is_equal)
+    ts(R("MK"), R("j16"), col(PI), A.is_equal, 0.5, A.subtract)
+    lin(R("SEL"), R("MK"), 33.0 * BIG, 15.5 * BIG)
+    for c, add in ((CB, 0.0), (C2K, 2048.0), (C4K, float(S)), (CRAW, -RAW)):
+        lin(col(c), col(PW15), BIG, add)
+    lin(R("M1"), R("M1b"), 1.0, 0.0)
+    lin(R("ones"), R("M1b"), 0.0, 1.0)
+    ts(col(NONE), col(PI), 4.0, A.is_equal, float(S), A.mult)
+    lin(col(NEG), col(NONE), (S + 200.0) / S, -200.0)
+    lin(R("neg"), R("M1b"), 0.0, col(NEG))
+    put([("S", lambda: g.scalar.activation(T.L2[:, 16:24], T.cum[:, 0:8], F.Silu), 1400.0)], [R("L2", 16, 24)], [R("cum", 0, 8)])
     ts(R("keep"), R("j16"), 1.0, A.min)
-    ts(R("MK"), R("j16"), col(PI), A.is_equal, 1.0, A.subtract)
-    lin(R("DW"), R("BLK"), col(PI), 0.0)
-    lin(R("B16"), R("BLK"), 16.0, 0.0)
-    lin(R("NB"), R("BLK"), -1.0, 0.0)
-    lin(R("ID"), R("NI"), -1.0, 0.0)
-    lin(R("HB"), R("BLK"), 1.0 / 32, 0.0)
-    for r in range(1, 16):
-        lin(mat("LL", r), R("BLK"), R("clt", r, r + 1), 0.0)
-    for k in range(16):
-        act(mat("TR", k), R("K0"), F.Relu, bias=-0.5 * k, scale=0.5)
-    for r in range(16):
-        ts(mat("WR", r), R("K0"), float(r + 1), A.is_equal)
-    ts(R("TRI"), R("K0"), col(PI), A.subtract, 0.0, A.max)
+    ts(col(M0), col(PI), 0.0, A.is_equal)
     ts(col(MH), col(PI), float(2 * rank + 1), A.is_equal)
+    for name, src, scale in (("I16", "ID", 16.0), ("I256", "ID", 256.0), ("NI", "ID", -1.0), ("ID32", "ID", 1.0),
+                             ("NI32", "ID", -1.0), ("B16", "BLK", 16.0), ("B256", "BLK", 256.0), ("B2K", "BLK", 2048.0),
+                             ("NB", "BLK", -1.0), ("DW", "BLK", col(PI)), ("R0", "BLK", col(M0)), ("RH", "BLK", col(MH)),
+                             ("WB16", "WB", 16.0), ("WBI", "WB", col(PI))):
+        lin(R(name), R(src), scale, 0.0)
+    tt(R("TRI"), R("tm"), R("ID"), A.subtract)
+    lin(R("TRI"), R("TRI"), 2048.0, 0.0)
+    lin(col(AB), col(PI), -512.0, 2048.0 - 255.5)
+    lin(col(ZK), col(PI), 2048.0, 2048.0)
+    ts(R("clt"), R("i16"), col(PI), A.is_gt)
+    for r in range(1, 16):
+        lin(R("LL", 128 * r, 128 * r + 128), R("NB"), R("clt", r, r + 1), 0.0)
     ts(col(ZI), col(PI), 3.5, A.is_gt, 256.0, A.mult)
-    ts(R("dwr"), R("i16"), 16.0, A.mult, col(PI), A.add)
-    ts(col(ZI + 1), col(PI), 256.0, A.mult, -1024.0, A.add)
-    ts(R("dwr"), R("dwr"), 1024.0, A.add)
-    tt(col(ZI), col(ZI), col(ZI + 1), A.add)
-    lin(R("c4096"), R("M16f"), 0.0, float(S))
-    lin(R("neg"), R("M16f"), 0.0, -200.0)
-    put([("G", lambda: g.dma_start(T.y[:, :], T.c4096[:, :]), 500.0)], [ext(None, "y")], [R("c4096")], "dY0", 16, DLAT,
-        keep=True)
+    lin(col(ZJ), col(PI), 256.0, -1024.0)
+    tt(col(ZI), col(ZI), col(ZJ), A.add)
+    lin(col(DW), col(PI), 1.0, 1024.0)
+    for lo, hi in HALVES if SPLIT else [(0, 256)]:
+        ts(R("dwr", lo // 8, (lo + hi) // 16), R("i16", lo // 16, hi // 16), 16.0, A.mult, col(DW), A.add)
+    ts(col(AS), col(PI), 2.0, A.not_equal)
+    ts(col(AO), col(AS), -2049.0, A.mult, col(NONE), A.add)
+    lin(col(AO), col(AO), 1.0, 1.0)
+    ts(R("pci", 6, 7), R("pci", 0, 1), 1, A.bitwise_and)
+    cp(col(ODD), R("pci", 6, 7))
+    lin(col(M2), col(ODD), -1.0, 1.0)
+    lin(col(MO), col(NONE), -1.0, 0.0)
+    lin(R("IO32"), R("ID"), col(ODD), 0.0)
     ts(W("buff", T.buff[:, :, :]), W("bufi", T.bufi[:, :, :]), float(S), A.subtract)
     for y in range(2):
         dma(ext(T.bd[16 * y:128:32, 0:S], "bd"), W("buff", T.buff[:, y, :]), "Y", "dR", 65536)
-    dma(ext(T.hmb[1:128:2, :], "hmb"), ext(T.hm[:, :]), "Y", "dH", 131072)
+    ts(W("bufi", T.bufi[:, :, :]), W("bufi", T.bufi[:, :, :]), 4097, A.bitwise_and)
+    ts(R("p7", 0, 256), W("bufi", T.bufi[:, :, :]), 0.0, A.is_equal, 2.0 * S, A.mult)
+    tt(W("buf2", T.buf2[:, :, :]), W("buff", T.buff[:, :, :]), R("p7", 0, 256), A.add)
+    for y in range(2):
+        dma(ext(T.bd[16 * y + 2:128:32, 0:S], "bd"), W("buf2", T.buf2[:, y, :]), "Y", "dR", 65536)
+    lin(W("buf4", T.buf4[:, :, :]), W("buff", T.buff[:, :, :]), 1.0, float(S))
+    for y in range(2):
+        dma(ext(T.bd[16 * y + 4:128:32, 0:S], "bd"), W("buf4", T.buf4[:, y, :]), "Y", "dR", 65536)
     cp(R("hmf"), R("hmb"))
 
     bdw = R("bd")
@@ -449,175 +532,254 @@ def build(g, core, T, topo, m):
         cp(R("q16", o + lo, o + hi), R("q", o + lo, o + hi))
         ts(R("qo", o + lo, o + hi), R("q16", o + lo, o + hi), 2048.0, A.subtract)
 
-    def pick(base, lo, hi, o, wb, wx, wk):
-        n = hi - lo
-        z1, z2 = R("Z", 2 * lo, 2 * lo + n), R("Z", 2 * lo + n, 2 * hi)
-        tt(z1, R("p2", 256 + lo, 256 + hi), R("qo", o + lo, o + hi), A.mult)
-        tt(z2, R("p2", 256 + lo, 256 + hi), R(base, lo, hi), A.mult)
-        wrap(R("p3", lo // 8, hi // 8), "Z", 2 * lo, 2 * hi)
-        mm(R("p5", lo, hi), R("ID"), R(base, lo, hi), True, False)
-        mm(R("p5", lo, hi), R("BLK"), z1, False, False)
-        mm(R("p5", lo, hi), R("NB"), z2, False, True)
-        if o == 0:
-            mm(R("p6", lo, hi), R("BLK"), z1, True, False)
-            mm(R("p6", lo, hi), R("NB"), z2, False, True)
-        tt(w(wx, lo, hi), R("p3", lo // 8, lo // 8 + n // 16), w(wb, lo, hi), A.add)
-        tt(w(wk, lo, hi), w(wx, lo, hi), R("p3", lo // 8 + n // 16, hi // 8), A.subtract)
-        cp(R("key", o + lo, o + hi), R("p5", lo, hi))
+    def square(o, lo, hi, stop):
+        for i, (mat, name) in enumerate((("B256", "T1"), ("B16", "T2"), ("DW", "OH"))):
+            mm(o, R(mat), R(name, lo, hi), i == 0, stop and i == 2)
 
-    def dedupe(kw, o):
-        mm(R("p7", 0, 256), R("BLK"), R("dm"), True, False)
-        for c in range(16):
-            ts(R("E", 272 * c, 256 * c + 256), R("key", o + 16 * c, o + 256), 2048.0, A.add, R("w32", kw + c, kw + c + 1), A.is_equal)
-            if c < 15:
-                mm(R("p7", 16 * c + 16, 256), R("BLK"), R("E", 272 * c + 16, 256 * c + 256), False, False)
-        for r in range(1, 16):
-            mm(R("p7", r, 256, 16), mat("LL", r), R("E", 0, 4352, 272, r), False, r == 15)
+    def dedupe(pb, kw, o):
+        def equal(b, c, a, hi, stop=False):
+            step[0] = "equal %d %d %d" % (o, c // 8, hi)
+            ts(R("E", 256 * c + a, 256 * c + hi), R("key", o + a, o + hi), 2048.0, A.add, R("w32", kw + c, kw + c + 1), A.is_equal)
+            row("equal")
+            a = max(a, 16 * c + 16)
+            if a < hi:
+                mm(R(b, a, hi), R("NB"), R("E", 256 * c + a, 256 * c + hi), False, stop)
+
+        for b, (lo, hi) in zip(pb, HALVES if len(pb) > 1 else [(0, 256)]):
+            if o:
+                mm(R(b, lo, hi), R("ID"), R("MK", lo, hi), True, False)
+            mm(R(b, lo, hi), R("NB"), R("dm", lo, hi), o == 0, False)
+            early = LEAD if hi == 256 else 0
+            for c in range(lo // 16, 8):
+                equal(b, c, 16 * c, 128)
+            for c in range(early):
+                equal(b, c, 128, 256)
+            for c in range(8, hi // 16):
+                equal(b, c, 16 * c, 256)
+            for r in range(1, 16):
+                diag = (T.E[:, 17 * lo + r:17 * hi:272], [("E", 272 * i, 272 * i + 16) for i in range(lo // 16, hi // 16)],
+                        [], 16, "E", False)
+                mm(R(b, lo, hi, 16, lo + r), R("LL", 128 * r, 128 * r + 128), diag, False, r == 15 and hi < 256)
+            for c in range(early, 8) if hi == 256 else []:
+                equal(b, c, 128, 256, c == 7)
 
     for t in range(RO):
         PW = "PW%d" % t
         land = "land%d" % t
+        step[:] = ["search", t]
         for b in range(8):
             put([("V", (lambda b: lambda: g.vector.transpose(T.Bw[:, b:256:8], T.buff[:, :, 16 * b:16 * b + 16]))(b), 64 * CY)],
                 [R("Bw", 32 * b, 32 * b + 32)], [W("buff", None)])
-        ts(R("Bi"), R("Bw"), float(S), A.add)
+        if t == 0:
+            ts(R("Bi"), R("Bw"), float(S), A.add)
+            ts(R("X"), R("Bi"), 4097, A.bitwise_and)
+            ts(R("f", 0, 256), R("X"), 0.0, A.is_equal)
+            ts(R("p2", 256, 512), R("X"), 1.0, A.not_equal, float(S), A.mult)
+            tt(R("ox"), R("p2", 256, 512), R("Bw"), A.add)
+            ts(R("xo", 0, 256), R("ox"), 0.0, A.min, float(S), A.add)
+            for c in range(0, 256, CH):
+                gather(R("XB0", 16 * c, 16 * (c + CH)), IND(XS, R("xo", c, c + CH)))
+        else:
+            ts(R("f", 0, 256), R("Bw"), 0.0, A.is_lt)
         lin(R("Bo", 0, 256), R("Bw"), 1.0, 2048.0)
-        ts(R("X"), R("Bi"), 4097, A.bitwise_and)
-        ts(R("f", 0, 256), R("X"), float(t), A.is_equal)
         mm(R("p0", 0, 272), R("BLK"), R("f"), True, True)
         mm(R("p1", 0, 272), R("UP"), R("f"), True, False)
-        ts(R("p2", 256, 512), R("X"), float(1 - t), A.not_equal, float(S), A.mult)
         scan(R("cum", 16, 288), R("p0", 0, 272), R("c256"), 0.0, A.add, A.min)
         wrap(R("p4", 0, 17), "cum", 16, 288)
-        tt(R("ox"), R("p2", 256, 512), R("Bw"), A.add)
-        ts(R("xo"), R("ox"), 0.0, A.min, float(S), A.add)
-        for c in range(0, 256, CH):
-            gather(R("XB", 16 * c, 16 * (c + CH)), IND(R("xsb"), R("xo", c, c + CH)))
-        tt(R("T1"), IND(R("cum", 16, 288), u(U_L)), R("MW"), A.is_le)
-        scan(R("sg"), R("keep"), R("T1"), 0.0, A.mult, A.add)
-        lin(R("L2", 0, 17), R("p4", 0, 17), 1.0, 0.0)
+        ends = own("s1", R("cum", 16, 272, 16, 31), 0, 16)
+        ts(R("T1"), R("M1b"), ends, A.subtract, col(CB), A.is_ge)
+        wrap(R("p3", 0, 16), "T1", 0, 256)
+        lin(R("L2", 0, 17), R("p4", 0, 17), 1.0 / 16, 0.0)
         mm(R("p1", 0, 272), R("ID"), R("cum", 15, 287), False, True)
-        lin(R("G"), R("p1", 0, 272), 1.0, 0.0)
-        cp(u(U_C1), R("sg", 0, 256, 16, 15))
-        ts(w(W_C1), R("sg", 0, 256, 16, 15), 16.0, A.mult)
-        tt(R("T2"), IND(R("L2"), u(U_C1)), R("M16f"), A.is_le)
-        gather(R("C1"), IND(R("M16f", 0, 24), u(U_C1)))
-        wrap(R("p4", 32, 48), "T2", 0, 256)
-        mm(R("p5", 0, 256), R("B16"), R("T2"), True, False)
-        mm(R("p5", 0, 256), R("BLK"), R("C1"), False, False)
-        tt(w(W_C), R("p4", 32, 48), w(W_C1), A.add)
-        cp(u(U_C), w(W_C))
+        lin(R("G"), R("p1", 0, 272), 1.0, -512.0)
+        cp(u(U_C1), R("p3", 0, 16))
+        lin(R("C1"), R("p3", 0, 16), 1.0, 0.0)
+        if t == 0:
+            act(R("p2", 256, 512), R("G", 0, 256), F.Relu, bias=256.0 * S, scale=-float(S))
+            tt(R("ox"), R("p2", 256, 512), R("Bw"), A.add)
+            ts(R("xo", 256, 512), R("ox"), 0.0, A.min, float(S), A.add)
+            for c in range(0, 256, CH):
+                gather(R("XB1", 16 * c, 16 * (c + CH)), IND(XS, R("xo", 256 + c, 256 + c + CH)))
+        tt(R("T2"), IND(R("L2"), u(U_C1)), R("M1"), A.is_le)
+        mm(R("p4", 32, 48), R("I16"), R("C1"), True, False)
+        wrap(R("p4", 32, 48), "T2", 0, 256, False)
+        cp(u(U_C), R("p4", 32, 48))
         tt(R("OH"), IND(R("G"), u(U_C)), R("M1"), A.is_equal)
-        mm(R("p5", 0, 256), R("DW"), R("OH"), False, True)
-        ts(R("Zu", 256, 512), R("OH"), col(PI), A.mult)
-        tt(R("Zu", 0, 256), IND(R("Bo"), u(U_C)), R("OH"), A.mult)
-        wrap(R("p3", 32, 64), "Zu", 0, 512)
-        mm(R("p6", 0, 256), R("BLK"), R("Zu", 0, 256), True, True)
+        tt(R("Zu"), IND(R("Bo"), u(U_C)), R("OH"), A.mult)
+        square(R("p5", 0, 256), 0, 256, True)
+        mm(R("p6", 0, 256), R("BLK"), R("Zu"), True, True)
+        if "a" in SCAN:
+            aw, add = own("s1", R("p6", 0, 256), 0, 256), col(C2K)
+        else:
+            aw, add = R("p3", 32, 48), 2048.0
+            wrap(aw, "Zu", 0, 256)
+        mm(R("p4", 64, 80), R("I256"), R("C1"), True, False)
+        wrap(R("p4", 64, 80), "T2", 0, 256, False, False, "WB16")
+        wrap(R("p4", 64, 80), "OH", 0, 256, False, True, "WBI")
         lin(R("srep"), R("p5", 0, 256), 1.0, 0.0)
-        ts(u(U_A), R("p3", 32, 48), 2048.0, A.add)
-        ts(w(W_C16), w(W_C), 16.0, A.mult)
-        ts(R("wi", 0, 16), R("p3", 32, 48), 2048.0, A.add)
-        tt(w(W_S), R("p3", 48, 64), w(W_C16), A.add)
+        ts(u(U_A), aw, add, A.add)
+        ts(R("wi", 0, 16), aw, add, A.add)
+        lin(w(W_S), R("p4", 64, 80), 1.0, 0.0)
+        step[0] = "aside"
         cp(u(U_S), w(W_S))
-        ts(R("so"), R("srep"), 2048.0, A.subtract)
         act(R("dm"), R("srep"), F.Relu, bias=-4095.0)
-        lin(R("arep"), R("p6", 0, 256), 1.0, -2048.0)
+        lin(R("arep"), R("p6", 0, 256), col(AS), col(AO))
         act(R("absb"), R("p6", 0, 256), F.Abs, bias=col(AB))
-        act(R("absb"), R("absb"), F.Relu, bias=-255.5 * 8192, scale=8192.0)
+        act(R("nb"), R("absb"), F.Relu, bias=-255.5 * 64, scale=64.0)
         ts(R("wi", 16, 32), R("wi", 0, 16), 511, A.bitwise_and)
         cp(u(U_A9), R("wi", 16, 32))
         gather(R("hg"), IND(R("hmf"), u(U_A9)))
-        gather(R("xa"), IND(R("xsb"), u(U_A)))
-        lin(R("p2", 0, 256), R("xa"), 1.0, 0.0)
-        for (lo, hi) in PARTS:
+        for lo, hi in HALVES:
+            step[0] = "targets %d" % lo
+            gather(R("xa", lo, hi), IND(XS, u(U_A, lo, hi)))
             targets(U_A, "srep", lo, hi, 0)
-            for c in range(lo, hi, CH):
-                gather(R("xv", 16 * c, 16 * (c + CH)), IND(R("XB"), R("q16", c, c + CH)))
-        for c in range(0, 256, 64):
+        for b in range(4):
+            step[0] = "compare %d" % b
+            lo, hi = 64 * b, 64 * b + 64
+            pc = R("p3" if b % 2 else "p4", 128 + lo, 128 + hi)
+            mine = WHO[t][b] == "V"
+            if mine:
+                lin(R("p2", lo, hi), R("xa", lo, hi), 1.0, 0.0)
+            for c in range(lo, hi, 32):
+                xv, pd = R("xv", 16 * c, 16 * c + 512), "p%d" % (c // 32 % 2)
+                gather(xv, IND(R("XB%d" % t, 0, S), R("q16", c, c + 32)), XV[c // 32])
+                if not mine:
+                    mm(R(pd), R("NI"), xv, True, False)
+                    for k in range(16):
+                        mm(R(pd, 0, 512, 16, k), R("ID"), R("xa", c, c + 32), False, k == 15)
+                    act(R("cmp", 16 * c, 16 * c + 512), R(pd), F.Sign, bias=-TINY)
             for k in range(16):
-                tt(R("cmp", 256 * k + c, 256 * k + c + 64), R("xv", 16 * c, 16 * c + 1024, 16, 16 * c + k),
-                   R("p2", c, c + 64), A.is_lt)
-                mm(R("p0", c, c + 64) if c < PARTS[0][1] else R("p7", 256 + c, 320 + c), mat("WR", k), R("cmp", 256 * k + c, 256 * k + c + 64), k == 0, k == 15)
-        for (lo, hi) in PARTS:
-            ts(R("good", lo, hi), R("p0", lo, hi) if lo == 0 else R("p7", 256 + lo, 256 + hi), 8.0, A.is_ge)
-            mm(R("p1", lo, hi), R("TRI"), R("good", lo, hi), True, True)
-            ts(R("p2", 256 + lo, 256 + hi), R("p1", lo, hi), 1.0, A.is_equal)
-            pick("so", lo, hi, 0, W_S, W_X, W_AT)
-            cp(u(U_AT, lo, hi), w(W_AT, lo, hi))
-            lin(R("atrep", lo, hi), R("p5", lo, hi), 1.0, 2048.0)
-            ts(R("who", lo, hi), IND(bdw, u(U_AT, lo, hi)), 2048.0, A.add, col(M0), A.mult)
-            wrap(R("p4", lo // 16, hi // 16), "who", lo, hi)
-            ts(u(U_W, lo, hi), R("p4", lo // 16, hi // 16), 2048.0, A.add)
+                if mine:
+                    o = R("cmp", 16 * lo + 64 * k, 16 * lo + 64 * k + 64)
+                    tt(o, R("xv", 16 * lo, 16 * hi, 16, 16 * lo + k), R("p2", lo, hi), A.is_lt)
+                    row("compare")
+                else:
+                    o = R("cmp", 16 * lo, 16 * hi, 16, 16 * lo + k)
+                mm(pc, R("WB", 15 - k, 143 - k), o, k == 0, k == 15)
+            act(R("good", lo, hi), pc, F.Sign, bias=-7.5 if mine else 0.5)
+        for h, (lo, hi) in enumerate(HALVES):
+            pb, pw = ("p5", "p4") if h == 0 else ("p6", "p3")
+            good = R("good", lo, hi)
+            step[0] = "claim %d" % h
+            mm(R(pb, 256, 384), R("ID"), R("qo", lo, hi), True, False)
+            mm(R(pb, 256, 384), R("TRI"), good, False, True)
+            square(R("p7", lo, hi), lo, hi, False)
+            mm(R("p7", lo, hi), R("B2K"), good, False, True)
+            mm(R("p7", 256 + lo, 256 + hi), R("NI"), R("nb", lo, hi), True, False)
+            mm(R("p7", 256 + lo, 256 + hi), R("BLK"), good, False, True)
+            ts(R("Z", lo, hi), R(pb, 256, 384), col(ZK), A.add, 2048.0, A.min)
+            act(R("back", lo, hi), R("p7", lo, hi), F.Relu, bias=S - 32768.0, scale=-1.0)
+            act(R("A1", lo, hi), R("p7", 256 + lo, 256 + hi), F.Sign, bias=-15.0, scale=-1.0)
+            at = R(pb, lo, hi)
+            mm(at, R("NI32"), R("back", lo, hi), True, False)
+            mm(at, R("BLK"), R("Z", lo, hi), False, True)
+            aw = own("s2", at, lo, hi)
+            ts(u(U_AT, lo, hi), aw, col(CRAW), A.add)
+            lin(w(W_AT, lo, hi), aw, 1.0, col(CRAW))
+            lin(R("atrep", lo, hi), at, 1.0, 0.0)
+            ts(R("key", lo, hi), at, RAW + 2048.0, A.subtract)
+            step[0] = "victim %d" % h
+            lin(R("whom", lo, hi), IND(bdw, u(U_AT, lo, hi)), col(M2), col(MO))
+            mm(R(pw, 0, 128), R("R0"), R("whom", lo, hi), True, True)
+            ts(u(U_W, lo, hi), own("s1", R(pw, 0, 128), lo, hi), col(C4K), A.add)
             targets(U_W, "atrep", lo, hi, 256)
+            step[0] = "free %d" % h
             for c in range(lo, hi, CH):
-                o, i = R("fr", 16 * c, 16 * (c + CH)), IND(bdw, R("q16", 256 + c, 256 + c + CH))
-                put([a_act(o, i, F.Relu, col(M0), col(M0)), a_ts(o, i, 0.0, A.is_equal, col(M0), A.mult)], [o], [i, col(M0)])
-        lin(R("whom"), IND(bdw, u(U_AT)), col(M0), 0.0)
-        tt(w(W_D), w(W_AT), w(W_S), A.subtract)
-        for c in range(0, 256, 64):
-            pb = "p1" if c < 128 else "p0"
-            mm(R(pb, c, c + 64), R("HB"), R("ones", c, c + 64), True, False)
-            for k in range(16):
-                mm(R(pb, c, c + 64), mat("TR", k), R("fr", 16 * c, 16 * c + 1024, 16, 16 * c + k), False, k == 15)
-        act(R("p6", 256, 512), R("p6", 0, 256), F.Abs)
-        tt(R("A1"), R("absb"), R("p6", 256, 512), A.is_lt)
-        dedupe(W_AT, 0)
-        ts(R("Zp", 256, 512), R("p7", 0, 256), 0.0, A.is_equal)
-        tt(R("fl"), R("p7", 0, 256), R("A1"), A.is_lt)
-        ts(w(W_D), w(W_D), 1.0 / 16, A.mult)
-        scan(R("p6", 0, 256), R("fl"), R("ones"), col(ZI), A.add, A.subtract)
-        tt(R("Zp", 0, 256), R("p6", 0, 256), R("fl"), A.mult)
-        wrap(R("p4", 32, 64), "Zp", 0, 512)
-        tt(w(W_Y), R("p4", 48, 64), w(W_D), A.mult)
-        tt(w(W_FB), w(W_Y), w(W_S), A.add)
-        cp(u(U_FB), w(W_FB))
-        tt(w(W_P), R("p4", 32, 48), R("dwr"), A.add)
-        cp(u(U_P), w(W_P))
-        tt(IND(R(PW), u(U_P)), R("whom"), R("hg"), A.add)
-        mine = masks_from(core, cores, topo)
-        trs = []
+                empty(R("fr", 16 * c, 16 * (c + CH)), IND(bdw, R("q16", 256 + c, 256 + c + CH)), FR[c // 32])
+        step[0] = "payload"
         for p in range(N):
             z = 256 * (p if p < 4 else p + 1)
-            if p == rank:
-                lin(R(land, 16 * rank, 16 * rank + 16), R(PW, z, z + 16), 1.0, 0.0)
-                continue
-            rid, pid, _e = topo.addr(cores[p])
-            trs.append(RemoteDMATransfer(dst_ids=[DstId(rid=rid, pnc=pid)], dma_engine_mask=sum(1 << e for e in mine[cores[p]]),
-                                         remote_sem=T.sem["arr%d" % t], src=T[PW][:, z:z + 16],
-                                         dst=T[land][:, 16 * rank:16 * rank + 16]))
+            iota(R(PW, z, z + 16), [[2, 16]], REB0 + int(LIFT) + 32 * rank, 0)
+        for lo, hi in HALVES:
+            mm(R("p2", 256 + lo, 256 + hi), R("IO32"), R("hg", lo, hi), True, False)
+            mm(R("p2", 256 + lo, 256 + hi), R("ID32"), R("whom", lo, hi), False, True)
+            lin(R("pay", lo, hi), R("p2", 256 + lo, 256 + hi), 1.0, LIFT)
+        tt(w(W_D), w(W_AT), w(W_S), A.subtract)
+        for h, (lo, hi) in enumerate(HALVES):
+            pb = "p1" if h == 0 else "p2"
+            step[0] = "weigh %d" % h
+            mm(R(pb, 0, 128), R("ID"), R("qo", 256 + lo, 256 + hi), True, False)
+            for c in range(0, 128, 64):
+                for k in range(16):
+                    z = 16 * (lo + c)
+                    mm(R(pb, c, c + 64), R("TR", 128 * k, 128 * k + 128), R("fr", z, z + 1024, 16, z + k), False, False)
+        banks = ["p0", "p3"] if SPLIT else ["p0"]
+        dedupe(banks, W_AT, 0)
+        for b, (lo, hi) in zip(banks, HALVES if SPLIT else [(0, 256)]):
+            n = hi - lo
+            step[0] = "send"
+            fl, pp = R("Zp", 2 * lo + n, 2 * hi), 32 + lo // 8
+            act(R("lose", lo, hi), R(b, lo, hi), F.Relu, scale=-4096.0)
+            tt(fl, R(b, lo, hi), R("A1", lo, hi), A.is_gt)
+            scan(R("p7", lo, hi), fl, R("ones", lo, hi), R("p7", lo - 1, lo) if lo else col(ZI), A.add, A.subtract)
+            tt(R("Zp", 2 * lo, 2 * lo + n), R("p7", lo, hi), fl, A.mult)
+            mm(R("p4", pp, pp + n // 8), R("ID"), R("dwr", lo // 8, hi // 8), True, False)
+            wrap(R("p4", pp, pp + n // 8), "Zp", 2 * lo, 2 * hi, False)
+            cp(u(U_P, lo, hi), R("p4", pp, pp + n // 16))
+            tt(w(W_Y, lo, hi), R("p4", pp + n // 16, pp + n // 8), w(W_D, lo, hi), A.mult)
+            act(IND(R(PW), u(U_P, lo, hi)), R("pay", lo, hi), F.Silu)
+        tt(w(W_FB), w(W_Y), w(W_S), A.add)
+        cp(u(U_FB), w(W_FB))
+        z = 256 * (rank if rank < 4 else rank + 1)
+        lin(R(land, 16 * rank, 16 * rank + 16), R(PW, z, z + 16), 1.0, 0.0)
         sent = ext(None, "sent%d" % t)
-        put([("G", (lambda trs, t: lambda: g.remote_dma_fused(trs, local_sem=T.sem["snt%d" % t]))(trs, t), 500.0)],
-            [sent], [R(PW)], "snt%d" % t, -sum(len(v) for v in mine.values()), FAR, keep=True)
-        arrivals = sum(len(masks_from(c, cores, topo)[core]) for c in cores if c != core)
+        for mine in masks_from(core, cores, topo):
+            trs = []
+            for c in mine:
+                p = cores.index(c)
+                z = 256 * (p if p < 4 else p + 1)
+                rid, pid, _e = topo.addr(c)
+                trs.append(RemoteDMATransfer(dst_ids=[DstId(rid=rid, pnc=pid)], dma_engine_mask=sum(1 << e for e in mine[c]),
+                                             remote_sem=T.sem["arr%d" % t], src=T[PW][:, z:z + 16],
+                                             dst=T[land][:, 16 * rank:16 * rank + 16]))
+            put([("G", (lambda trs, t: lambda: g.remote_dma_fused(trs, local_sem=T.sem["snt%d" % t]))(trs, t), 300.0)],
+                [sent], [R(PW)], "snt%d" % t, -sum(len(v) for v in mine.values()), FAR, keep=True)
+        arrivals = sum(len(call[core]) for c in cores if c != core for call in masks_from(c, cores, topo) if core in call)
         put([("X", None, 0.0)], [(None, [(land, 16 * p, 16 * p + 16) for p in range(N) if p != rank], [])], [sent],
             "arr%d" % t, -arrivals)
-        tt(R("p2", 256, 384), R("p1", 0, 128), R("Zp", 256, 384), A.is_equal)
-        tt(R("p2", 384, 512), R("p0", 128, 256), R("Zp", 384, 512), A.is_equal)
-        for (lo, hi) in PARTS2:
-            pick("key", lo, hi, 256, W_AT, W_X2, W_K)
-        act(IND(bdw, u(U_S)), R("neg"), F.Sigmoid)
-        act(IND(bdw, u(U_FB)), R("neg"), F.Sigmoid)
-        ts(R("h16"), R(land), 2048.0, A.subtract, col(MH), A.mult)
-        wrap(R("p4", 0, 8), "h16", 0, 128)
-        ts(u(U_H, 0, 128), R("p4", 0, 8), 2048.0, A.add)
-        dedupe(W_K, 256)
-        tt(R("T1"), R("p7", 0, 256), R("MK"), A.is_equal)
-        scan(R("sg"), R("keep"), R("T1"), 0.0, A.mult, A.add)
-        tt(w(W_D2), w(W_K), w(W_AT), A.subtract)
-        tt(w(W_Y2), R("sg", 0, 256, 16, 15), w(W_D2), A.mult)
-        tt(w(W_E), w(W_Y2), w(W_FB), A.add)
+        for h, (lo, hi) in enumerate(HALVES):
+            step[0] = "name %d" % h
+            pb = R("p1" if h == 0 else "p2", 0, 128)
+            mm(pb, R("ID"), R("lose", lo, hi), False, True)
+            ts(R("Z", 256 + lo, 256 + hi), pb, float(S), A.add, 2048.0, A.min)
+            mm(R("p6", lo, hi), R("BLK"), R("Z", 256 + lo, 256 + hi), True, True)
+            ts(R("key", 256 + lo, 256 + hi), R("p6", lo, hi), RAW + 2048.0, A.subtract)
+            if h == 1 or "0" in SCAN:
+                ts(w(W_K, lo, hi), own("s2", R("p6", lo, hi), lo, hi), col(CRAW), A.add, S - 0.5, A.min)
+            else:
+                wrap(R("p5", 384, 392), "Z", 256 + lo, 256 + hi)
+                ts(w(W_K, lo, hi), R("p5", 384, 392), RAW, A.subtract, S - 0.5, A.min)
+        dedupe(["p7"], W_K, 256)
+        step[0] = "ends"
+        ts(w(W_NZ), w(W_K), S - 0.75, A.is_lt, 2.0, A.mult)
+        tt(w(W_D1), w(W_K), w(W_FB), A.subtract)
+        tt(w(W_D2), w(W_D1), w(W_NZ), A.mult)
+        act(IND(bdw, u(U_S)), R("neg"), F.Silu)
+        act(IND(bdw, u(U_FB)), R("neg"), F.Silu)
+        ts(R("rl"), R(land), ROUND, A.add, ROUND + LIFT, A.subtract)
+        mm(R("p4", 0, 128), R("RH"), R(land), True, True)
+        ts(u(U_H, 0, 128), own("s1", R("p4", 0, 128), 0, 128), col(CB), A.add, LIFT, A.subtract)
+
+        def reborn():
+            ts(R("em"), IND(bdw, u(U_H, 0, 128)), col(NONE), A.is_equal)
+            gather(R("old"), IND(bdw, u(U_H, 0, 128)))
+            tt(R("dd"), R("em"), R("rl"), A.mult)
+            tt(IND(bdw, u(U_H, 0, 128)), R("old"), R("dd"), A.add)
+        if EARLY[t]:
+            reborn()
+        scan(R("sg"), R("keep"), R("p7", 0, 256), 0.0, A.mult, A.max)
+        tt(w(W_Y), R("sg", 0, 256, 16, 15), w(W_D2), A.mult)
+        tt(w(W_E), w(W_Y), w(W_FB), A.add)
         cp(u(U_E), w(W_E))
         cp(IND(bdw, u(U_E)), R("arep"))
-        ts(R("em"), IND(bdw, u(U_H, 0, 128)), 0.0, A.is_equal)
-        gather(R("old"), IND(bdw, u(U_H, 0, 128)))
-        tt(R("dd"), R("em"), R(land), A.mult)
-        tt(IND(bdw, u(U_H, 0, 128)), R("old"), R("dd"), A.add)
+        if not EARLY[t]:
+            reborn()
         if t + 1 < RO:
-            dma(W("buff", T.buff[:, 0, :]), ext(T.bd[0:128:32, 0:S], "bd"), "Y", "dF", 65536)
-            dma(W("buff", T.buff[:, 1, :]), ext(T.bd[16:128:32, 0:S], "bd"), "S", "dF", 65536)
+            dma(W("buff", T.buff[:, 0, :]), ext(T.bd[2:128:32, 0:S], "bd"), "Y", "dF", 65536)
+            dma(W("buff", T.buff[:, 1, :]), ext(T.bd[18:128:32, 0:S], "bd"), "S", "dF", 65536)
+            cp(IND(R("XB1"), u(U_E)), R("xa"))
         else:
-            put([("G", lambda: g.dma_start(T.y[:, :], T.bd[0:128:16, 0:S], accum_op=A.add, max_dma_last_dim=8192), 500.0)],
-                [ext(None, "y")], [R("bd", 0, S)], "dY1", 16, DLAT, keep=True)
+            dma(ext(T.y[:, :], "y"), ext(T.bd[4:128:16, 0:S], "bd"), "Y", "dY", 131072)
 
     return ops
 

@@ -9,56 +9,60 @@ S = 4096
 RO = 2
 REB0 = 4352
 BW = 4608
+AW = 4104
 PWW = 2304
 LIFT = 8192.0
 ROUND = 1.5 * 2 ** 23
 HALVES = [(0, 128), (128, 256)]
-WHO = ["VVVV", "VVVV"]
-SCAN = "s"
-CH = 32
-TINY = 2.0 ** -110
 BIG = 65536.0
 DLAT = 2000.0
 MODELS = [dict(far=4500.0, pe=0.54, cy=1.04, ga=1.56, sc=3.8, wake=60.0, bpn=310.0),
           dict(far=3500.0, pe=0.47, cy=0.9, ga=1.3, sc=2.8, wake=90.0, bpn=260.0),
           dict(far=6500.0, pe=0.62, cy=1.2, ga=1.9, sc=5.0, wake=80.0, bpn=380.0),
           dict(far=5500.0, pe=0.6, cy=1.0, ga=1.4, sc=3.0, wake=120.0, bpn=340.0)]
-CALLS = 1
 SEED = 1
 HEAT = 0.002
 MIX = 3
-XV = "********"
-FR = "********"
-SPLIT = False
 LEAD = 3
-EARLY = [True, True]
-TRG = 10
-ROUNDS = 2200
+CX = [64, 64]
+CV = 32
+CF = 32
+SEARCH = [HALVES, HALVES]
+FIRST = [HALVES, HALVES]
+PC = ["p4", "p4", "p3", "p3"]
+GROUPS = [range(0, 4), range(4, 8), range(8, 12), range(12, 14), range(14, 15), range(15, 16)]
+SCAN = ["m", "m"]
+REB = [1, 1]
+DIRECT = True
+ROUNDS = 100
+STEPS = 42000
+MEAN = 0.02
+WARM = 0.001
+REACH = 40
 SPAN = []
 ORDER = []
 
 SCRATCH = {
     "bufi": ("sbuf", [128, 2, 128], "int32"), "buff": ("sbuf", [128, 2, 128], "float32"),
-    "buf4": ("sbuf", [128, 2, 128], "float32"), "buf2": ("sbuf", [128, 2, 128], "float32"), "TB": ("sbuf", [128, 8, 32], "bfloat16"),
+    "bufy": ("sbuf", [128, 2, 128], "float32"), "TB": ("sbuf", [128, 8, 32], "bfloat16"),
 }
 for _d, _names in (
-        ("int32", dict(dsb=4104, hmb=512, pci=8, Bi=256, X=256, wi=32, t=512, q=512)),
-        ("uint16", dict(xo=512, u16=256, q16=512)),
-        ("float16", dict(Zu=256, Z=512, Zp=512, qo=512, key=512, dwr=32)),
-        ("bfloat16", dict(xsb=4112, XB0=S, XB1=REB0, xv=S, cmp=S, fr=S, E=4352, LL=2048, TR=2048, WB=144, WB16=144, WBI=144,
-                          XP=144, grp=128, BLK=128, TRI=128, UP=128, B2K=128, B256=128, B16=128, DW=128, NI=128, tm=128,
-                          NB=128, ID=128, I16=128, I256=128, j16=256, keep=256, MK=256, SEL=256, M1b=256, c256=272,
-                          ones=256, f=272, cum=288, T1=256, T2=256, OH=256, C1=16, sg=256, nb=256, lose=256, A1=256,
-                          dm=256, xa=256, good=256)),
-        ("float32", dict(bd=BW, PW0=PWW, PW1=PWW, land0=128, land1=128, ID32=128, IO32=128, NI32=128, R0=128, RH=128, neg=256,
-                         col=24, clt=16, i16=16, M1=256, c4096=256, Bw=256, ox=256, Bo=272, G=272, L2=24, w32=160,
-                         srep=256, arep=256, absb=256, atrep=256, back=256, hmf=512, whom=256, hg=256, pay=256, s1=256,
-                         s2=256, rl=128, em=128, old=128, dd=128))):
+        ("int32", dict(dsb=4104, hmb=512, pci=8, X=256, wi=32, t=512, q=512)),
+        ("uint16", dict(xo=512, u16=256, q16=512, key=512)),
+        ("float16", dict(Zu=256, Z=512, Zp=512, qo=512, dwr=32, f=272, rc=288, sc=256, whom=256, hg=256, l16=128, C2=16)),
+        ("bfloat16", dict(xsb=4128, XB0=S, XB1=REB0, xv=S, cmp=S, fr=S, E=4352, LL=2048, TR=2048, WB=144, WB16=144, WBI=144,
+                          WB0=144, WBH=144, XP=144, grp=128, BLK=128, TRI=128, UP=128, B2K=128, B256=128, B16=128, DW=128,
+                          NI=128, tm=128, NB=128, ID=128, I16=128, I256=128, N4K=128, N15=128, IE=128, IO=128, NBM=128,
+                          j16=128, keep=128, MK=128, SEL=128, B0=128, M1b=256, ones=272, T1=256, T2=256, OH=256, C1=16, sg=128,
+                          ge=256, A1=256, xa=256, good=256, fx=256, gl=128, zz=128)),
+        ("float32", dict(bd=BW, ba=AW, PW0=PWW, PW1=PWW, land0=128, land1=128, ID32=128, NI32=128, neg=256,
+                         col=24, clt=16, i16=16, M1=256, Bw=256, Bo=272, G=272, L2=24, w32=208, s1=512,
+                         srep=256, arep=256, atrep=256, back=256, pay=256, old=128, dd=128))):
     for _n in _names:
         SCRATCH[_n] = ("sbuf", [128, _names[_n]], _d)
 for _b in range(8):
     SCRATCH["p%d" % _b] = ("psum", [128, 512], "float32")
-SEMAPHORES = ["V", "S", "P", "G", "arr0", "arr1", "snt0", "snt1", "dB", "dX", "dD", "dR", "dH", "dF", "dY"]
+SEMAPHORES = ["V", "S", "P", "G", "arr0", "arr1", "snt0", "snt1", "dB", "dX", "dD", "dR", "dH", "dC", "dF", "dA", "dY"]
 
 
 def masks_from(src, cores, topo):
@@ -69,15 +73,8 @@ def masks_from(src, cores, topo):
     off = sorted(off, key=near)
     eng = list(topo.engines(src, off[0]))
     rest = [e for e in topo.engines(src, on[0]) if e not in eng]
-    if CALLS == 1:
-        out = [{c: eng[i::len(off)] for i, c in enumerate(off)}]
-        out[0][on[0]] = rest[:1]
-        return out
-    first = len(eng) // 2
-    out = []
-    for part in (off[:first], off[first:]):
-        out.append({c: eng[i::len(part)] for i, c in enumerate(part)})
-    out[0][on[0]] = rest[0:4:2]
+    out = {c: eng[i::len(off)] for i, c in enumerate(off)}
+    out[on[0]] = rest[:1]
     return out
 
 
@@ -203,7 +200,7 @@ def place(ops, before, after, rank, spare, m, lat, forward):
                             s = iv[lo][1] + gap
                             moved = True
                         lo += 1
-            v = s + c + (spare[j] if a else 0.0)
+            v = s + c + (spare[j] if a == len(o["alts"]) - 1 > 0 else 0.0)
             if best is None or v < best[0]:
                 best = (v, s, c, q, a, lists)
         v, s, c, q, a, lists = best
@@ -255,11 +252,11 @@ def plan(builds):
             for _ in range(int(rng.integers(3))):
                 k, v = either[int(rng.integers(len(either)))], float(rng.choice([0.0, 200.0, 500.0, 1000.0, 2000.0, 5000.0]))
                 spare = [v if kind[j] == k else spare[j] for j in range(n)]
-        else:
+        elif held:
             for _ in range(1 + int(rng.integers(3))):
                 i, j, a = held[int(rng.integers(len(held)))]
                 if len(ops[i]["alts"]) > 1 and rng.random() < 0.4:
-                    spare[i] = 5000.0 if a else -5000.0
+                    spare[i] = 5000.0 if a == len(ops[i]["alts"]) - 1 else -5000.0
                 elif rng.random() < 0.5:
                     now[i] = max(now[i], now[j]) + float(rng.choice([1.0, 300.0, 1500.0]))
                 else:
@@ -287,8 +284,125 @@ def plan(builds):
                     replay(b, before, order, x, held=held)
             if best is None or v <= best[0]:
                 best = (v, order, t)
-    SPAN[:] = best[2]
-    return best[1]
+    return refine(builds, before, after, best[1], rng)
+
+
+def refine(builds, before, after, order, rng):
+    n = len(order)
+    ops = builds[0]
+    names = {}
+    number = lambda x: names.setdefault(x, len(names))
+    on = [[number(q) for q, call, c in o["alts"]] for o in ops]
+    banks = [[number(b) for b in o["banks"]] for o in ops]
+    pe = [o["alts"][0][0] == "P" for o in ops]
+    cases = []
+    for b, m in zip(builds, MODELS):
+        cases.append(([[x[2] for x in o["alts"]] for o in b], [o["lat"] for o in b], [o["bytes"] / m["bpn"] for o in b],
+                      [[(i, 0.0 if pe[i] and pe[j] else m["wake"]) for i, link in before[j] if not link] for j in range(n)],
+                      m["wake"]))
+
+    def times(seq, alt, first, old):
+        out, v, state = [], 0.0, []
+        for (price, lat, flow, need, wake), (done, marks) in zip(cases, old):
+            done, marks = list(done), marks[:first // 32 + 1]
+            free, who, df = list(marks[-1][0]), list(marks[-1][1]), marks[-1][2]
+            for z in range(first // 32 * 32, n, 32):
+                for j in seq[z:z + 32]:
+                    a = alt[j]
+                    q = on[j][a]
+                    s = free[q]
+                    for i, d in need[j]:
+                        d += done[i]
+                        if d > s:
+                            s = d
+                    mine = banks[j]
+                    if mine:
+                        for b in mine:
+                            if who[b] != q and free[b] > s:
+                                s = free[b]
+                        s += price[j][a]
+                        free[q] = done[j] = s
+                        for b in mine:
+                            who[b], free[b] = q, s + wake
+                    else:
+                        s += price[j][a]
+                        free[q] = s
+                        if flow[j]:
+                            df = max(df, s + 0.6 * DLAT) + flow[j]
+                            done[j] = df + 0.4 * DLAT
+                        else:
+                            done[j] = s + lat[j]
+                marks.append((list(free), list(who), df))
+            end = max(done)
+            out.append(end)
+            state.append((done, marks))
+            v += math.log(end) + MEAN * sum(done) / (n * end)
+        return v, out, state
+
+    def chain(seq, alt):
+        held, k = [], int(rng.integers(len(MODELS)))
+        replay(builds[k], before, [(j, alt[j]) for j in seq], MODELS[k], held=held)
+        return held
+
+    def ahead(seq, lo, hi, links):
+        tied = {seq[hi - 1]}
+        for x in range(hi - 2, lo - 1, -1):
+            if any(i in tied for i, link in links[seq[x]]):
+                tied.add(seq[x])
+        return [x for x in seq[lo:hi] if x in tied], [x for x in seq[lo:hi] if x not in tied]
+
+    seq, alt = [j for j, a in order], [0] * n
+    for j, a in order:
+        alt[j] = a
+    either = [j for j in range(n) if len(on[j]) > 1]
+    cur, t, state = times(seq, alt, 0, [([0.0] * n, [([0.0] * len(names), [-1] * len(names), 0.0)])] * len(cases))
+    best, held, stale = (sum(math.log(x) for x in t), seq, alt, t), [], True
+    for r in range(STEPS):
+        move = float(rng.random())
+        new, pick = seq, alt
+        if move < 0.7 and (stale or r % 16 == 0):
+            held, stale = chain(seq, alt), False
+        if move < 0.7 and held:
+            i, j, a = held[int(rng.integers(len(held)))]
+            lo, hi = seq.index(i), seq.index(j) + 1
+            if lo >= hi:
+                continue
+            if move < 0.2:
+                x = i if len(on[i]) > 1 and (move < 0.1 or len(on[j]) == 1) else j
+                if len(on[x]) == 1:
+                    continue
+                pick = list(alt)
+                pick[x] = (alt[x] + 1 + int(rng.integers(len(on[x]) - 1))) % len(on[x])
+            elif move < 0.45:
+                tied, rest = ahead(seq, lo, hi, after)
+                new = seq[:lo] + tied + rest + seq[hi:]
+            else:
+                tied, rest = ahead(seq[lo:hi][::-1], 0, hi - lo, before)
+                new = seq[:lo] + rest[::-1] + tied[::-1] + seq[hi:]
+        elif move < 0.8:
+            x = either[int(rng.integers(len(either)))]
+            pick = list(alt)
+            pick[x] = (alt[x] + 1 + int(rng.integers(len(on[x]) - 1))) % len(on[x])
+        else:
+            lo = int(rng.integers(n - 1))
+            hi = min(n, lo + 2 + int(rng.integers(REACH)))
+            if move < 0.9:
+                tied, rest = ahead(seq, lo, hi, after)
+                new = seq[:lo] + tied + rest + seq[hi:]
+            else:
+                tied, rest = ahead(seq[lo:hi][::-1], 0, hi - lo, before)
+                new = seq[:lo] + rest[::-1] + tied[::-1] + seq[hi:]
+        if new == seq and pick is alt:
+            continue
+        v, t, then = times(new, pick, lo if pick is alt else seq.index(x), state)
+        if v <= cur - WARM * (1.0 - r / STEPS) * math.log(1.0 - float(rng.random())):
+            stale = stale or move < 0.7
+            cur, seq, alt, state = v, new, pick, then
+            v = sum(math.log(x) for x in t)
+            if v < best[0]:
+                best = (v, seq, alt, t)
+    SPAN[:] = best[3]
+    return [(j, best[2][j]) for j in best[1]]
 
 
 def build(g, core, T, topo, m):
@@ -349,6 +463,9 @@ def build(g, core, T, topo, m):
             return ("S", lambda: g.scalar.activation(o[0], i[0], func), cost(o, i, 1.0, 65.0))
         return ("S", lambda: g.scalar.activation(o[0], i[0], func, bias=ap(bias), scale=ap(scale)), cost(o, i, 1.0, 65.0))
 
+    def a_sel(o, i, pat, op, fill, base, ch):
+        return ("G", lambda: g.affine_select(o[0], i[0], pat, op, fill, base, ch), 170.0 + 2 * o[3] * CY)
+
     def cp(o, i):
         put([a_cp(o, i)], [o], [i])
 
@@ -360,7 +477,7 @@ def build(g, core, T, topo, m):
         put([a_ts(o, a, s1, op0, s2, op1)], [o], [a, s1, s2])
 
     def scan(o, a, b, init, op0, op1):
-        put([("V", lambda: g.vector.tensor_tensor_scan(o[0], a[0], b[0], ap(init), op0, op1), cost(o, a, half(o, a, b)))],
+        put([("V", lambda: g.vector.tensor_tensor_scan(o[0], a[0], b[0], ap(init), op0, op1), cost(o, a, 2 * half(o, a, b)))],
             [o], [a, b, init])
 
     def ms(o, c):
@@ -372,19 +489,33 @@ def build(g, core, T, topo, m):
     def lin(o, i, scale, bias):
         put([a_act(o, i, F.Identity, bias, scale), a_ts(o, i, scale, A.mult, bias, A.add)], [o], [i, scale, bias])
 
-    def either(alts, o, i, on):
-        put([a for a in alts if on in ("*", a[0])], [o], [i])
-        if on != "*":
-            row("large")
+    def relu(o, i, bias):
+        put([a_act(o, i, F.Relu, bias), a_ts(o, i, bias, A.add, 0.0, A.max)], [o], [i, bias])
+
+    def both(o, i, s_form, v_form):
+        put([a_act(o, i, *s_form), a_ts(o, i, *v_form)], [o], [i] + list(s_form[1:]) + list(v_form[0::2]))
 
     def row(name):
         ops[-1]["keep"] = name
 
-    def gather(o, i, on="*"):
-        either([a_act(o, i, F.Copy), a_cp(o, i)], o, i, on)
+    def gather(o, i):
+        put([a_act(o, i, F.Copy), a_cp(o, i)], [o], [i])
 
-    def empty(o, i, on):
-        either([a_act(o, i, F.Relu, 1.0), a_ts(o, i, 0.0, A.is_equal)], o, i, on)
+    def add_list(o, via, a, b):
+        if DIRECT:
+            tt(o, a, b, A.add)
+        else:
+            tt(via, a, b, A.add)
+            gather(o, via)
+
+    def join(n):
+        part = ops[-n:]
+        del ops[-n:]
+        calls = [o["alts"][0][1] for o in part]
+        ops.append(dict(part[0], rd=list(dict.fromkeys(x for o in part for x in o["rd"])),
+                        wr=list(dict.fromkeys(x for o in part for x in o["wr"])),
+                        banks=set(x for o in part for x in o["banks"]),
+                        alts=[(part[0]["alts"][0][0], lambda: [c() for c in calls][-1], sum(o["alts"][0][2] for o in part))]))
 
     def mm(o, l, r, start, stop):
         slow = 4 if SCRATCH[r[4]][2] == "float32" else 1
@@ -395,11 +526,10 @@ def build(g, core, T, topo, m):
             call = lambda: g.iota(o[0], pat, base, ch, allow_small_or_imprecise_dtypes=True)
         else:
             call = lambda: g.iota(o[0], pat, base, ch)
-        put([("G", call, 130.0 + 2 * o[3] * CY)], [o], [], keep=True)
+        put([("G", call, 130.0 + 2 * o[3] * CY)], [o], [])
 
-    def select(o, pat, op, fill, base, ch, i=None):
-        i = i or o
-        put([("G", lambda: g.affine_select(o[0], i[0], pat, op, fill, base, ch), 170.0 + 2 * o[3] * CY)], [o], [i], keep=True)
+    def select(o, pat, op, fill, base, ch):
+        put([a_sel(o, o, pat, op, fill, base, ch)], [o], [o])
 
     def dma(o, i, q, sem, nbytes):
         eng = g.sync if q == "Y" else g.scalar
@@ -408,20 +538,25 @@ def build(g, core, T, topo, m):
     def wrap(o, name, lo, hi, start=True, stop=True, base="WB"):
         for r in range(16):
             mm(o, R(base, 15 - r, 143 - r), R(name, lo, hi, 16, lo + r), start and r == 0, stop and r == 15)
+        join(16)
 
     def col(j):
         return R("col", j, j + 1)
 
-    def own(name, i, lo, hi):
-        scan(R(name, lo, hi), R("SEL", lo, hi), i, 0.0, A.add, A.min)
-        return R(name, lo, hi, 16, lo + 15)
+    held = [0]
+
+    def own(i):
+        z = held[0] % 4 * 128
+        held[0] += 1
+        scan(R("s1", z, z + i[3]), R("SEL", 0, i[3]), i, 0.0, A.add, A.min)
+        return R("s1", z, z + i[3], 16, z + 15)
 
     def ext(t, name="hbm"):
         return (t, [] if name == "hbm" else [(name, 0, S)], [], 0, name, False)
 
-    PG, PI, PW15, M0, MH, AB, ZI, ZJ, ZK, DW, AS, AO, M2, CB, C2K, C4K, CRAW, ODD, NONE, MO, NEG = range(21)
+    PG, PI, PW15, M0, MH, M15, AB, ZI, ZJ, ZK, DW, AS, AO, M2, CB, ODD, AC, C2K, CRAW = range(19)
     U_C1, U_C, U_A, U_A9, U_S, U_AT, U_W, U_P, U_FB, U_E, U_H = [16 * i for i in range(11)]
-    W_S, W_AT, W_D, W_Y, W_FB, W_K, W_NZ, W_D1, W_D2, W_E = [16 * i for i in range(10)]
+    W_S, W_AT, W_D, W_Y, W_FB, W_K, W_NZ, W_D1, W_D2, W_E, W_A, W_N, W_AD = [16 * i for i in range(13)]
 
     def u(c, lo=0, hi=256):
         return R("u16", c + lo // 16, c + hi // 16)
@@ -429,11 +564,15 @@ def build(g, core, T, topo, m):
     def w(c, lo=0, hi=256):
         return R("w32", c + lo // 16, c + hi // 16)
 
-    XS = R("xsb")
+    def pl(b, c, lo, hi):
+        return R(b, c + lo // 16, c + hi // 16)
+
+    XS = R("xsb", 16)
     RAW = 7.0 * S
+    bufi, buff, bufy = (W(x, T[x][:, :, :]) for x in ("bufi", "buff", "bufy"))
     for y in range(2):
         dma(W("bufi", T.bufi[:, y, :]), ext(T.board[y:8:2, :]), "Y", "dB", 65536)
-    dma(R("xsb", 0, S), ext(T.xs[:, :]), "Y", "dX", 1 << 20)
+    dma(R("xsb", 16, 16 + S), ext(T.xs[:, :]), "Y", "dX", 1 << 20)
     dma(R("dsb", 0, S), ext(T.ds[:, :]), "Y", "dD", 1 << 21)
     for y in range(2):
         dma(ext(T.hmb[y:128:2, :], "hmb"), ext(T.hm[:, :]), "Y", "dH", 131072)
@@ -442,22 +581,29 @@ def build(g, core, T, topo, m):
     iota(R("grp"), [[1, 8], [0, 16]], 0, 0)
     iota(R("i16"), [[1, 16]], 0, 0)
     iota(R("XP"), [[1, 144]], 0, -1)
-    iota(R("j16"), [[0, 16], [1, 16]], 0, 0)
+    iota(R("j16"), [[0, 8], [1, 16]], 0, 0)
     iota(R("M1b"), [[1, 256]], 0, 0)
+    iota(R("ba"), [[0, AW]], S, 0)
+    for o in ops[-7:]:
+        o["keep"] = "first"
+    iota(R("bd", S), [[0, BW - S]], S, 0)
+    iota(R("neg"), [[0, 256]], S, 0)
     iota(TB, [[0, 256]], 4096, 0)
     select(TB, [[0, 8], [1, 32]], A.is_gt, -4096.0, -15, 0)
     select(TB, [[0, 8], [1, 32]], A.is_ge, 0.0, -15, 0)
     select(TB, [[-16, 8], [0, 32]], A.is_equal, 0.0, 0, 1)
-    iota(R("bd"), [[0, BW]], 0, 0)
-    for k in range(TRG):
-        select(R("TR", 128 * k, 128 * k + 128), [[0, 128]], A.is_ge, 0.0, 0, 0, W("TB", T.TB[:, :, 15 - k:31 - k], 128))
-    for k in range(TRG, 16):
-        lin(R("TR", 128 * k, 128 * k + 128), W("TB", T.TB[:, :, 15 - k:31 - k], 128), 1.0, 0.0)
-    ms(R("c256"), 256.0)
-    ms(R("cum", 0, 16), 0.0)
+    for k in range(16):
+        o, i = R("TR", 128 * k, 128 * k + 128), W("TB", T.TB[:, :, 15 - k:31 - k], 128)
+        put([a_sel(o, i, [[0, 128]], A.is_ge, 0.0, 0, 0), a_act(o, i, F.Copy), a_cp(o, i)], [o], [i])
+    iota(R("NBM"), [[0, 128]], 0, 0)
+    select(R("NBM"), [[-1, 128]], A.not_equal, 32.0, 0, 1)
+    select(R("NBM"), [[-1, 128]], A.not_equal, -32.0, -1, 1)
+    ms(R("ones"), 1.0)
+    ms(R("rc", 0, 16), 0.0)
     ms(R("f", 256, 272), 1.0)
     ms(R("Bo", 256, 272), 2048.0)
-    ms(R("xsb", S, S + 16), 1e29)
+    ms(R("xsb", 0, 16), 1e29)
+    ms(R("xsb", 16 + S), 1e29)
     ms(R("dsb", S, S + 8), 0)
     ms(R("dwr"), 0.0)
     ts(R("pci", 2, 3), R("pci", 0, 1), 4, A.arith_shift_right)
@@ -468,90 +614,93 @@ def build(g, core, T, topo, m):
     ts(R("ID"), R("XP", 0, 128), 0.0, A.is_equal)
     ts(R("tm"), R("XP", 0, 128), 0.0, A.is_gt)
     tt(R("tm"), R("tm"), R("BLK"), A.mult)
-    lin(R("UP"), R("ID"), 512.0, 0.0)
+    lin(R("UP"), R("ID"), float(S), 0.0)
     tt(R("UP"), R("UP"), R("tm"), A.add)
     lin(col(PW15), col(PI), -1.0, 15.0)
     ts(R("WB"), R("XP"), col(PW15), A.is_equal)
     ts(R("MK"), R("j16"), col(PI), A.is_equal, 0.5, A.subtract)
     lin(R("SEL"), R("MK"), 33.0 * BIG, 15.5 * BIG)
-    for c, add in ((CB, 0.0), (C2K, 2048.0), (C4K, float(S)), (CRAW, -RAW)):
+    for c, add in ((CB, 0.0), (C2K, 2048.0), (CRAW, -RAW)):
         lin(col(c), col(PW15), BIG, add)
     lin(R("M1"), R("M1b"), 1.0, 0.0)
-    lin(R("ones"), R("M1b"), 0.0, 1.0)
-    ts(col(NONE), col(PI), 4.0, A.is_equal, float(S), A.mult)
-    lin(col(NEG), col(NONE), (S + 200.0) / S, -200.0)
-    lin(R("neg"), R("M1b"), 0.0, col(NEG))
-    put([("S", lambda: g.scalar.activation(T.L2[:, 16:24], T.cum[:, 0:8], F.Silu), 1400.0)], [R("L2", 16, 24)], [R("cum", 0, 8)])
+    put([("S", lambda: g.scalar.activation(T.L2[:, 16:24], T.rc[:, 0:8], F.Silu), 1400.0)], [R("L2", 16, 24)], [R("rc", 0, 8)])
     ts(R("keep"), R("j16"), 1.0, A.min)
     ts(col(M0), col(PI), 0.0, A.is_equal)
     ts(col(MH), col(PI), float(2 * rank + 1), A.is_equal)
-    for name, src, scale in (("I16", "ID", 16.0), ("I256", "ID", 256.0), ("NI", "ID", -1.0), ("ID32", "ID", 1.0),
+    ts(col(M15), col(PI), 15.0, A.is_equal, -1.0, A.mult)
+    ts(R("pci", 6, 7), R("pci", 0, 1), 1, A.bitwise_and)
+    cp(col(ODD), R("pci", 6, 7))
+    lin(col(M2), col(ODD), -1.0, 1.0)
+    for name, src, scale in (("I16", "ID", 16.0), ("NI", "ID", -1.0), ("ID32", "ID", 1.0),
                              ("NI32", "ID", -1.0), ("B16", "BLK", 16.0), ("B256", "BLK", 256.0), ("B2K", "BLK", 2048.0),
-                             ("NB", "BLK", -1.0), ("DW", "BLK", col(PI)), ("R0", "BLK", col(M0)), ("RH", "BLK", col(MH)),
-                             ("WB16", "WB", 16.0), ("WBI", "WB", col(PI))):
+                             ("N4K", "BLK", -4096.0), ("NB", "BLK", -1.0), ("DW", "BLK", col(PI)), ("N15", "BLK", col(M15)),
+                             ("WBI", "WB", col(PI)), ("WB0", "WB", col(M0)), ("B0", "BLK", col(M0)),
+                             ("IE", "ID", col(M2)), ("IO", "ID", col(ODD))):
         lin(R(name), R(src), scale, 0.0)
+    if "h" in SCAN[0]:
+        lin(R("WBH", 0, 128), R("BLK"), col(MH), 0.0)
+    else:
+        lin(R("WBH"), R("WB"), col(MH), 0.0)
     tt(R("TRI"), R("tm"), R("ID"), A.subtract)
     lin(R("TRI"), R("TRI"), 2048.0, 0.0)
-    lin(col(AB), col(PI), -512.0, 2048.0 - 255.5)
+    lin(col(AB), col(PI), -512.0, 2048.5)
+    lin(col(AC), col(AB), -1.0, 0.0)
     lin(col(ZK), col(PI), 2048.0, 2048.0)
     ts(R("clt"), R("i16"), col(PI), A.is_gt)
     for r in range(1, 16):
-        lin(R("LL", 128 * r, 128 * r + 128), R("NB"), R("clt", r, r + 1), 0.0)
+        o, i, c = R("LL", 128 * r, 128 * r + 128), R("NB"), R("clt", r, r + 1)
+        put([a_sel(o, i, [[16, 8], [0, 16]], A.is_gt, 0.0, r, -1), a_act(o, i, F.Identity, 0.0, c), a_ts(o, i, c, A.mult)],
+            [o], [i, c])
     ts(col(ZI), col(PI), 3.5, A.is_gt, 256.0, A.mult)
     lin(col(ZJ), col(PI), 256.0, -1024.0)
     tt(col(ZI), col(ZI), col(ZJ), A.add)
     lin(col(DW), col(PI), 1.0, 1024.0)
-    for lo, hi in HALVES if SPLIT else [(0, 256)]:
-        ts(R("dwr", lo // 8, (lo + hi) // 16), R("i16", lo // 16, hi // 16), 16.0, A.mult, col(DW), A.add)
+    ts(R("dwr", 0, 16), R("i16"), 16.0, A.mult, col(DW), A.add)
     ts(col(AS), col(PI), 2.0, A.not_equal)
-    ts(col(AO), col(AS), -2049.0, A.mult, col(NONE), A.add)
-    lin(col(AO), col(AO), 1.0, 1.0)
-    ts(R("pci", 6, 7), R("pci", 0, 1), 1, A.bitwise_and)
-    cp(col(ODD), R("pci", 6, 7))
-    lin(col(M2), col(ODD), -1.0, 1.0)
-    lin(col(MO), col(NONE), -1.0, 0.0)
-    lin(R("IO32"), R("ID"), col(ODD), 0.0)
-    ts(W("buff", T.buff[:, :, :]), W("bufi", T.bufi[:, :, :]), float(S), A.subtract)
+    lin(col(AO), col(AS), 2048.0 - 2 * S, 2.0 * S)
+    step[0] = "fold"
+    ts(R("X"), bufi, S + 1, A.bitwise_and)
+    both(R("p7", 0, 256), R("X"), (F.Relu, 2.0 * S, -2.0 * S), (0.0, A.is_equal, 2.0 * S, A.mult))
+    tt(buff, bufi, R("p7", 0, 256), A.add)
+    gather(bufy, bufi)
     for y in range(2):
-        dma(ext(T.bd[16 * y:128:32, 0:S], "bd"), W("buff", T.buff[:, y, :]), "Y", "dR", 65536)
-    ts(W("bufi", T.bufi[:, :, :]), W("bufi", T.bufi[:, :, :]), 4097, A.bitwise_and)
-    ts(R("p7", 0, 256), W("bufi", T.bufi[:, :, :]), 0.0, A.is_equal, 2.0 * S, A.mult)
-    tt(W("buf2", T.buf2[:, :, :]), W("buff", T.buff[:, :, :]), R("p7", 0, 256), A.add)
-    for y in range(2):
-        dma(ext(T.bd[16 * y + 2:128:32, 0:S], "bd"), W("buf2", T.buf2[:, y, :]), "Y", "dR", 65536)
-    lin(W("buf4", T.buf4[:, :, :]), W("buff", T.buff[:, :, :]), 1.0, float(S))
-    for y in range(2):
-        dma(ext(T.bd[16 * y + 4:128:32, 0:S], "bd"), W("buf4", T.buf4[:, y, :]), "Y", "dR", 65536)
-    cp(R("hmf"), R("hmb"))
+        dma(ext(T.ba[16 * y:128:32, 0:S], "ba"), W("bufy", T.bufy[:, y, :]), "Y", "dR", 65536)
+        dma(ext(T.ba[16 * y + 2:128:32, 0:S], "ba"), W("buff", T.buff[:, y, :]), "Y", "dR", 65536)
+    dma(R("bd", 0, S), R("ba", 0, S), "Y", "dC", 1 << 21)
 
-    bdw = R("bd")
+    bdw, baw = R("bd"), R("ba")
 
     def targets(lst, base, lo, hi, o):
         tt(R("t", o + lo, o + hi), IND(R("dsb"), u(lst, lo, hi)), R(base, lo, hi), A.add)
         ts(R("q", o + lo, o + hi), R("t", o + lo, o + hi), S - 1, A.bitwise_and)
-        cp(R("q16", o + lo, o + hi), R("q", o + lo, o + hi))
-        ts(R("qo", o + lo, o + hi), R("q16", o + lo, o + hi), 2048.0, A.subtract)
+        gather(R("q16", o + lo, o + hi), R("q", o + lo, o + hi))
+        lin(R("qo", o + lo, o + hi), R("q16", o + lo, o + hi), 1.0, -2048.0)
 
     def square(o, lo, hi, stop):
         for i, (mat, name) in enumerate((("B256", "T1"), ("B16", "T2"), ("DW", "OH"))):
             mm(o, R(mat), R(name, lo, hi), i == 0, stop and i == 2)
+        join(3)
 
-    def dedupe(pb, kw, o):
+    def dedupe(pb, kw, o, after):
         def equal(b, c, a, hi, stop=False):
             step[0] = "equal %d %d %d" % (o, c // 8, hi)
-            ts(R("E", 256 * c + a, 256 * c + hi), R("key", o + a, o + hi), 2048.0, A.add, R("w32", kw + c, kw + c + 1), A.is_equal)
+            ts(R("E", 256 * c + a, 256 * c + hi), R("key", o + a, o + hi), R("w32", kw + c, kw + c + 1), A.is_equal)
             row("equal")
             a = max(a, 16 * c + 16)
             if a < hi:
                 mm(R(b, a, hi), R("NB"), R("E", 256 * c + a, 256 * c + hi), False, stop)
 
         for b, (lo, hi) in zip(pb, HALVES if len(pb) > 1 else [(0, 256)]):
-            if o:
-                mm(R(b, lo, hi), R("ID"), R("MK", lo, hi), True, False)
-            mm(R(b, lo, hi), R("NB"), R("dm", lo, hi), o == 0, False)
+            mm(R(b, lo, hi), R("N15"), R("T1", lo, hi), True, False)
+            if o == 0:
+                mm(R(b, 0, 128), R("ID"), R("A1", 0, 128), False, False)
+            elif lo:
+                mm(R(b, lo, hi), R("ID"), R("MK"), False, False)
             early = LEAD if hi == 256 else 0
             for c in range(lo // 16, 8):
                 equal(b, c, 16 * c, 128)
+            if o == 0:
+                mm(R(b, 128, 256), R("ID"), R("A1", 128, 256), False, False)
             for c in range(early):
                 equal(b, c, 128, 256)
             for c in range(8, hi // 16):
@@ -560,8 +709,10 @@ def build(g, core, T, topo, m):
                 diag = (T.E[:, 17 * lo + r:17 * hi:272], [("E", 272 * i, 272 * i + 16) for i in range(lo // 16, hi // 16)],
                         [], 16, "E", False)
                 mm(R(b, lo, hi, 16, lo + r), R("LL", 128 * r, 128 * r + 128), diag, False, r == 15 and hi < 256)
+            join(15)
             for c in range(early, 8) if hi == 256 else []:
                 equal(b, c, 128, 256, c == 7)
+            after(lo, hi)
 
     for t in range(RO):
         PW = "PW%d" % t
@@ -570,93 +721,86 @@ def build(g, core, T, topo, m):
         for b in range(8):
             put([("V", (lambda b: lambda: g.vector.transpose(T.Bw[:, b:256:8], T.buff[:, :, 16 * b:16 * b + 16]))(b), 64 * CY)],
                 [R("Bw", 32 * b, 32 * b + 32)], [W("buff", None)])
-        if t == 0:
-            ts(R("Bi"), R("Bw"), float(S), A.add)
-            ts(R("X"), R("Bi"), 4097, A.bitwise_and)
-            ts(R("f", 0, 256), R("X"), 0.0, A.is_equal)
-            ts(R("p2", 256, 512), R("X"), 1.0, A.not_equal, float(S), A.mult)
-            tt(R("ox"), R("p2", 256, 512), R("Bw"), A.add)
-            ts(R("xo", 0, 256), R("ox"), 0.0, A.min, float(S), A.add)
-            for c in range(0, 256, CH):
-                gather(R("XB0", 16 * c, 16 * (c + CH)), IND(XS, R("xo", c, c + CH)))
-        else:
-            ts(R("f", 0, 256), R("Bw"), 0.0, A.is_lt)
-        lin(R("Bo", 0, 256), R("Bw"), 1.0, 2048.0)
-        mm(R("p0", 0, 272), R("BLK"), R("f"), True, True)
+        join(8)
+        ts(R("f", 0, 256), R("Bw"), float(S), A.is_lt if t else A.is_gt)
+        scan(R("rc", 16, 288), R("f"), R("ones"), 0.0, A.add, A.mult)
+        lin(R("Bo", 0, 256), R("Bw"), 1.0, -2048.0 if t else -2048.0 - 2 * S)
+        mm(R("p0", 0, 16), R("BLK"), R("rc", 16, 272, 16, 31), True, True)
+        ts(R("T1"), R("M1b"), own(R("p0", 0, 16)), A.subtract, col(CB), A.is_ge)
+        wrap(R("p4", 0, 17), "rc", 16, 288)
         mm(R("p1", 0, 272), R("UP"), R("f"), True, False)
-        scan(R("cum", 16, 288), R("p0", 0, 272), R("c256"), 0.0, A.add, A.min)
-        wrap(R("p4", 0, 17), "cum", 16, 288)
-        ends = own("s1", R("cum", 16, 272, 16, 31), 0, 16)
-        ts(R("T1"), R("M1b"), ends, A.subtract, col(CB), A.is_ge)
+        mm(R("p1", 0, 272), R("BLK"), R("rc", 15, 287), False, True)
         wrap(R("p3", 0, 16), "T1", 0, 256)
-        lin(R("L2", 0, 17), R("p4", 0, 17), 1.0 / 16, 0.0)
-        mm(R("p1", 0, 272), R("ID"), R("cum", 15, 287), False, True)
-        lin(R("G"), R("p1", 0, 272), 1.0, -512.0)
-        cp(u(U_C1), R("p3", 0, 16))
-        lin(R("C1"), R("p3", 0, 16), 1.0, 0.0)
+        lin(R("L2", 0, 17), R("p4", 0, 17), 1.0, 0.0)
+        lin(R("G"), R("p1", 0, 272), 1.0, -float(S))
+        gather(u(U_C1), R("p3", 0, 16))
+        gather(R("C1"), R("p3", 0, 16))
         if t == 0:
-            act(R("p2", 256, 512), R("G", 0, 256), F.Relu, bias=256.0 * S, scale=-float(S))
-            tt(R("ox"), R("p2", 256, 512), R("Bw"), A.add)
-            ts(R("xo", 256, 512), R("ox"), 0.0, A.min, float(S), A.add)
-            for c in range(0, 256, CH):
-                gather(R("XB1", 16 * c, 16 * (c + CH)), IND(XS, R("xo", 256 + c, 256 + c + CH)))
-        tt(R("T2"), IND(R("L2"), u(U_C1)), R("M1"), A.is_le)
-        mm(R("p4", 32, 48), R("I16"), R("C1"), True, False)
-        wrap(R("p4", 32, 48), "T2", 0, 256, False)
-        cp(u(U_C), R("p4", 32, 48))
-        tt(R("OH"), IND(R("G"), u(U_C)), R("M1"), A.is_equal)
-        tt(R("Zu"), IND(R("Bo"), u(U_C)), R("OH"), A.mult)
-        square(R("p5", 0, 256), 0, 256, True)
-        mm(R("p6", 0, 256), R("BLK"), R("Zu"), True, True)
-        if "a" in SCAN:
-            aw, add = own("s1", R("p6", 0, 256), 0, 256), col(C2K)
-        else:
-            aw, add = R("p3", 32, 48), 2048.0
-            wrap(aw, "Zu", 0, 256)
-        mm(R("p4", 64, 80), R("I256"), R("C1"), True, False)
-        wrap(R("p4", 64, 80), "T2", 0, 256, False, False, "WB16")
-        wrap(R("p4", 64, 80), "OH", 0, 256, False, True, "WBI")
-        lin(R("srep"), R("p5", 0, 256), 1.0, 0.0)
-        ts(u(U_A), aw, add, A.add)
-        ts(R("wi", 0, 16), aw, add, A.add)
-        lin(w(W_S), R("p4", 64, 80), 1.0, 0.0)
-        step[0] = "aside"
-        cp(u(U_S), w(W_S))
-        act(R("dm"), R("srep"), F.Relu, bias=-4095.0)
+            step[0] = "table 0"
+            ts(R("xo", 0, 256), R("Bw"), float(S), A.min)
+            for c in range(0, 256, CX[0]):
+                gather(R("XB0", 16 * c, 16 * (c + CX[0])), IND(XS, R("xo", c, c + CX[0])))
+            step[0] = "table 1"
+            both(R("fx"), R("G", 0, 256), (F.Relu, 256.0 * 4 * S, -4.0 * S), (256.0, A.is_lt, 4.0 * S, A.mult))
+            mm(R("p7", 0, 256), R("ID32"), R("Bo", 0, 256), True, False)
+            mm(R("p7", 0, 256), R("NI"), R("fx"), False, True)
+            relu(R("xo", 256, 512), R("p7", 0, 256), 2048.0 + 16)
+            for c in range(0, 256, CX[1]):
+                gather(R("XB1", 16 * c, 16 * (c + CX[1])), IND(R("xsb"), R("xo", 256 + c, 256 + c + CX[1])))
+        for lo, hi in SEARCH[t]:
+            step[0] = "level %d" % lo
+            tt(R("T2", lo, hi), IND(R("L2"), u(U_C1, lo, hi)), R("M1", lo, hi), A.is_le)
+            pb = "p4" if lo == 0 else "p0"
+            mm(pl(pb, 32, lo, hi), R("I16"), R("C1", lo // 16, hi // 16), True, False)
+            wrap(pl(pb, 32, lo, hi), "T2", lo, hi, False)
+            gather(u(U_C, lo, hi), pl(pb, 32, lo, hi))
+            gather(R("C2", lo // 16, hi // 16), u(U_C, lo, hi))
+        for lo, hi in SEARCH[t]:
+            step[0] = "row %d" % lo
+            pa, pb = ("p3", "p4") if lo == 0 else ("p2", "p0")
+            tt(R("OH", lo, hi), IND(R("G"), u(U_C, lo, hi)), R("M1", lo, hi), A.is_equal)
+            tt(R("Zu", lo, hi), IND(R("Bo"), u(U_C, lo, hi)), R("OH", lo, hi), A.mult)
+            square(R("p5", lo, hi), lo, hi, True)
+            aw = pl(pa, 32, lo, hi)
+            wrap(aw, "Zu", lo, hi)
+            lin(R("srep", lo, hi), R("p5", lo, hi), 1.0, 0.0)
+            lin(u(U_A, lo, hi), aw, 1.0, 2048.0)
+            step[0] = "aside"
+            mm(R("p6", lo, hi), R("BLK"), R("Zu", lo, hi), True, True)
+            lin(w(W_A, lo, hi), aw, 1.0, -2048.0)
+        mm(R("p0", 64, 80), R("I16"), R("C2"), True, False)
+        wrap(R("p0", 64, 80), "OH", 0, 256, False, True, "WBI")
+        gather(w(W_S), R("p0", 64, 80))
+        gather(u(U_S), w(W_S))
         lin(R("arep"), R("p6", 0, 256), col(AS), col(AO))
-        act(R("absb"), R("p6", 0, 256), F.Abs, bias=col(AB))
-        act(R("nb"), R("absb"), F.Relu, bias=-255.5 * 64, scale=64.0)
+        both(R("ge"), R("p6", 0, 256), (F.Sign, col(AB), 1.0), (col(AC), A.is_gt, 2.0, A.mult))
+        ts(R("wi", 0, 16), w(W_A), float(S), A.add)
         ts(R("wi", 16, 32), R("wi", 0, 16), 511, A.bitwise_and)
-        cp(u(U_A9), R("wi", 16, 32))
-        gather(R("hg"), IND(R("hmf"), u(U_A9)))
-        for lo, hi in HALVES:
+        gather(u(U_A9), R("wi", 16, 32))
+        lin(R("hg"), IND(R("hmb"), u(U_A9)), 1.0, -2048.0)
+        act(IND(bdw, u(U_S)), R("neg"), F.Silu)
+        for lo, hi in FIRST[t]:
             step[0] = "targets %d" % lo
-            gather(R("xa", lo, hi), IND(XS, u(U_A, lo, hi)))
             targets(U_A, "srep", lo, hi, 0)
+        for lo, hi in HALVES:
+            gather(R("xa", lo, hi), IND(XS, u(U_A, lo, hi)))
+            mm(R("p2", lo, hi), R("ID"), R("xa", lo, hi), True, True)
         for b in range(4):
             step[0] = "compare %d" % b
             lo, hi = 64 * b, 64 * b + 64
-            pc = R("p3" if b % 2 else "p4", 128 + lo, 128 + hi)
-            mine = WHO[t][b] == "V"
-            if mine:
-                lin(R("p2", lo, hi), R("xa", lo, hi), 1.0, 0.0)
-            for c in range(lo, hi, 32):
-                xv, pd = R("xv", 16 * c, 16 * c + 512), "p%d" % (c // 32 % 2)
-                gather(xv, IND(R("XB%d" % t, 0, S), R("q16", c, c + 32)), XV[c // 32])
-                if not mine:
-                    mm(R(pd), R("NI"), xv, True, False)
-                    for k in range(16):
-                        mm(R(pd, 0, 512, 16, k), R("ID"), R("xa", c, c + 32), False, k == 15)
-                    act(R("cmp", 16 * c, 16 * c + 512), R(pd), F.Sign, bias=-TINY)
-            for k in range(16):
-                if mine:
-                    o = R("cmp", 16 * lo + 64 * k, 16 * lo + 64 * k + 64)
+            pc = R(PC[b], 128 + lo, 128 + hi)
+            for c in range(lo, hi, CV):
+                gather(R("xv", 16 * c, 16 * (c + CV)), IND(R("XB%d" % t, 0, S), R("q16", c, c + CV)))
+            for ks in GROUPS:
+                outs = [(k, R("cmp", 16 * lo + 64 * k, 16 * lo + 64 * k + 64)) for k in ks]
+                for k, o in outs:
                     tt(o, R("xv", 16 * lo, 16 * hi, 16, 16 * lo + k), R("p2", lo, hi), A.is_lt)
-                    row("compare")
-                else:
-                    o = R("cmp", 16 * lo, 16 * hi, 16, 16 * lo + k)
-                mm(pc, R("WB", 15 - k, 143 - k), o, k == 0, k == 15)
-            act(R("good", lo, hi), pc, F.Sign, bias=-7.5 if mine else 0.5)
+                join(len(ks))
+                row("compare")
+                for k, o in outs:
+                    mm(pc, R("WB", 15 - k, 143 - k), o, k == 0, k == 15)
+                join(len(ks))
+            act(R("good", lo, hi), pc, F.Sign, bias=-7.5)
         for h, (lo, hi) in enumerate(HALVES):
             pb, pw = ("p5", "p4") if h == 0 else ("p6", "p3")
             good = R("good", lo, hi)
@@ -665,121 +809,142 @@ def build(g, core, T, topo, m):
             mm(R(pb, 256, 384), R("TRI"), good, False, True)
             square(R("p7", lo, hi), lo, hi, False)
             mm(R("p7", lo, hi), R("B2K"), good, False, True)
-            mm(R("p7", 256 + lo, 256 + hi), R("NI"), R("nb", lo, hi), True, False)
+            mm(R("p7", 256 + lo, 256 + hi), R("NBM"), R("ge", lo, hi), True, False)
             mm(R("p7", 256 + lo, 256 + hi), R("BLK"), good, False, True)
             ts(R("Z", lo, hi), R(pb, 256, 384), col(ZK), A.add, 2048.0, A.min)
             act(R("back", lo, hi), R("p7", lo, hi), F.Relu, bias=S - 32768.0, scale=-1.0)
-            act(R("A1", lo, hi), R("p7", 256 + lo, 256 + hi), F.Sign, bias=-15.0, scale=-1.0)
+            act(R("A1", lo, hi), R("p7", 256 + lo, 256 + hi), F.Sign, bias=-49.0)
             at = R(pb, lo, hi)
             mm(at, R("NI32"), R("back", lo, hi), True, False)
             mm(at, R("BLK"), R("Z", lo, hi), False, True)
-            aw = own("s2", at, lo, hi)
-            ts(u(U_AT, lo, hi), aw, col(CRAW), A.add)
+            aw = own(at)
+            lin(u(U_AT, lo, hi), aw, 1.0, col(CRAW))
             lin(w(W_AT, lo, hi), aw, 1.0, col(CRAW))
-            lin(R("atrep", lo, hi), at, 1.0, 0.0)
-            ts(R("key", lo, hi), at, RAW + 2048.0, A.subtract)
+            lin(R("atrep", lo, hi), at, 1.0, -RAW)
+            lin(R("key", lo, hi), at, 1.0, -RAW)
             step[0] = "victim %d" % h
-            lin(R("whom", lo, hi), IND(bdw, u(U_AT, lo, hi)), col(M2), col(MO))
-            mm(R(pw, 0, 128), R("R0"), R("whom", lo, hi), True, True)
-            ts(u(U_W, lo, hi), own("s1", R(pw, 0, 128), lo, hi), col(C4K), A.add)
+            lin(R("whom", lo, hi), IND(baw, u(U_AT, lo, hi)), 1.0, -2048.0)
+            if "vw"[h] in SCAN[t]:
+                mm(R(pw, 0, 128), R("B0"), R("whom", lo, hi), True, True)
+                lin(u(U_W, lo, hi), own(R(pw, 0, 128)), 1.0, col(C2K))
+            else:
+                wrap(R(pw, 0, 8), "whom", lo, hi, True, True, "WB0")
+                lin(u(U_W, lo, hi), R(pw, 0, 8), 1.0, 2048.0)
             targets(U_W, "atrep", lo, hi, 256)
+            step[0] = "payload"
+            mm(R(pb, 384, 512), R("IO"), R("hg", lo, hi), True, False)
+            mm(R(pb, 384, 512), R("IE"), R("whom", lo, hi), False, True)
+            lin(R("pay", lo, hi), R(pb, 384, 512), 1.0, LIFT + 2048.0)
             step[0] = "free %d" % h
-            for c in range(lo, hi, CH):
-                empty(R("fr", 16 * c, 16 * (c + CH)), IND(bdw, R("q16", 256 + c, 256 + c + CH)), FR[c // 32])
+            for c in range(lo, hi, CF):
+                both(R("fr", 16 * c, 16 * (c + CF)), IND(baw, R("q16", 256 + c, 256 + c + CF)),
+                     (F.Relu, 1.0 - S, 1.0), (float(S), A.is_equal))
         step[0] = "payload"
         for p in range(N):
             z = 256 * (p if p < 4 else p + 1)
             iota(R(PW, z, z + 16), [[2, 16]], REB0 + int(LIFT) + 32 * rank, 0)
-        for lo, hi in HALVES:
-            mm(R("p2", 256 + lo, 256 + hi), R("IO32"), R("hg", lo, hi), True, False)
-            mm(R("p2", 256 + lo, 256 + hi), R("ID32"), R("whom", lo, hi), False, True)
-            lin(R("pay", lo, hi), R("p2", 256 + lo, 256 + hi), 1.0, LIFT)
         tt(w(W_D), w(W_AT), w(W_S), A.subtract)
         for h, (lo, hi) in enumerate(HALVES):
             pb = "p1" if h == 0 else "p2"
             step[0] = "weigh %d" % h
             mm(R(pb, 0, 128), R("ID"), R("qo", 256 + lo, 256 + hi), True, False)
+            mm(R(pb, 0, 128), R("B2K"), R("A1", lo, hi), False, False)
             for c in range(0, 128, 64):
                 for k in range(16):
                     z = 16 * (lo + c)
                     mm(R(pb, c, c + 64), R("TR", 128 * k, 128 * k + 128), R("fr", z, z + 1024, 16, z + k), False, False)
-        banks = ["p0", "p3"] if SPLIT else ["p0"]
-        dedupe(banks, W_AT, 0)
-        for b, (lo, hi) in zip(banks, HALVES if SPLIT else [(0, 256)]):
-            n = hi - lo
-            step[0] = "send"
-            fl, pp = R("Zp", 2 * lo + n, 2 * hi), 32 + lo // 8
-            act(R("lose", lo, hi), R(b, lo, hi), F.Relu, scale=-4096.0)
-            tt(fl, R(b, lo, hi), R("A1", lo, hi), A.is_gt)
-            scan(R("p7", lo, hi), fl, R("ones", lo, hi), R("p7", lo - 1, lo) if lo else col(ZI), A.add, A.subtract)
-            tt(R("Zp", 2 * lo, 2 * lo + n), R("p7", lo, hi), fl, A.mult)
-            mm(R("p4", pp, pp + n // 8), R("ID"), R("dwr", lo // 8, hi // 8), True, False)
-            wrap(R("p4", pp, pp + n // 8), "Zp", 2 * lo, 2 * hi, False)
-            cp(u(U_P, lo, hi), R("p4", pp, pp + n // 16))
-            tt(w(W_Y, lo, hi), R("p4", pp + n // 16, pp + n // 8), w(W_D, lo, hi), A.mult)
-            act(IND(R(PW), u(U_P, lo, hi)), R("pay", lo, hi), F.Silu)
+                join(16)
+        dedupe(["p0"], W_AT, 0, lambda lo, hi: None)
+        step[0] = "send"
+        fl = R("Zp", 256, 512)
+        relu(fl, R("p0", 0, 256), 0.0)
+        relu(R("p7", 0, 256), R("p0", 0, 256), 0.0)
+        scan(R("sc"), fl, R("ones", 0, 256), col(ZI), A.add, A.subtract)
+        tt(R("Zp", 0, 256), R("sc"), R("p7", 0, 256), A.mult)
+        mm(R("p4", 32, 64), R("ID"), R("dwr"), True, False)
+        wrap(R("p4", 32, 64), "Zp", 0, 512, False)
+        gather(u(U_P), R("p4", 32, 48))
+        act(IND(R(PW), u(U_P)), R("pay"), F.Silu)
+        tt(w(W_Y), R("p4", 48, 64), w(W_D), A.mult)
         tt(w(W_FB), w(W_Y), w(W_S), A.add)
-        cp(u(U_FB), w(W_FB))
+        gather(u(U_FB), w(W_FB))
+        act(IND(bdw, u(U_FB)), R("neg"), F.Silu)
         z = 256 * (rank if rank < 4 else rank + 1)
-        lin(R(land, 16 * rank, 16 * rank + 16), R(PW, z, z + 16), 1.0, 0.0)
+        gather(R(land, 16 * rank, 16 * rank + 16), R(PW, z, z + 16))
         sent = ext(None, "sent%d" % t)
-        for mine in masks_from(core, cores, topo):
-            trs = []
-            for c in mine:
-                p = cores.index(c)
-                z = 256 * (p if p < 4 else p + 1)
-                rid, pid, _e = topo.addr(c)
-                trs.append(RemoteDMATransfer(dst_ids=[DstId(rid=rid, pnc=pid)], dma_engine_mask=sum(1 << e for e in mine[c]),
-                                             remote_sem=T.sem["arr%d" % t], src=T[PW][:, z:z + 16],
-                                             dst=T[land][:, 16 * rank:16 * rank + 16]))
-            put([("G", (lambda trs, t: lambda: g.remote_dma_fused(trs, local_sem=T.sem["snt%d" % t]))(trs, t), 300.0)],
-                [sent], [R(PW)], "snt%d" % t, -sum(len(v) for v in mine.values()), FAR, keep=True)
-        arrivals = sum(len(call[core]) for c in cores if c != core for call in masks_from(c, cores, topo) if core in call)
+        mine = masks_from(core, cores, topo)
+        trs = []
+        for c in mine:
+            p = cores.index(c)
+            z = 256 * (p if p < 4 else p + 1)
+            rid, pid, _e = topo.addr(c)
+            trs.append(RemoteDMATransfer(dst_ids=[DstId(rid=rid, pnc=pid)], dma_engine_mask=sum(1 << e for e in mine[c]),
+                                         remote_sem=T.sem["arr%d" % t], src=T[PW][:, z:z + 16],
+                                         dst=T[land][:, 16 * rank:16 * rank + 16]))
+        put([("G", (lambda trs, t: lambda: g.remote_dma_fused(trs, local_sem=T.sem["snt%d" % t]))(trs, t), 300.0)],
+            [sent], [R(PW)], "snt%d" % t, -sum(len(v) for v in mine.values()), FAR)
+        arrivals = sum(len(masks_from(c, cores, topo)[core]) for c in cores if c != core)
         put([("X", None, 0.0)], [(None, [(land, 16 * p, 16 * p + 16) for p in range(N) if p != rank], [])], [sent],
             "arr%d" % t, -arrivals)
         for h, (lo, hi) in enumerate(HALVES):
             step[0] = "name %d" % h
             pb = R("p1" if h == 0 else "p2", 0, 128)
-            mm(pb, R("ID"), R("lose", lo, hi), False, True)
-            ts(R("Z", 256 + lo, 256 + hi), pb, float(S), A.add, 2048.0, A.min)
+            mm(pb, R("N4K"), R("Zp", 256 + lo, 256 + hi), False, True)
+            ts(R("Z", 256 + lo, 256 + hi), pb, 9.0 * S, A.add, 2048.0, A.min)
             mm(R("p6", lo, hi), R("BLK"), R("Z", 256 + lo, 256 + hi), True, True)
-            ts(R("key", 256 + lo, 256 + hi), R("p6", lo, hi), RAW + 2048.0, A.subtract)
-            if h == 1 or "0" in SCAN:
-                ts(w(W_K, lo, hi), own("s2", R("p6", lo, hi), lo, hi), col(CRAW), A.add, S - 0.5, A.min)
+            lin(R("key", 256 + lo, 256 + hi), R("p6", lo, hi), 1.0, -RAW)
+            if "nm"[h] in SCAN[t]:
+                ts(w(W_K, lo, hi), own(R("p6", lo, hi)), col(CRAW), A.add, S - 0.5, A.min)
             else:
-                wrap(R("p5", 384, 392), "Z", 256 + lo, 256 + hi)
-                ts(w(W_K, lo, hi), R("p5", 384, 392), RAW, A.subtract, S - 0.5, A.min)
-        dedupe(["p7"], W_K, 256)
-        step[0] = "ends"
-        ts(w(W_NZ), w(W_K), S - 0.75, A.is_lt, 2.0, A.mult)
-        tt(w(W_D1), w(W_K), w(W_FB), A.subtract)
-        tt(w(W_D2), w(W_D1), w(W_NZ), A.mult)
-        act(IND(bdw, u(U_S)), R("neg"), F.Silu)
-        act(IND(bdw, u(U_FB)), R("neg"), F.Silu)
-        ts(R("rl"), R(land), ROUND, A.add, ROUND + LIFT, A.subtract)
-        mm(R("p4", 0, 128), R("RH"), R(land), True, True)
-        ts(u(U_H, 0, 128), own("s1", R("p4", 0, 128), 0, 128), col(CB), A.add, LIFT, A.subtract)
+                wrap(pl("p5", 384, lo, hi), "Z", 256 + lo, 256 + hi)
+                ts(w(W_K, lo, hi), pl("p5", 384, lo, hi), RAW, A.subtract, S - 0.5, A.min)
+            ts(w(W_NZ, lo, hi), w(W_K, lo, hi), S - 0.75, A.is_lt, 2.0, A.mult)
+            tt(w(W_D1, lo, hi), w(W_K, lo, hi), w(W_FB, lo, hi), A.subtract)
+            tt(w(W_D2, lo, hi), w(W_D1, lo, hi), w(W_NZ, lo, hi), A.mult)
 
         def reborn():
-            ts(R("em"), IND(bdw, u(U_H, 0, 128)), col(NONE), A.is_equal)
-            gather(R("old"), IND(bdw, u(U_H, 0, 128)))
-            tt(R("dd"), R("em"), R("rl"), A.mult)
-            tt(IND(bdw, u(U_H, 0, 128)), R("old"), R("dd"), A.add)
-        if EARLY[t]:
-            reborn()
-        scan(R("sg"), R("keep"), R("p7", 0, 256), 0.0, A.mult, A.max)
-        tt(w(W_Y), R("sg", 0, 256, 16, 15), w(W_D2), A.mult)
-        tt(w(W_E), w(W_Y), w(W_FB), A.add)
-        cp(u(U_E), w(W_E))
-        cp(IND(bdw, u(U_E)), R("arep"))
-        if not EARLY[t]:
-            reborn()
+            step[0] = "reborn"
+            ts(R("l16"), R(land), ROUND, A.add, ROUND + LIFT + 2048.0, A.subtract)
+            if "h" in SCAN[0]:
+                mm(R("p4", 0, 128), R("WBH", 0, 128), R("l16"), True, True)
+                lin(u(U_H, 0, 128), own(R("p4", 0, 128)), 1.0, col(C2K))
+            else:
+                wrap(R("p4", 0, 8), "l16", 0, 128, True, True, "WBH")
+                lin(u(U_H, 0, 128), R("p4", 0, 8), 1.0, 2048.0)
+            at = IND(bdw, u(U_H, 0, 128))
+            both(R("zz"), at, (F.Abs, -2.0 * S * S, 2.0 * S), (float(S), A.not_equal, 2.0 * S, A.mult))
+            gather(R("old"), at)
+            mm(R("p3", 0, 128), R("NI"), R("l16"), True, False)
+            mm(R("p3", 0, 128), R("NI"), R("zz"), False, True)
+            relu(R("dd"), R("p3", 0, 128), 2048.0)
+            tt(at, R("old"), R("dd"), A.subtract)
+
+        def ends(lo, hi):
+            if REB[t] == lo // 128:
+                reborn()
+            step[0] = "ends %d" % lo
+            if lo:
+                scan(R("sg"), R("keep"), R("p7", lo, hi), 0.0, A.mult, A.max)
+                go = R("sg", 0, 128, 16, 15)
+            else:
+                both(R("gl"), R("p0", 0, 128), (F.Relu, 0.5, 0.5), (-0.5, A.is_gt, 0.5, A.mult))
+                go = R("p1", 128, 136)
+                wrap(go, "gl", 0, 128, True, True, "WB0")
+            tt(w(W_Y, lo, hi), go, w(W_D2, lo, hi), A.mult)
+            add_list(u(U_E, lo, hi), w(W_E, lo, hi), w(W_Y, lo, hi), w(W_FB, lo, hi))
+            cp(IND(bdw, u(U_E, lo, hi)), R("arep", lo, hi))
+            if lo and REB[t] == 2:
+                reborn()
+
+        dedupe(["p0", "p7"], W_K, 256, ends)
+        step[0] = "next"
         if t + 1 < RO:
             dma(W("buff", T.buff[:, 0, :]), ext(T.bd[2:128:32, 0:S], "bd"), "Y", "dF", 65536)
             dma(W("buff", T.buff[:, 1, :]), ext(T.bd[18:128:32, 0:S], "bd"), "S", "dF", 65536)
+            dma(ext(T.ba[0:128:16, 0:S], "ba"), ext(T.bd[0:128:16, 0:S], "bd"), "Y", "dA", 131072)
             cp(IND(R("XB1"), u(U_E)), R("xa"))
         else:
-            dma(ext(T.y[:, :], "y"), ext(T.bd[4:128:16, 0:S], "bd"), "Y", "dY", 131072)
+            dma(ext(T.y[:, :], "y"), ext(T.bd[0:128:16, 0:S], "bd"), "Y", "dY", 131072)
 
     return ops
 

@@ -17,28 +17,54 @@ HALVES = [(0, 128), (128, 256)]
 BIG = 65536.0
 DLAT = 2000.0
 MODELS = [dict(far=4500.0, pe=0.54, cy=1.04, ga=1.56, sc=3.8, wake=60.0, bpn=310.0),
-          dict(far=3500.0, pe=0.47, cy=0.9, ga=1.3, sc=2.8, wake=90.0, bpn=260.0),
-          dict(far=6500.0, pe=0.62, cy=1.2, ga=1.9, sc=5.0, wake=80.0, bpn=380.0),
-          dict(far=5500.0, pe=0.6, cy=1.0, ga=1.4, sc=3.0, wake=120.0, bpn=340.0)]
+          dict(far=5200.0, pe=0.6, cy=1.14, ga=1.8, sc=4.6, wake=90.0, bpn=290.0),
+          dict(far=6000.0, pe=0.65, cy=1.24, ga=2.05, sc=5.8, wake=80.0, bpn=340.0)]
 SEED = 1
 HEAT = 0.002
 MIX = 3
-LEAD = 3
-CX = [64, 64]
-CV = 32
+PAIR = 2
+LEAD = 4
+CX = [64, 32]
+CV = [32, 32, 32, 32]
 CF = 32
 SEARCH = [HALVES, HALVES]
-FIRST = [HALVES, HALVES]
-PC = ["p4", "p4", "p3", "p3"]
+FIRST = [[(0, 64), (64, 128), (128, 256)]] * 2
+PC = ["p4", "p1", "p3", "p1"]
 GROUPS = [range(0, 4), range(4, 8), range(8, 12), range(12, 14), range(14, 15), range(15, 16)]
 SCAN = ["m", "m"]
+ANDU = False
+ONCE = 0.0
+PLAIN = True
+SPLIT = [False, False]
+XV = "********"
+FR = "********"
 REB = [1, 1]
 DIRECT = True
-ROUNDS = 100
-STEPS = 42000
-MEAN = 0.02
+ROUNDS = 40
+STEPS = 3000
+MEAN = 0.05
 WARM = 0.001
 REACH = 40
+SLACK = 1000.0
+TIDY = 100
+SORT = 100
+SWEEPS = 88
+WINDOW = 80
+TRIES = 200
+GLOW = 0.0007
+GLOW2 = 0.001
+FIRSTS = 3
+STARTS = 6
+NEAR = 0.02
+TABLE = 0
+CE = 64
+LIFTED = False
+WIDE = False
+LEAST = True
+CUT = ["rc"]
+BIAS = {}
+AHEAD = {}
+SHARE = dict(xv=0.9, fr=0.9)
 SPAN = []
 ORDER = []
 
@@ -47,22 +73,22 @@ SCRATCH = {
     "bufy": ("sbuf", [128, 2, 128], "float32"), "TB": ("sbuf", [128, 8, 32], "bfloat16"),
 }
 for _d, _names in (
-        ("int32", dict(dsb=4104, hmb=512, pci=8, X=256, wi=32, t=512, q=512)),
-        ("uint16", dict(xo=512, u16=256, q16=512, key=512)),
-        ("float16", dict(Zu=256, Z=512, Zp=512, qo=512, dwr=32, f=272, rc=288, sc=256, whom=256, hg=256, l16=128, C2=16)),
-        ("bfloat16", dict(xsb=4128, XB0=S, XB1=REB0, xv=S, cmp=S, fr=S, E=4352, LL=2048, TR=2048, WB=144, WB16=144, WBI=144,
+        ("int32", dict(dsb=4104, hmb=512, pci=8, X=256, t=512, q=512, wi=32)),
+        ("uint16", dict(xo=512, u16=256, q16=512, key=512, s2=256)),
+        ("float16", dict(Zu=256, Z=512, Zp=512, qo=512, dwr=64, f=272, rc=288, sc=256, whom=256, hg=256, l16=128, C2=16)),
+        ("bfloat16", dict(xsb=4128, XB0=S, XB1=REB0, xv=S, cmp=S, fr=S, E=4352, LL=2048, TR=2048, WB=144, WB2=144, WBI=144,
                           WB0=144, WBH=144, XP=144, grp=128, BLK=128, TRI=128, UP=128, B2K=128, B256=128, B16=128, DW=128,
-                          NI=128, tm=128, NB=128, ID=128, I16=128, I256=128, N4K=128, N15=128, IE=128, IO=128, NBM=128,
-                          j16=128, keep=128, MK=128, SEL=128, B0=128, M1b=256, ones=272, T1=256, T2=256, OH=256, C1=16, sg=128,
+                          NI=128, tm=128, NB=128, ID=128, I16=128, N2K=128, B15=128, N4I=128, BRAW=128, N4K=128, N15=128, IE=128, IO=128, NBM=128,
+                          j16=128, keep=128, MK=128, SEL=128, SE2=128, B0=128, M1b=256, ones=272, T1=256, T2=256, OH=256, C1=16, sg=128,
                           ge=256, A1=256, xa=256, good=256, fx=256, gl=128, zz=128)),
-        ("float32", dict(bd=BW, ba=AW, PW0=PWW, PW1=PWW, land0=128, land1=128, ID32=128, NI32=128, neg=256,
+        ("float32", dict(bd=BW, ba=AW, PW0=PWW, PW1=PWW, land0=128, land1=128, ID32=128, TI32=128, nat=256, neg=256,
                          col=24, clt=16, i16=16, M1=256, Bw=256, Bo=272, G=272, L2=24, w32=208, s1=512,
                          srep=256, arep=256, atrep=256, back=256, pay=256, old=128, dd=128))):
     for _n in _names:
         SCRATCH[_n] = ("sbuf", [128, _names[_n]], _d)
 for _b in range(8):
     SCRATCH["p%d" % _b] = ("psum", [128, 512], "float32")
-SEMAPHORES = ["V", "S", "P", "G", "arr0", "arr1", "snt0", "snt1", "dB", "dX", "dD", "dR", "dH", "dC", "dF", "dA", "dY"]
+SEMAPHORES = ["V", "S", "P", "G", "arr0", "arr1", "snt0", "snt1", "dB", "dX", "dD", "dR", "dH", "dC", "dF", "dA", "dN", "dY"]
 
 
 def masks_from(src, cores, topo):
@@ -73,8 +99,9 @@ def masks_from(src, cores, topo):
     off = sorted(off, key=near)
     eng = list(topo.engines(src, off[0]))
     rest = [e for e in topo.engines(src, on[0]) if e not in eng]
-    out = {c: eng[i::len(off)] for i, c in enumerate(off)}
-    out[on[0]] = rest[:1]
+    first = len(eng) // 2
+    out = [{c: eng[i::len(part)] for i, c in enumerate(part)} for part in (off[:first], off[first:])]
+    out[0][on[0]] = rest[0:4:2]
     return out
 
 
@@ -94,9 +121,11 @@ def schedule(ops):
                     if l2 < hi and lo < h2 and (w2 or writes) and not (o["sem"] and ops[i]["sem"] == o["sem"]):
                         pred[j][i] = 0
                 if q == "P" and psum(name) and writes:
-                    if name in lastq:
+                    if lastq.get(name, j) != j:
                         pred[j].setdefault(lastq[name], 2)
                     lastq[name] = j
+        for i in o.get("behind", []):
+            pred[j].setdefault(i, 2)
         if o["keep"]:
             row = (q, o["keep"])
             if row in lastq:
@@ -221,7 +250,7 @@ def place(ops, before, after, rank, spare, m, lat, forward):
     return st, en, alt
 
 
-def plan(builds):
+def plan(builds, seed):
     ops, m = builds[0], MODELS[0]
     n = len(ops)
     before, kind, kinds = schedule(ops)
@@ -230,9 +259,15 @@ def plan(builds):
         for i, link in before[j]:
             after[i].append((j, link))
     rank = [0.0] * n
+    later = {}
     for j in range(n - 1, -1, -1):
         rank[j] = min([0.0] + [rank[i] for i, link in after[j]]) - ops[j]["alts"][0][2] - ops[j]["lat"] - m["wake"]
-    rng = np.random.default_rng(SEED)
+        name = ops[j]["wr"][0][0]
+        if name == "fr":
+            rank[j] -= BIAS.get(ops[j]["step"][0], 0.0)
+        if name in SHARE:
+            rank[j] = later[name] = min(rank[j], later.get(name, 0.0) - SHARE[name] * ops[j]["alts"][0][2])
+    rng = np.random.default_rng(seed)
     lat = [0.0] * n
     either = sorted(set(kind[j] for j in range(n) if len(ops[j]["alts"]) > 1))
     steps = sorted(set(o["step"][0] for o in ops))
@@ -284,7 +319,19 @@ def plan(builds):
                     replay(b, before, order, x, held=held)
             if best is None or v <= best[0]:
                 best = (v, order, t)
-    return refine(builds, before, after, best[1], rng)
+    return polish(builds, before, after, best[1], rng, FIRSTS, GLOW)
+
+
+def best_plan(builds):
+    before = schedule(builds[0])[0]
+    after = [[] for _ in before]
+    for j, p in enumerate(before):
+        for i, link in p:
+            after[i].append((j, link))
+    found = sorted((plan(builds, SEED + i) for i in range(STARTS)), key=lambda x: x[0])
+    rng = np.random.default_rng(SEED)
+    found = sorted((polish(builds, before, after, x[1], rng, SWEEPS // 4, GLOW2) for x in found[:2]), key=lambda x: x[0])
+    return polish(builds, before, after, found[0][1], rng, SWEEPS, GLOW2)[1]
 
 
 def refine(builds, before, after, order, rng):
@@ -295,19 +342,22 @@ def refine(builds, before, after, order, rng):
     on = [[number(q) for q, call, c in o["alts"]] for o in ops]
     banks = [[number(b) for b in o["banks"]] for o in ops]
     pe = [o["alts"][0][0] == "P" for o in ops]
-    cases = []
+    cases, weight = [], np.full(n, 1.0 / n)
     for b, m in zip(builds, MODELS):
         cases.append(([[x[2] for x in o["alts"]] for o in b], [o["lat"] for o in b], [o["bytes"] / m["bpn"] for o in b],
                       [[(i, 0.0 if pe[i] and pe[j] else m["wake"]) for i, link in before[j] if not link] for j in range(n)],
                       m["wake"]))
 
-    def times(seq, alt, first, old):
+    def times(seq, alt, first, last, old):
         out, v, state = [], 0.0, []
-        for (price, lat, flow, need, wake), (done, marks) in zip(cases, old):
-            done, marks = list(done), marks[:first // 32 + 1]
+        for (price, lat, flow, need, wake), (was, past) in zip(cases, old):
+            done, marks = list(was), past[:first // 16 + 1]
             free, who, df = list(marks[-1][0]), list(marks[-1][1]), marks[-1][2]
-            for z in range(first // 32 * 32, n, 32):
-                for j in seq[z:z + 32]:
+            for z in range(first // 16 * 16, n, 16):
+                if z > last and marks[-1] == past[z // 16] and done == was:
+                    marks = past
+                    break
+                for j in seq[z:z + 16]:
                     a = alt[j]
                     q = on[j][a]
                     s = free[q]
@@ -336,13 +386,63 @@ def refine(builds, before, after, order, rng):
             end = max(done)
             out.append(end)
             state.append((done, marks))
-            v += math.log(end) + MEAN * sum(done) / (n * end)
+            v += math.log(end) + MEAN * float(np.dot(weight, done)) / end
         return v, out, state
 
-    def chain(seq, alt):
-        held, k = [], int(rng.integers(len(MODELS)))
-        replay(builds[k], before, [(j, alt[j]) for j in seq], MODELS[k], held=held)
-        return held
+    def weigh(seq, alt, state):
+        total = np.zeros(n)
+        for (price, lat, flow, need, wake), (done, marks) in zip(cases, state):
+            tail, rest, who = [0.0] * n, [0.0] * len(names), [-1] * len(names)
+            for j in seq[::-1]:
+                q = on[j][alt[j]]
+                s = max(tail[j], rest[q] - lat[j])
+                for b in banks[j]:
+                    if who[b] != q and rest[b] > s:
+                        s = rest[b]
+                tail[j] = s
+                s += lat[j] + price[j][alt[j]]
+                rest[q] = s
+                for b in banks[j]:
+                    who[b], rest[b] = q, s + wake
+                for i, d in need[j]:
+                    if s + d > tail[i]:
+                        tail[i] = s + d
+            total += np.exp(np.minimum(np.array(done) + np.array(tail) - max(done), 0.0) / SLACK)
+        weight[:] = total / total.sum()
+
+    def chain(seq, alt, state):
+        k = int(rng.integers(len(cases)))
+        price, lat, flow, need, wake = cases[k]
+        done, held = state[k][0], []
+        p = seq.index(done.index(max(done)))
+        while True:
+            j = seq[p]
+            q, s, by, z, left = on[j][alt[j]], 0.0, None, -1, set(banks[j])
+            for i, d in need[j]:
+                if done[i] + d > s:
+                    s, by = done[i] + d, i
+            mate = True
+            for x in range(p - 1, -1, -1):
+                i = seq[x]
+                if on[i][alt[i]] == q:
+                    if mate and not flow[i] and done[i] - lat[i] > s:
+                        s, z = done[i] - lat[i], x
+                    mate = False
+                    left.difference_update(banks[i])
+                elif left and not left.isdisjoint(banks[i]):
+                    if done[i] + wake > s:
+                        s, z = done[i] + wake, x
+                    left.difference_update(banks[i])
+                if not mate and not left:
+                    break
+            if z >= 0:
+                if all(i != seq[z] for i, link in before[j]):
+                    held.append((z, p))
+                p = z
+            elif by is None:
+                return held
+            else:
+                p = seq.index(by)
 
     def ahead(seq, lo, hi, links):
         tied = {seq[hi - 1]}
@@ -355,18 +455,32 @@ def refine(builds, before, after, order, rng):
     for j, a in order:
         alt[j] = a
     either = [j for j in range(n) if len(on[j]) > 1]
-    cur, t, state = times(seq, alt, 0, [([0.0] * n, [([0.0] * len(names), [-1] * len(names), 0.0)])] * len(cases))
+    cur, t, state = times(seq, alt, 0, n, [([0.0] * n, [([0.0] * len(names), [-1] * len(names), 0.0)])] * len(cases))
     best, held, stale = (sum(math.log(x) for x in t), seq, alt, t), [], True
     for r in range(STEPS):
         move = float(rng.random())
         new, pick = seq, alt
+        if r % SORT == 0:
+            log, k = [], int(rng.integers(len(cases)))
+            replay(builds[k], before, [(j, alt[j]) for j in seq], MODELS[k], log=log)
+            new = seq = [seq[x] for x in sorted(range(n), key=lambda x: (log[x][0], x))]
+            cur, t, state = times(seq, alt, 0, n, state)
+            stale = True
         if move < 0.7 and (stale or r % 16 == 0):
-            held, stale = chain(seq, alt), False
+            held, stale = chain(seq, alt, state), False
         if move < 0.7 and held:
-            i, j, a = held[int(rng.integers(len(held)))]
-            lo, hi = seq.index(i), seq.index(j) + 1
-            if lo >= hi:
-                continue
+            lo, hi = held[int(rng.integers(len(held)))]
+            i, j, hi = seq[lo], seq[hi], hi + 1
+        if r % TIDY == 0:
+            k = int(rng.integers(len(cases)))
+            d = float(rng.choice([100.0, 500.0, 5000.0]))
+            spare, lat = [-d if alt[j] == len(on[j]) - 1 else d for j in range(n)], [0.0] * n
+            st, en, pick = place(builds[k], before, after, state[k][0], spare, MODELS[k], lat, True)
+            if move < 0.7:
+                st, en, pick = place(builds[k], after, before, [-x for x in en], spare, MODELS[k], lat, False)
+                st, en, pick = place(builds[k], before, after, [-x for x in en], spare, MODELS[k], lat, True)
+            new, x = sorted(range(n), key=lambda j: (st[j], j)), None
+        elif move < 0.7 and held:
             if move < 0.2:
                 x = i if len(on[i]) > 1 and (move < 0.1 or len(on[j]) == 1) else j
                 if len(on[x]) == 1:
@@ -394,15 +508,202 @@ def refine(builds, before, after, order, rng):
                 new = seq[:lo] + rest[::-1] + tied[::-1] + seq[hi:]
         if new == seq and pick is alt:
             continue
-        v, t, then = times(new, pick, lo if pick is alt else seq.index(x), state)
+        if pick is not alt:
+            lo, hi = (0, n) if x is None else (seq.index(x),) * 2
+        v, t, then = times(new, pick, lo, hi, state)
         if v <= cur - WARM * (1.0 - r / STEPS) * math.log(1.0 - float(rng.random())):
-            stale = stale or move < 0.7
+            stale = True
             cur, seq, alt, state = v, new, pick, then
             v = sum(math.log(x) for x in t)
             if v < best[0]:
                 best = (v, seq, alt, t)
     SPAN[:] = best[3]
     return [(j, best[2][j]) for j in best[1]]
+
+
+def polish(builds, before, after, order, rng, sweeps, glow):
+    n = len(order)
+    ops = builds[0]
+    names = {}
+    number = lambda x: names.setdefault(x, len(names))
+    on = [[number(q) for q, call, c in o["alts"]] for o in ops]
+    banks = [[number(b) for b in o["banks"]] for o in ops]
+    pe = [o["alts"][0][0] == "P" for o in ops]
+    busy = [names["V"], names["S"], names["P"]]
+    width = len(names)
+    cases = []
+    for b, m in zip(builds, MODELS):
+        cases.append(([[x[2] for x in o["alts"]] for o in b], [o["lat"] for o in b], [o["bytes"] / m["bpn"] for o in b],
+                      [[(i, 0.0 if pe[i] and pe[j] else m["wake"]) for i, link in before[j] if not link] for j in range(n)],
+                      m["wake"]))
+
+    def run(case, part, alt, done, free, who, df):
+        price, lat, flow, need, wake = case
+        for j in part:
+            a = alt[j]
+            q = on[j][a]
+            s = free[q]
+            for i, d in need[j]:
+                d += done[i]
+                if d > s:
+                    s = d
+            mine = banks[j]
+            if mine:
+                for b in mine:
+                    if who[b] != q and free[b] > s:
+                        s = free[b]
+                s += price[j][a]
+                free[q] = done[j] = s
+                for b in mine:
+                    who[b], free[b] = q, s + wake
+            else:
+                s += price[j][a]
+                free[q] = s
+                if flow[j]:
+                    df = max(df, s + 0.6 * DLAT) + flow[j]
+                    done[j] = df + 0.4 * DLAT
+                else:
+                    done[j] = s + lat[j]
+        return df
+
+    def frame(case, seq, alt, a, b):
+        price, lat, flow, need, wake = case
+        done, free, who = [0.0] * n, [0.0] * width, [-1] * width
+        df = run(case, seq[:a], alt, done, free, who, 0.0)
+        tail, rest, next_, flows = [0.0] * n, [0.0] * width, [-1] * width, 0.0
+        for j in seq[:b - 1:-1] if b < n else []:
+            q = on[j][alt[j]]
+            if flow[j]:
+                flows = flow[j] + max(flows, 0.4 * DLAT + tail[j])
+                s = max(0.6 * DLAT + flows, rest[q])
+            else:
+                s = max(tail[j] + lat[j], rest[q])
+            for x in banks[j]:
+                if next_[x] != q and next_[x] >= 0 and rest[x] + wake > s:
+                    s = rest[x] + wake
+            s += price[j][alt[j]]
+            rest[q] = s
+            for x in banks[j]:
+                next_[x], rest[x] = q, s
+            for i, d in need[j]:
+                if s + d > tail[i]:
+                    tail[i] = s + d
+        return done, free, who, df, tail, rest, next_, flows, max([0.0] + [done[i] + tail[i] for i in seq[:a]])
+
+    def value(part, alt, frames):
+        v, ends = 0.0, []
+        for case, (done, free, who, df, tail, rest, next_, flows, over) in zip(cases, frames):
+            free, who = list(free), list(who)
+            df = run(case, part, alt, done, free, who, df)
+            end = max(over, df + flows, max([done[j] + tail[j] for j in part]),
+                      max([free[x] + rest[x] for x in range(width) if who[x] != next_[x] or who[x] < 0]))
+            ends.append(end)
+            v += math.log(end) + (MEAN * sum([done[j] for j in part]) / len(part)
+                                  + NEAR * sum([free[q] + rest[q] for q in busy])) / end
+        return v, ends
+
+    def chain(part, alt, k, frames):
+        price, lat, flow, need, wake = cases[k]
+        done, free, who, df, tail, rest, next_ = frames[k][:7]
+        run(cases[k], part, alt, done, list(free), list(who), df)
+        where, seen, top, held = {j: x for x, j in enumerate(part)}, set(), (0.0, 0), []
+        for x in range(len(part) - 1, -1, -1):
+            j = part[x]
+            q = on[j][alt[j]]
+            s = tail[j]
+            for y in [q] + banks[j]:
+                if y not in seen and (y == q or next_[y] != q):
+                    s = max(s, rest[y] - lat[j])
+                seen.add(y)
+            top = max(top, (done[j] + s, x))
+        p = top[1]
+        while True:
+            j = part[p]
+            q, s, by, z, left = on[j][alt[j]], 0.0, None, -1, set(banks[j])
+            for i, d in need[j]:
+                if done[i] + d > s:
+                    s, by = done[i] + d, i
+            mate = True
+            for x in range(p - 1, -1, -1):
+                i = part[x]
+                if on[i][alt[i]] == q:
+                    if mate and not flow[i] and done[i] - lat[i] > s:
+                        s, z = done[i] - lat[i], x
+                    mate = False
+                    left.difference_update(banks[i])
+                elif left and not left.isdisjoint(banks[i]):
+                    if done[i] + wake > s:
+                        s, z = done[i] + wake, x
+                    left.difference_update(banks[i])
+                if not mate and not left:
+                    break
+            if z >= 0:
+                if all(i != part[z] for i, link in before[j]):
+                    held.append((z, p))
+                p = z
+            elif by in where:
+                p = where[by]
+            else:
+                return held
+
+    def tied(part, links):
+        mine = {part[-1]}
+        for x in part[-2::-1]:
+            if any(i in mine for i, link in links[x]):
+                mine.add(x)
+        return [x for x in part if x in mine], [x for x in part if x not in mine]
+
+    seq, alt = [j for j, a in order], [0] * n
+    for j, a in order:
+        alt[j] = a
+    best = None
+    for sweep in range(sweeps):
+        log, k = [], sweep % len(cases)
+        replay(builds[k], before, [(j, alt[j]) for j in seq], MODELS[k], log=log)
+        seq = [seq[x] for x in sorted(range(n), key=lambda x: (log[x][0], x))]
+        warm = glow * (1.0 - sweep / sweeps)
+        for a in range(-int(rng.integers(WINDOW // 2)), n - WINDOW // 2, WINDOW // 2):
+            a, b = max(a, 0), min(n, a + WINDOW)
+            frames = [frame(case, seq, alt, a, b) for case in cases]
+            part = seq[a:b]
+            cur, ends = value(part, alt, frames)
+            held, stale = [], True
+            idle = all(max(f[8], f[3] + f[7]) > e - 1.0 for f, e in zip(frames, ends))
+            for move, u1, u2, u3 in rng.random((TRIES // 5 if idle else TRIES, 4)).tolist():
+                if move < 0.7 and stale:
+                    held, stale = chain(part, alt, int(u3 * 997) % len(cases), frames), False
+                if move < 0.7 and held:
+                    lo, hi = held[int(u1 * len(held))]
+                    turn, first = move < 0.2, move < 0.45
+                    x = part[lo if (u2 < 0.5 or len(on[part[hi]]) == 1) and len(on[part[lo]]) > 1 else hi]
+                else:
+                    lo = int(u1 * (len(part) - 1))
+                    hi = min(len(part) - 1, lo + 1 + int(u2 * REACH))
+                    turn, first, x = move < 0.78, move < 0.89, part[lo]
+                new, was = part, alt[x]
+                if turn:
+                    if len(on[x]) == 1:
+                        continue
+                    alt[x] = (was + 1 + int(u2 * 991) % (len(on[x]) - 1)) % len(on[x])
+                elif first:
+                    mine, others = tied(part[lo:hi + 1], after)
+                    new = part[:lo] + mine + others + part[hi + 1:]
+                else:
+                    mine, others = tied(part[lo:hi + 1][::-1], before)
+                    new = part[:lo] + others[::-1] + mine[::-1] + part[hi + 1:]
+                if new == part and not turn:
+                    continue
+                v, t = value(new, alt, frames)
+                if v <= cur - warm * math.log(1.0 - u3):
+                    cur, part, ends, stale = v, new, t, True
+                else:
+                    alt[x] = was
+            seq[a:b] = part
+            v = sum(math.log(x) for x in ends)
+            if best is None or v < best[0]:
+                best = (v, [(j, alt[j]) for j in seq], ends)
+    SPAN[:] = best[2]
+    return best
 
 
 def build(g, core, T, topo, m):
@@ -508,6 +809,19 @@ def build(g, core, T, topo, m):
             tt(via, a, b, A.add)
             gather(o, via)
 
+    def zone(p):
+        return 256 * (p if p < 4 or LIFTED else p + 1)
+
+    def only(q):
+        ops[-1]["alts"] = [a for a in ops[-1]["alts"] if q in ("*", a[0])]
+
+    def low(o, via, i, bits):
+        if ANDU:
+            ts(o, i, bits, A.bitwise_and)
+        else:
+            ts(via, i, bits, A.bitwise_and)
+            gather(o, via)
+
     def join(n):
         part = ops[-n:]
         del ops[-n:]
@@ -538,7 +852,9 @@ def build(g, core, T, topo, m):
     def wrap(o, name, lo, hi, start=True, stop=True, base="WB"):
         for r in range(16):
             mm(o, R(base, 15 - r, 143 - r), R(name, lo, hi, 16, lo + r), start and r == 0, stop and r == 15)
-        join(16)
+            if r == 7 and name in CUT:
+                join(8)
+        join(8 if name in CUT else 16)
 
     def col(j):
         return R("col", j, j + 1)
@@ -554,7 +870,7 @@ def build(g, core, T, topo, m):
     def ext(t, name="hbm"):
         return (t, [] if name == "hbm" else [(name, 0, S)], [], 0, name, False)
 
-    PG, PI, PW15, M0, MH, M15, AB, ZI, ZJ, ZK, DW, AS, AO, M2, CB, ODD, AC, C2K, CRAW = range(19)
+    PG, PI, PW15, M0, MH, M15, AB, ZI, ZJ, ZK, DW, AS, AO, M2, CB, ODD, AC, C2K, CRAW, ZC = range(20)
     U_C1, U_C, U_A, U_A9, U_S, U_AT, U_W, U_P, U_FB, U_E, U_H = [16 * i for i in range(11)]
     W_S, W_AT, W_D, W_Y, W_FB, W_K, W_NZ, W_D1, W_D2, W_E, W_A, W_N, W_AD = [16 * i for i in range(13)]
 
@@ -620,7 +936,9 @@ def build(g, core, T, topo, m):
     ts(R("WB"), R("XP"), col(PW15), A.is_equal)
     ts(R("MK"), R("j16"), col(PI), A.is_equal, 0.5, A.subtract)
     lin(R("SEL"), R("MK"), 33.0 * BIG, 15.5 * BIG)
-    for c, add in ((CB, 0.0), (C2K, 2048.0), (CRAW, -RAW)):
+    ts(R("SE2"), R("MK"), -2.0 ** 21, A.mult, float(S), A.min)
+    lin(col(C2K), col(PW15), -float(S), 0.0)
+    for c, add in ((CB, 0.0), (CRAW, -RAW)):
         lin(col(c), col(PW15), BIG, add)
     lin(R("M1"), R("M1b"), 1.0, 0.0)
     put([("S", lambda: g.scalar.activation(T.L2[:, 16:24], T.rc[:, 0:8], F.Silu), 1400.0)], [R("L2", 16, 24)], [R("rc", 0, 8)])
@@ -632,9 +950,9 @@ def build(g, core, T, topo, m):
     cp(col(ODD), R("pci", 6, 7))
     lin(col(M2), col(ODD), -1.0, 1.0)
     for name, src, scale in (("I16", "ID", 16.0), ("NI", "ID", -1.0), ("ID32", "ID", 1.0),
-                             ("NI32", "ID", -1.0), ("B16", "BLK", 16.0), ("B256", "BLK", 256.0), ("B2K", "BLK", 2048.0),
+                             ("B16", "BLK", 16.0), ("B256", "BLK", 256.0), ("B2K", "BLK", 2048.0),
                              ("N4K", "BLK", -4096.0), ("NB", "BLK", -1.0), ("DW", "BLK", col(PI)), ("N15", "BLK", col(M15)),
-                             ("WBI", "WB", col(PI)), ("WB0", "WB", col(M0)), ("B0", "BLK", col(M0)),
+                             ("B15", "BLK", -15.0 / 16), ("WB2", "WB", 2.0), ("WBI", "WB", col(PI)), ("WB0", "WB", col(M0)),
                              ("IE", "ID", col(M2)), ("IO", "ID", col(ODD))):
         lin(R(name), R(src), scale, 0.0)
     if "h" in SCAN[0]:
@@ -651,11 +969,25 @@ def build(g, core, T, topo, m):
         o, i, c = R("LL", 128 * r, 128 * r + 128), R("NB"), R("clt", r, r + 1)
         put([a_sel(o, i, [[16, 8], [0, 16]], A.is_gt, 0.0, r, -1), a_act(o, i, F.Identity, 0.0, c), a_ts(o, i, c, A.mult)],
             [o], [i, c])
-    ts(col(ZI), col(PI), 3.5, A.is_gt, 256.0, A.mult)
-    lin(col(ZJ), col(PI), 256.0, -1024.0)
-    tt(col(ZI), col(ZI), col(ZJ), A.add)
+    if LEAST:
+        lin(R("BRAW"), R("BLK"), -RAW / 16, 0.0)
+    if LIFTED:
+        lin(col(ZI), col(PI), 256.0, -896.0)
+        lin(R("N4I"), R("ID"), -4096.0, 0.0)
+    else:
+        ts(col(ZI), col(PI), 3.5, A.is_gt, 256.0, A.mult)
+        lin(col(ZJ), col(PI), 256.0, -1024.0)
+        tt(col(ZI), col(ZI), col(ZJ), A.add)
+    if PLAIN:
+        ts(R("TI32"), R("UP"), 0.5, A.min)
+        lin(col(ZJ), col(PI), 128.0, 128.0)
     lin(col(DW), col(PI), 1.0, 1024.0)
-    ts(R("dwr", 0, 16), R("i16"), 16.0, A.mult, col(DW), A.add)
+    for split in set(SPLIT):
+        for lo, hi in HALVES if split else [(0, 256)]:
+            z = 32 * split
+            ts(R("dwr", z + lo // 8, z + (lo + hi) // 16), R("i16", lo // 16, hi // 16), 16.0, A.mult, col(DW), A.add)
+    if "p" in SCAN[0]:
+        lin(w(W_E, 0, 128), R("dwr", 48, 56), 1.0, col(CB))
     ts(col(AS), col(PI), 2.0, A.not_equal)
     lin(col(AO), col(AS), 2048.0 - 2 * S, 2.0 * S)
     step[0] = "fold"
@@ -672,8 +1004,7 @@ def build(g, core, T, topo, m):
 
     def targets(lst, base, lo, hi, o):
         tt(R("t", o + lo, o + hi), IND(R("dsb"), u(lst, lo, hi)), R(base, lo, hi), A.add)
-        ts(R("q", o + lo, o + hi), R("t", o + lo, o + hi), S - 1, A.bitwise_and)
-        gather(R("q16", o + lo, o + hi), R("q", o + lo, o + hi))
+        low(R("q16", o + lo, o + hi), R("q", o + lo, o + hi), R("t", o + lo, o + hi), S - 1)
         lin(R("qo", o + lo, o + hi), R("q16", o + lo, o + hi), 1.0, -2048.0)
 
     def square(o, lo, hi, stop):
@@ -682,38 +1013,56 @@ def build(g, core, T, topo, m):
         join(3)
 
     def dedupe(pb, kw, o, after):
-        def equal(b, c, a, hi, stop=False):
-            step[0] = "equal %d %d %d" % (o, c // 8, hi)
-            ts(R("E", 256 * c + a, 256 * c + hi), R("key", o + a, o + hi), R("w32", kw + c, kw + c + 1), A.is_equal)
-            row("equal")
-            a = max(a, 16 * c + 16)
-            if a < hi:
-                mm(R(b, a, hi), R("NB"), R("E", 256 * c + a, 256 * c + hi), False, stop)
+        def equal(b, first, last, cross, hi, stop=False):
+            for z in range(first, last, PAIR):
+                step[0] = "equal %d %d %d" % (o, z // 8, hi)
+                cs = range(z, min(z + PAIR, last))
+                for c in cs:
+                    a = 128 if cross else 16 * c
+                    ts(R("E", 256 * c + a, 256 * c + hi), R("key", o + a, o + hi), R("w32", kw + c, kw + c + 1), A.is_equal)
+                join(len(cs))
+                row("equal")
+                cs = [(c, 128 if cross else 16 * c + 16) for c in cs if cross or 16 * c + 16 < hi]
+                for c, a in cs:
+                    mm(R(b, a, hi), R("NB"), R("E", 256 * c + a, 256 * c + hi), False, stop and c == last - 1)
+                if cs:
+                    join(len(cs))
 
         for b, (lo, hi) in zip(pb, HALVES if len(pb) > 1 else [(0, 256)]):
             mm(R(b, lo, hi), R("N15"), R("T1", lo, hi), True, False)
             if o == 0:
-                mm(R(b, 0, 128), R("ID"), R("A1", 0, 128), False, False)
-            elif lo:
-                mm(R(b, lo, hi), R("ID"), R("MK"), False, False)
+                mm(R(b, lo, lo + 128), R("ID"), R("A1", lo, lo + 128), False, False)
+            else:
+                for i in range(2 if lo else 0):
+                    mm(R(b, lo, hi), R("ID"), R("MK"), False, False)
+                both(R("E", S + lo, S + hi), R("key", o + lo, o + hi), (F.Relu, 1.0 - S, 1.0), (float(S), A.is_equal))
+                mm(R(b, lo, hi), R("NB"), R("E", S + lo, S + hi), False, False)
             early = LEAD if hi == 256 else 0
-            for c in range(lo // 16, 8):
-                equal(b, c, 16 * c, 128)
-            if o == 0:
+            if WIDE and hi - lo == 256:
                 mm(R(b, 128, 256), R("ID"), R("A1", 128, 256), False, False)
-            for c in range(early):
-                equal(b, c, 128, 256)
-            for c in range(8, hi // 16):
-                equal(b, c, 16 * c, 256)
+                equal(b, 8, 16, False, 256)
+                equal(b, 0, 8, False, 256)
+                for r in range(1, 16):
+                    diag = (T.E[:, r:17 * 256:272], [("E", 272 * i, 272 * i + 16) for i in range(16)], [], 16, "E", False)
+                    mm(R(b, 0, 256, 16, r), R("LL", 128 * r, 128 * r + 128), diag, False, r == 15)
+                join(15)
+                after(lo, hi)
+                continue
+            equal(b, lo // 16, 8, False, 128)
+            if o == 0 and hi - lo == 256:
+                mm(R(b, 128, 256), R("ID"), R("A1", 128, 256), False, False)
+            equal(b, 0, early, True, 256)
+            equal(b, 8, hi // 16, False, 256)
             for r in range(1, 16):
                 diag = (T.E[:, 17 * lo + r:17 * hi:272], [("E", 272 * i, 272 * i + 16) for i in range(lo // 16, hi // 16)],
                         [], 16, "E", False)
                 mm(R(b, lo, hi, 16, lo + r), R("LL", 128 * r, 128 * r + 128), diag, False, r == 15 and hi < 256)
             join(15)
-            for c in range(early, 8) if hi == 256 else []:
-                equal(b, c, 128, 256, c == 7)
+            if hi == 256:
+                equal(b, early, 8, True, 256, True)
             after(lo, hi)
 
+    table = []
     for t in range(RO):
         PW = "PW%d" % t
         land = "land%d" % t
@@ -722,19 +1071,30 @@ def build(g, core, T, topo, m):
             put([("V", (lambda b: lambda: g.vector.transpose(T.Bw[:, b:256:8], T.buff[:, :, 16 * b:16 * b + 16]))(b), 64 * CY)],
                 [R("Bw", 32 * b, 32 * b + 32)], [W("buff", None)])
         join(8)
+        ops[-1]["behind"] = table
         ts(R("f", 0, 256), R("Bw"), float(S), A.is_lt if t else A.is_gt)
         scan(R("rc", 16, 288), R("f"), R("ones"), 0.0, A.add, A.mult)
         lin(R("Bo", 0, 256), R("Bw"), 1.0, -2048.0 if t else -2048.0 - 2 * S)
-        mm(R("p0", 0, 16), R("BLK"), R("rc", 16, 272, 16, 31), True, True)
-        ts(R("T1"), R("M1b"), own(R("p0", 0, 16)), A.subtract, col(CB), A.is_ge)
+        if t and PLAIN:
+            put([("S", lambda: g.scalar.activation(T.fx[:, :], T.nat[:, :], F.Sign, bias=S - 0.5, scale=-1.0,
+                                                   accum_out=T.col[:, ZC:ZC + 1]), 256 * CY + 25.0)],
+                [R("fx"), col(ZC)], [R("nat")])
+            mm(R("p0", 0, 1), R("TI32"), col(ZC), True, True)
+            ts(R("T1"), R("M1b"), R("p0", 0, 1), A.subtract, col(ZJ), A.is_ge)
+        else:
+            mm(R("p0", 0, 16), R("BLK"), R("rc", 16, 272, 16, 31), True, True)
+            ts(R("T1"), R("M1b"), own(R("p0", 0, 16)), A.subtract, col(CB), A.is_ge)
         wrap(R("p4", 0, 17), "rc", 16, 288)
         mm(R("p1", 0, 272), R("UP"), R("f"), True, False)
         mm(R("p1", 0, 272), R("BLK"), R("rc", 15, 287), False, True)
-        wrap(R("p3", 0, 16), "T1", 0, 256)
+        first = 128 if "a" in SCAN[t] else 0
+        if first:
+            mm(R("p5", 0, 128), R("BLK"), R("T1", 0, 128), True, True)
+            lin(u(U_C1, 0, 128), own(R("p5", 0, 128)), 1.0, col(CB))
+        wrap(pl("p3", 0, first, 256), "T1", first, 256)
         lin(R("L2", 0, 17), R("p4", 0, 17), 1.0, 0.0)
         lin(R("G"), R("p1", 0, 272), 1.0, -float(S))
-        gather(u(U_C1), R("p3", 0, 16))
-        gather(R("C1"), R("p3", 0, 16))
+        gather(u(U_C1, first, 256), pl("p3", 0, first, 256))
         if t == 0:
             step[0] = "table 0"
             ts(R("xo", 0, 256), R("Bw"), float(S), A.min)
@@ -751,32 +1111,40 @@ def build(g, core, T, topo, m):
             step[0] = "level %d" % lo
             tt(R("T2", lo, hi), IND(R("L2"), u(U_C1, lo, hi)), R("M1", lo, hi), A.is_le)
             pb = "p4" if lo == 0 else "p0"
-            mm(pl(pb, 32, lo, hi), R("I16"), R("C1", lo // 16, hi // 16), True, False)
-            wrap(pl(pb, 32, lo, hi), "T2", lo, hi, False)
-            gather(u(U_C, lo, hi), pl(pb, 32, lo, hi))
+            if "bB"[lo > 0] in SCAN[t]:
+                mm(R(pb, 256 + lo, 256 + hi), R("B16"), R("T1", lo, hi), True, False)
+                mm(R(pb, 256 + lo, 256 + hi), R("BLK"), R("T2", lo, hi), False, True)
+                lin(u(U_C, lo, hi), own(R(pb, 256 + lo, 256 + hi)), 1.0, col(CB))
+            else:
+                gather(R("C1", lo // 16, hi // 16), u(U_C1, lo, hi))
+                mm(pl(pb, 32, lo, hi), R("I16"), R("C1", lo // 16, hi // 16), True, False)
+                wrap(pl(pb, 32, lo, hi), "T2", lo, hi, False)
+                gather(u(U_C, lo, hi), pl(pb, 32, lo, hi))
             gather(R("C2", lo // 16, hi // 16), u(U_C, lo, hi))
         for lo, hi in SEARCH[t]:
             step[0] = "row %d" % lo
-            pa, pb = ("p3", "p4") if lo == 0 else ("p2", "p0")
+            pa = "p3" if lo == 0 else "p2"
             tt(R("OH", lo, hi), IND(R("G"), u(U_C, lo, hi)), R("M1", lo, hi), A.is_equal)
             tt(R("Zu", lo, hi), IND(R("Bo"), u(U_C, lo, hi)), R("OH", lo, hi), A.mult)
             square(R("p5", lo, hi), lo, hi, True)
-            aw = pl(pa, 32, lo, hi)
-            wrap(aw, "Zu", lo, hi)
             lin(R("srep", lo, hi), R("p5", lo, hi), 1.0, 0.0)
-            lin(u(U_A, lo, hi), aw, 1.0, 2048.0)
-            step[0] = "aside"
-            mm(R("p6", lo, hi), R("BLK"), R("Zu", lo, hi), True, True)
-            lin(w(W_A, lo, hi), aw, 1.0, -2048.0)
+            if "cC"[lo > 0] in SCAN[t]:
+                mm(R("p6", lo, hi), R("BLK"), R("Zu", lo, hi), True, True)
+                lin(u(U_A, lo, hi), own(R("p6", lo, hi)), 1.0, col(C2K))
+            else:
+                wrap(pl(pa, 32, lo, hi), "Zu", lo, hi)
+                lin(u(U_A, lo, hi), pl(pa, 32, lo, hi), 1.0, 2048.0)
+                step[0] = "aside"
+                mm(R("p6", lo, hi), R("BLK"), R("Zu", lo, hi), True, True)
+        step[0] = "aside"
         mm(R("p0", 64, 80), R("I16"), R("C2"), True, False)
         wrap(R("p0", 64, 80), "OH", 0, 256, False, True, "WBI")
         gather(w(W_S), R("p0", 64, 80))
         gather(u(U_S), w(W_S))
         lin(R("arep"), R("p6", 0, 256), col(AS), col(AO))
         both(R("ge"), R("p6", 0, 256), (F.Sign, col(AB), 1.0), (col(AC), A.is_gt, 2.0, A.mult))
-        ts(R("wi", 0, 16), w(W_A), float(S), A.add)
-        ts(R("wi", 16, 32), R("wi", 0, 16), 511, A.bitwise_and)
-        gather(u(U_A9), R("wi", 16, 32))
+        cp(R("wi", 0, 16), u(U_A))
+        low(u(U_A9), R("wi", 16, 32), R("wi", 0, 16), 511)
         lin(R("hg"), IND(R("hmb"), u(U_A9)), 1.0, -2048.0)
         act(IND(bdw, u(U_S)), R("neg"), F.Silu)
         for lo, hi in FIRST[t]:
@@ -785,23 +1153,30 @@ def build(g, core, T, topo, m):
         for lo, hi in HALVES:
             gather(R("xa", lo, hi), IND(XS, u(U_A, lo, hi)))
             mm(R("p2", lo, hi), R("ID"), R("xa", lo, hi), True, True)
-        for b in range(4):
+        def compare(b):
             step[0] = "compare %d" % b
             lo, hi = 64 * b, 64 * b + 64
             pc = R(PC[b], 128 + lo, 128 + hi)
-            for c in range(lo, hi, CV):
-                gather(R("xv", 16 * c, 16 * (c + CV)), IND(R("XB%d" % t, 0, S), R("q16", c, c + CV)))
+            for c in range(lo, hi, CV[b]):
+                gather(R("xv", 16 * c, 16 * (c + CV[b])), IND(R("XB%d" % t, 0, S), R("q16", c, c + CV[b])))
             for ks in GROUPS:
                 outs = [(k, R("cmp", 16 * lo + 64 * k, 16 * lo + 64 * k + 64)) for k in ks]
                 for k, o in outs:
                     tt(o, R("xv", 16 * lo, 16 * hi, 16, 16 * lo + k), R("p2", lo, hi), A.is_lt)
                 join(len(ks))
                 row("compare")
+                ops[-1]["behind"] = [mark[x] for x in AHEAD if AHEAD[x] == (b, ks[0])]
+                if ks[0] == 0:
+                    mm(pc, R("B15"), R("ones", 0, 64), True, False)
                 for k, o in outs:
-                    mm(pc, R("WB", 15 - k, 143 - k), o, k == 0, k == 15)
+                    mm(pc, R("WB2", 15 - k, 143 - k), o, False, k == 15)
                 join(len(ks))
-            act(R("good", lo, hi), pc, F.Sign, bias=-7.5)
+            both(R("good", lo, hi), pc, (F.Sign, 0.0, 1.0), (1.0, A.min, -1.0, A.max))
+
+        mark = {}
         for h, (lo, hi) in enumerate(HALVES):
+            compare(2 * h)
+            compare(2 * h + 1)
             pb, pw = ("p5", "p4") if h == 0 else ("p6", "p3")
             good = R("good", lo, hi)
             step[0] = "claim %d" % h
@@ -812,16 +1187,27 @@ def build(g, core, T, topo, m):
             mm(R("p7", 256 + lo, 256 + hi), R("NBM"), R("ge", lo, hi), True, False)
             mm(R("p7", 256 + lo, 256 + hi), R("BLK"), good, False, True)
             ts(R("Z", lo, hi), R(pb, 256, 384), col(ZK), A.add, 2048.0, A.min)
-            act(R("back", lo, hi), R("p7", lo, hi), F.Relu, bias=S - 32768.0, scale=-1.0)
+            mark["pick"] = len(ops) - 1
+            if LEAST:
+                lin(R("back", lo, hi), R("p7", lo, hi), 1.0, 32768.0)
+            else:
+                relu(R("back", lo, hi), R("p7", lo, hi), S - 32768.0)
             act(R("A1", lo, hi), R("p7", 256 + lo, 256 + hi), F.Sign, bias=-49.0)
             at = R(pb, lo, hi)
-            mm(at, R("NI32"), R("back", lo, hi), True, False)
-            mm(at, R("BLK"), R("Z", lo, hi), False, True)
-            aw = own(at)
-            lin(u(U_AT, lo, hi), aw, 1.0, col(CRAW))
-            lin(w(W_AT, lo, hi), aw, 1.0, col(CRAW))
-            lin(R("atrep", lo, hi), at, 1.0, -RAW)
-            lin(R("key", lo, hi), at, 1.0, -RAW)
+            if LEAST:
+                mm(at, R("BRAW"), R("ones", 0, 128), True, False)
+                mm(at, R("BLK"), R("Z", lo, hi), False, True)
+                tt(R("key", lo, hi), at, R("back", lo, hi), A.min)
+                scan(R("s2", lo, hi), R("SE2"), R("key", lo, hi), 0.0, A.add, A.max)
+                aw = R("s2", lo, hi, 16, lo + 15)
+            else:
+                mm(at, R("NI32"), R("back", lo, hi), True, False)
+                mm(at, R("BLK"), R("Z", lo, hi), False, True)
+                aw = own(at)
+                lin(R("key", lo, hi), at, 1.0, -RAW)
+            mark["own"] = len(ops) - 1
+            lin(u(U_AT, lo, hi), aw, 1.0, col(C2K))
+            lin(w(W_AT, lo, hi), aw, 1.0, col(C2K))
             step[0] = "victim %d" % h
             lin(R("whom", lo, hi), IND(baw, u(U_AT, lo, hi)), 1.0, -2048.0)
             if "vw"[h] in SCAN[t]:
@@ -830,7 +1216,8 @@ def build(g, core, T, topo, m):
             else:
                 wrap(R(pw, 0, 8), "whom", lo, hi, True, True, "WB0")
                 lin(u(U_W, lo, hi), R(pw, 0, 8), 1.0, 2048.0)
-            targets(U_W, "atrep", lo, hi, 256)
+            mark["targets"] = len(ops)
+            targets(U_W, "key", lo, hi, 256)
             step[0] = "payload"
             mm(R(pb, 384, 512), R("IO"), R("hg", lo, hi), True, False)
             mm(R(pb, 384, 512), R("IE"), R("whom", lo, hi), False, True)
@@ -839,11 +1226,13 @@ def build(g, core, T, topo, m):
             for c in range(lo, hi, CF):
                 both(R("fr", 16 * c, 16 * (c + CF)), IND(baw, R("q16", 256 + c, 256 + c + CF)),
                      (F.Relu, 1.0 - S, 1.0), (float(S), A.is_equal))
+                only(FR[c // CF])
         step[0] = "payload"
         for p in range(N):
-            z = 256 * (p if p < 4 else p + 1)
+            z = zone(p)
             iota(R(PW, z, z + 16), [[2, 16]], REB0 + int(LIFT) + 32 * rank, 0)
-        tt(w(W_D), w(W_AT), w(W_S), A.subtract)
+        for lo, hi in HALVES if SPLIT[t] else [(0, 256)]:
+            tt(w(W_D, lo, hi), w(W_AT, lo, hi), w(W_S, lo, hi), A.subtract)
         for h, (lo, hi) in enumerate(HALVES):
             pb = "p1" if h == 0 else "p2"
             step[0] = "weigh %d" % h
@@ -854,53 +1243,73 @@ def build(g, core, T, topo, m):
                     z = 16 * (lo + c)
                     mm(R(pb, c, c + 64), R("TR", 128 * k, 128 * k + 128), R("fr", z, z + 1024, 16, z + k), False, False)
                 join(16)
-        dedupe(["p0"], W_AT, 0, lambda lo, hi: None)
-        step[0] = "send"
-        fl = R("Zp", 256, 512)
-        relu(fl, R("p0", 0, 256), 0.0)
-        relu(R("p7", 0, 256), R("p0", 0, 256), 0.0)
-        scan(R("sc"), fl, R("ones", 0, 256), col(ZI), A.add, A.subtract)
-        tt(R("Zp", 0, 256), R("sc"), R("p7", 0, 256), A.mult)
-        mm(R("p4", 32, 64), R("ID"), R("dwr"), True, False)
-        wrap(R("p4", 32, 64), "Zp", 0, 512, False)
-        gather(u(U_P), R("p4", 32, 48))
-        act(IND(R(PW), u(U_P)), R("pay"), F.Silu)
-        tt(w(W_Y), R("p4", 48, 64), w(W_D), A.mult)
-        tt(w(W_FB), w(W_Y), w(W_S), A.add)
+        def send(lo, hi):
+            step[0] = "send %d" % lo
+            n, pp = hi - lo, 32 + lo // 8
+            fl = R("Zp", 2 * lo + n, 2 * hi)
+            won = R("p5" if lo else "p0", lo, hi)
+            relu(fl, won, 0.0)
+            if LIFTED:
+                mm(R("p7", lo, hi), R("N4I"), fl, True, False)
+            else:
+                relu(R("p7", lo, hi), won, 0.0)
+            if lo:
+                gather(col(ZC), R("sc", lo - 1, lo))
+            scan(R("sc", lo, hi), fl, R("ones", lo, hi), col(ZC if lo else ZI), A.add, A.subtract)
+            if LIFTED:
+                mm(R("p7", lo, hi), R("ID"), R("sc", lo, hi), False, True)
+                ts(R("Zp", 2 * lo, 2 * lo + n), R("p7", lo, hi), float(S), A.add, 1152.0, A.min)
+            else:
+                tt(R("Zp", 2 * lo, 2 * lo + n), R("sc", lo, hi), R("p7", lo, hi), A.mult)
+            if lo and "p" in SCAN[0]:
+                mm(R("p3", 256, 384), R("BLK"), R("Zp", 2 * lo, 2 * lo + n), True, True)
+                tt(u(U_P, lo, hi), own(R("p3", 256, 384)), w(W_E, 0, n), A.add)
+                wrap(R("p4", pp + n // 16, pp + n // 8), "Zp", 2 * lo + n, 2 * hi)
+            else:
+                mm(R("p4", pp, pp + n // 8), R("ID"), R("dwr", 32 * SPLIT[t] + lo // 8, 32 * SPLIT[t] + hi // 8), True, False)
+                wrap(R("p4", pp, pp + n // 8), "Zp", 2 * lo, 2 * hi, False)
+                lin(u(U_P, lo, hi), R("p4", pp, pp + n // 16), 1.0, 1024.0 - 16 * 1152 if LIFTED else 0.0)
+            act(IND(R(PW), u(U_P, lo, hi)), R("pay", lo, hi), F.Silu)
+            tt(w(W_Y, lo, hi), R("p4", pp + n // 16, pp + n // 8), w(W_D, lo, hi), A.mult)
+            tt(w(W_FB, lo, hi), w(W_Y, lo, hi), w(W_S, lo, hi), A.add)
+
+        dedupe(["p0", "p5"] if SPLIT[t] else ["p0"], W_AT, 0, send)
         gather(u(U_FB), w(W_FB))
         act(IND(bdw, u(U_FB)), R("neg"), F.Silu)
-        z = 256 * (rank if rank < 4 else rank + 1)
-        gather(R(land, 16 * rank, 16 * rank + 16), R(PW, z, z + 16))
+        z = zone(rank)
+        o, i = R(land, 16 * rank, 16 * rank + 16), R(PW, z, z + 16)
+        put([a_sel(o, i, [[0, 16]], A.is_ge, 0.0, 0, 0), a_act(o, i, F.Copy), a_cp(o, i)], [o], [i])
         sent = ext(None, "sent%d" % t)
-        mine = masks_from(core, cores, topo)
-        trs = []
-        for c in mine:
-            p = cores.index(c)
-            z = 256 * (p if p < 4 else p + 1)
-            rid, pid, _e = topo.addr(c)
-            trs.append(RemoteDMATransfer(dst_ids=[DstId(rid=rid, pnc=pid)], dma_engine_mask=sum(1 << e for e in mine[c]),
-                                         remote_sem=T.sem["arr%d" % t], src=T[PW][:, z:z + 16],
-                                         dst=T[land][:, 16 * rank:16 * rank + 16]))
-        put([("G", (lambda trs, t: lambda: g.remote_dma_fused(trs, local_sem=T.sem["snt%d" % t]))(trs, t), 300.0)],
-            [sent], [R(PW)], "snt%d" % t, -sum(len(v) for v in mine.values()), FAR)
-        arrivals = sum(len(masks_from(c, cores, topo)[core]) for c in cores if c != core)
+        calls, used = [], 0
+        for mine in masks_from(core, cores, topo):
+            trs = []
+            for c in mine:
+                z = zone(cores.index(c))
+                rid, pid, _e = topo.addr(c)
+                trs.append(RemoteDMATransfer(dst_ids=[DstId(rid=rid, pnc=pid)], dma_engine_mask=sum(1 << e for e in mine[c]),
+                                             remote_sem=T.sem["arr%d" % t], src=T[PW][:, z:z + 16],
+                                             dst=T[land][:, 16 * rank:16 * rank + 16]))
+                used += len(mine[c])
+            calls.append(trs)
+        put([("G", (lambda calls, t: lambda: [g.remote_dma_fused(x, local_sem=T.sem["snt%d" % t]) for x in calls])(calls, t),
+              300.0)], [sent], [R(PW)], "snt%d" % t, -used, FAR - 300.0)
+        arrivals = sum(len(call[core]) for c in cores if c != core for call in masks_from(c, cores, topo) if core in call)
         put([("X", None, 0.0)], [(None, [(land, 16 * p, 16 * p + 16) for p in range(N) if p != rank], [])], [sent],
             "arr%d" % t, -arrivals)
         for h, (lo, hi) in enumerate(HALVES):
             step[0] = "name %d" % h
             pb = R("p1" if h == 0 else "p2", 0, 128)
-            mm(pb, R("N4K"), R("Zp", 256 + lo, 256 + hi), False, True)
+            z = 2 * lo + 128 if SPLIT[t] else 256 + lo
+            mm(pb, R("N4K"), R("Zp", z, z + 128), False, True)
             ts(R("Z", 256 + lo, 256 + hi), pb, 9.0 * S, A.add, 2048.0, A.min)
             mm(R("p6", lo, hi), R("BLK"), R("Z", 256 + lo, 256 + hi), True, True)
             lin(R("key", 256 + lo, 256 + hi), R("p6", lo, hi), 1.0, -RAW)
             if "nm"[h] in SCAN[t]:
-                ts(w(W_K, lo, hi), own(R("p6", lo, hi)), col(CRAW), A.add, S - 0.5, A.min)
+                lin(w(W_K, lo, hi), own(R("p6", lo, hi)), 1.0, col(CRAW))
             else:
                 wrap(pl("p5", 384, lo, hi), "Z", 256 + lo, 256 + hi)
-                ts(w(W_K, lo, hi), pl("p5", 384, lo, hi), RAW, A.subtract, S - 0.5, A.min)
-            ts(w(W_NZ, lo, hi), w(W_K, lo, hi), S - 0.75, A.is_lt, 2.0, A.mult)
-            tt(w(W_D1, lo, hi), w(W_K, lo, hi), w(W_FB, lo, hi), A.subtract)
-            tt(w(W_D2, lo, hi), w(W_D1, lo, hi), w(W_NZ, lo, hi), A.mult)
+                lin(w(W_K, lo, hi), pl("p5", 384, lo, hi), 1.0, -RAW)
+            tt(w(W_D2, lo, hi), w(W_K, lo, hi), w(W_FB, lo, hi), A.subtract)
 
         def reborn():
             step[0] = "reborn"
@@ -924,10 +1333,11 @@ def build(g, core, T, topo, m):
                 reborn()
             step[0] = "ends %d" % lo
             if lo:
-                scan(R("sg"), R("keep"), R("p7", lo, hi), 0.0, A.mult, A.max)
+                relu(R("ge", 0, 128), R("p7", lo, hi), 0.0)
+                scan(R("sg"), R("keep"), R("ge", 0, 128), 0.0, A.mult, A.max)
                 go = R("sg", 0, 128, 16, 15)
             else:
-                both(R("gl"), R("p0", 0, 128), (F.Relu, 0.5, 0.5), (-0.5, A.is_gt, 0.5, A.mult))
+                relu(R("gl"), R("p0", 0, 128), 1.0)
                 go = R("p1", 128, 136)
                 wrap(go, "gl", 0, 128, True, True, "WB0")
             tt(w(W_Y, lo, hi), go, w(W_D2, lo, hi), A.mult)
@@ -940,9 +1350,13 @@ def build(g, core, T, topo, m):
         step[0] = "next"
         if t + 1 < RO:
             dma(W("buff", T.buff[:, 0, :]), ext(T.bd[2:128:32, 0:S], "bd"), "Y", "dF", 65536)
-            dma(W("buff", T.buff[:, 1, :]), ext(T.bd[18:128:32, 0:S], "bd"), "S", "dF", 65536)
+            dma(W("buff", T.buff[:, 1, :]), ext(T.bd[18:128:32, 0:S], "bd"), "Y", "dF", 65536)
+            if PLAIN:
+                dma(R("nat"), ext(T.bd[2:128:16, 0:S], "bd"), "Y", "dN", 131072)
             dma(ext(T.ba[0:128:16, 0:S], "ba"), ext(T.bd[0:128:16, 0:S], "bd"), "Y", "dA", 131072)
-            cp(IND(R("XB1"), u(U_E)), R("xa"))
+            for lo in range(0, 256, CE):
+                cp(IND(R("XB1"), u(U_E, lo, lo + CE)), R("xa", lo, lo + CE))
+            table = [len(ops) - 1] * TABLE
         else:
             dma(ext(T.y[:, :], "y"), ext(T.bd[0:128:16, 0:S], "bd"), "Y", "dY", 131072)
 
@@ -953,7 +1367,7 @@ def rank_program(g, core, T, topo):
     if T.rank_of(core) is None:
         return
     if not ORDER:
-        ORDER.extend(plan([build(g, core, T, topo, m) for m in MODELS]))
+        ORDER.extend(best_plan([build(g, core, T, topo, m) for m in MODELS]))
     calls = build(g, core, T, topo, MODELS[0])
     ops = [calls[j]["alts"][a][:2] + (calls[j]["rd"], calls[j]["wr"], calls[j]["sem"], calls[j]["cnt"]) for j, a in ORDER]
     queue = {"V": g.vector, "S": g.scalar, "P": g.tensor, "G": g, "Y": g.sync}

import math
import numpy as np
from concourse.bass import DstId, RemoteDMATransfer
from concourse.mybir import AluOpType as A
from concourse.mybir import ActivationFunctionType as F

N = 8
S = 4096
RO = 2
REB0 = 4352
BW = 4608
AW = 4104
PWW = 2304
LIFT = 8192.0
ROUND = 1.5 * 2 ** 23
HALVES = [(0, 128), (128, 256)]
BIG = 65536.0
DLAT = 2000.0
MODELS = [dict(far=4500.0, pe=0.54, cy=1.04, ga=1.56, sc=3.8, wake=60.0, bpn=310.0),
          dict(far=5200.0, pe=0.6, cy=1.14, ga=1.8, sc=4.6, wake=90.0, bpn=290.0),
          dict(far=6000.0, pe=0.65, cy=1.24, ga=2.05, sc=5.8, wake=80.0, bpn=340.0)]
SEED = 1
HEAT = 0.002
MIX = 3
PAIR = 2
LEAD = 4
CX = [64, 32]
CV = [32, 32, 32, 32]
CF = 32
SEARCH = [HALVES, HALVES]
FIRST = [[(0, 64), (64, 128), (128, 256)]] * 2
PC = ["p4", "p1", "p3", "p1"]
GROUPS = [range(0, 4), range(4, 8), range(8, 12), range(12, 14), range(14, 15), range(15, 16)]
SCAN = ["m", "m"]
ANDU = False
ONCE = 0.0
PLAIN = True
SPLIT = [False, False]
XV = "********"
FR = "********"
REB = [1, 1]
DIRECT = True
ROUNDS = 40
STEPS = 3000
MEAN = 0.05
WARM = 0.001
REACH = 40
SLACK = 1000.0
TIDY = 100
SORT = 100
SWEEPS = 88
WINDOW = 80
TRIES = 200
GLOW = 0.0007
GLOW2 = 0.001
FIRSTS = 3
STARTS = 6
NEAR = 0.02
TABLE = 0
CE = 64
LIFTED = False
WIDE = False
LEAST = True
CUT = ["rc"]
BIAS = {}
AHEAD = {}
SHARE = dict(xv=0.9, fr=0.9)
SPAN = []
ORDER = []

SCRATCH = {
    "bufi": ("sbuf", [128, 2, 128], "int32"), "buff": ("sbuf", [128, 2, 128], "float32"),
    "bufy": ("sbuf", [128, 2, 128], "float32"), "TB": ("sbuf", [128, 8, 32], "bfloat16"),
}
for _d, _names in (
        ("int32", dict(dsb=4104, hmb=512, pci=8, X=256, t=512, q=512, wi=32)),
        ("uint16", dict(xo=512, u16=256, q16=512, key=512, s2=256)),
        ("float16", dict(Zu=256, Z=512, Zp=512, qo=512, dwr=64, f=272, rc=288, sc=256, whom=256, hg=256, l16=128, C2=16)),
        ("bfloat16", dict(xsb=4128, XB0=S, XB1=REB0, xv=S, cmp=S, fr=S, E=4352, LL=2048, TR=2048, WB=144, WB2=144, WBI=144,
                          WB0=144, WBH=144, XP=144, grp=128, BLK=128, TRI=128, UP=128, B2K=128, B256=128, B16=128, DW=128,
                          NI=128, tm=128, NB=128, ID=128, I16=128, N2K=128, B15=128, N4I=128, BRAW=128, N4K=128, N15=128, IE=128, IO=128, NBM=128,
                          j16=128, keep=128, MK=128, SEL=128, SE2=128, B0=128, M1b=256, ones=272, T1=256, T2=256, OH=256, C1=16, sg=128,
                          ge=256, A1=256, xa=256, good=256, fx=256, gl=128, zz=128)),
        ("float32", dict(bd=BW, ba=AW, PW0=PWW, PW1=PWW, land0=128, land1=128, ID32=128, TI32=128, nat=256, neg=256,
                         col=24, clt=16, i16=16, M1=256, Bw=256, Bo=272, G=272, L2=24, w32=208, s1=512,
                         srep=256, arep=256, atrep=256, back=256, pay=256, old=128, dd=128))):
    for _n in _names:
        SCRATCH[_n] = ("sbuf", [128, _names[_n]], _d)
for _b in range(8):
    SCRATCH["p%d" % _b] = ("psum", [128, 512], "float32")
SEMAPHORES = ["V", "S", "P", "G", "arr0", "arr1", "snt0", "snt1", "dB", "dX", "dD", "dR", "dH", "dC", "dF", "dA", "dN", "dY"]


def masks_from(src, cores, topo):
    peers = [c for c in cores if c != src]
    off = [c for c in peers if topo.chip(c) != topo.chip(src)]
    on = [c for c in peers if topo.chip(c) == topo.chip(src)]
    near = lambda c: topo.mates(topo.chip(c), topo.chip(src)) or topo.same_plane(topo.chip(c), topo.chip(src))
    off = sorted(off, key=near)
    eng = list(topo.engines(src, off[0]))
    rest = [e for e in topo.engines(src, on[0]) if e not in eng]
    first = len(eng) // 2
    out = [{c: eng[i::len(part)] for i, c in enumerate(part)} for part in (off[:first], off[first:])]
    out[0][on[0]] = rest[0:4:2]
    return out


def psum(name):
    return name in SCRATCH and SCRATCH[name][0] == "psum"


def schedule(ops):
    n = len(ops)
    pred = [dict() for _ in range(n)]
    hist, lastq = {}, {}
    for j, o in enumerate(ops):
        q = o["alts"][0][0]
        for regs, writes in ((o["rd"], False), (o["wr"], True)):
            for (name, lo, hi) in regs:
                for (i, l2, h2, w2) in hist.get(name, []):
                    if l2 < hi and lo < h2 and (w2 or writes) and not (o["sem"] and ops[i]["sem"] == o["sem"]):
                        pred[j][i] = 0
                if q == "P" and psum(name) and writes:
                    if lastq.get(name, j) != j:
                        pred[j].setdefault(lastq[name], 2)
                    lastq[name] = j
        for i in o.get("behind", []):
            pred[j].setdefault(i, 2)
        if o["keep"]:
            row = (q, o["keep"])
            if row in lastq:
                pred[j].setdefault(lastq[row], 1 if ops[lastq[row]]["sem"] else 2)
            lastq[row] = j
        for regs, writes in ((o["rd"], False), (o["wr"], True)):
            for (name, lo, hi) in regs:
                h = hist.setdefault(name, [])
                if writes:
                    h[:] = [e for e in h if not (lo <= e[1] and e[2] <= hi and (not o["sem"] or ops[e[0]]["sem"] != o["sem"]))]
                h.append((j, lo, hi, writes))
    kinds, kind = {}, []
    for o in ops:
        name, lo = o["wr"][0][:2]
        lo = lo // 1024 if name == "cmp" else 0 if name in ("E", "LL", "TR", "Bw") else lo
        kind.append(kinds.setdefault((name, lo, o["rd"][-1][0] if o["rd"] else ""), len(kinds)))
    return [list(p.items()) for p in pred], kind, len(kinds)


def replay(ops, pred, order, m, log=None, held=None):
    wake = m["wake"]
    free, done, on, bank, df = {}, [0.0] * len(ops), [None] * len(ops), {}, 0.0
    by, last, alt = {}, {}, {}
    for j, a in order:
        o = ops[j]
        q, call, c = o["alts"][a]
        s = free.get(q, 0.0)
        by[j] = last.get(q)
        for i, link in pred[j]:
            if not link:
                d = done[i] + (0.0 if on[i] == q == "P" else wake)
                if d > s:
                    s, by[j] = d, i
        for b in o["banks"]:
            if b in bank and bank[b][0] != q and bank[b][1] + wake > s:
                s, by[j] = bank[b][1] + wake, bank[b][2]
        on[j], last[q], alt[j] = q, j, a
        free[q] = s + c
        done[j] = s + c + o["lat"]
        if o["bytes"]:
            df = max(df, s + c + 0.6 * DLAT) + o["bytes"] / m["bpn"]
            done[j] = df + 0.4 * DLAT
        for b in o["banks"]:
            bank[b] = (q, done[j], j)
        if log is not None:
            log.append((s, q, c, o["wr"][0]))
    if held is not None:
        j = done.index(max(done))
        while by[j] is not None:
            if all(i != by[j] for i, link in pred[j]):
                held.append((by[j], j, alt[by[j]]))
            j = by[j]
    return max(done)


def slot(seq, e):
    lo, hi = 0, len(seq)
    while lo < hi:
        mid = (lo + hi) // 2
        if seq[mid] < e:
            lo = mid + 1
        else:
            hi = mid
    seq.insert(lo, e)


def place(ops, before, after, rank, spare, m, lat, forward):
    n = len(ops)
    wake = m["wake"]
    left = [len(p) for p in before]
    st, en, on, alt = [0.0] * n, [0.0] * n, [None] * n, [0] * n
    busy, bank = {}, {}
    df = 0.0
    ready = sorted((rank[j], j) for j in range(n) if not left[j])
    while ready:
        j = ready.pop(0)[1]
        o = ops[j]
        best = None
        for a, (q, call, c) in enumerate(o["alts"]):
            s = 0.0
            for i, link in before[j]:
                d = st[i] if link == 1 and forward else en[i] + (0.0 if link or on[i] == q == "P" else wake)
                if d > s:
                    s = d
            if not forward:
                s += lat[j]
            lists = [(busy.setdefault(q, []), 0.0)] + [(bank.setdefault(b, []), wake) for b in o["banks"]]
            moved = True
            while moved:
                moved = False
                for iv, gap in lists:
                    lo, hi = 0, len(iv)
                    while lo < hi:
                        mid = (lo + hi) // 2
                        if iv[mid][1] + gap <= s:
                            lo = mid + 1
                        else:
                            hi = mid
                    while lo < len(iv) and iv[lo][0] - gap < s + c:
                        if (not gap or iv[lo][2] != q) and iv[lo][1] + gap > s:
                            s = iv[lo][1] + gap
                            moved = True
                        lo += 1
            v = s + c + (spare[j] if a == len(o["alts"]) - 1 > 0 else 0.0)
            if best is None or v < best[0]:
                best = (v, s, c, q, a, lists)
        v, s, c, q, a, lists = best
        for iv, gap in lists:
            slot(iv, (s, s + c, q))
        st[j], on[j], alt[j] = s, q, a
        en[j] = s + c
        if forward:
            en[j] += o["lat"]
            if o["bytes"]:
                df = max(df, s + c + 0.6 * DLAT) + o["bytes"] / m["bpn"]
                en[j] = df + 0.4 * DLAT
            lat[j] = en[j] - s - c
        for i, link in after[j]:
            left[i] -= 1
            if not left[i]:
                slot(ready, (rank[i], i))
    return st, en, alt


def plan(builds, seed):
    ops, m = builds[0], MODELS[0]
    n = len(ops)
    before, kind, kinds = schedule(ops)
    after = [[] for _ in range(n)]
    for j in range(n):
        for i, link in before[j]:
            after[i].append((j, link))
    rank = [0.0] * n
    later = {}
    for j in range(n - 1, -1, -1):
        rank[j] = min([0.0] + [rank[i] for i, link in after[j]]) - ops[j]["alts"][0][2] - ops[j]["lat"] - m["wake"]
        name = ops[j]["wr"][0][0]
        if name == "fr":
            rank[j] -= BIAS.get(ops[j]["step"][0], 0.0)
        if name in SHARE:
            rank[j] = later[name] = min(rank[j], later.get(name, 0.0) - SHARE[name] * ops[j]["alts"][0][2])
    rng = np.random.default_rng(seed)
    lat = [0.0] * n
    either = sorted(set(kind[j] for j in range(n) if len(ops[j]["alts"]) > 1))
    steps = sorted(set(o["step"][0] for o in ops))
    best, cur, lean, held = None, 0.0, [300.0] * n, []
    for r in range(ROUNDS):
        now = list(rank)
        spare = list(lean)
        if r % MIX == 1:
            for _ in range(1 + int(rng.integers(2))):
                k, t = steps[int(rng.integers(len(steps)))], int(rng.integers(3))
                d = float(rng.choice([-3000.0, -1500.0, -700.0, -300.0, 300.0, 700.0, 1500.0, 3000.0]))
                now = [now[j] + d if ops[j]["step"][0] == k and t in (2, ops[j]["step"][1]) else now[j] for j in range(n)]
        elif r % MIX == 0:
            size = float(rng.choice([30.0, 100.0, 300.0, 1000.0]))
            noise = rng.normal(0.0, 1.0, kinds) * size * (rng.random(kinds) < float(rng.choice([0.03, 0.1, 0.3])))
            now = [rank[j] + float(noise[kind[j]]) for j in range(n)]
            for _ in range(int(rng.integers(3))):
                k, v = either[int(rng.integers(len(either)))], float(rng.choice([0.0, 200.0, 500.0, 1000.0, 2000.0, 5000.0]))
                spare = [v if kind[j] == k else spare[j] for j in range(n)]
        elif held:
            for _ in range(1 + int(rng.integers(3))):
                i, j, a = held[int(rng.integers(len(held)))]
                if len(ops[i]["alts"]) > 1 and rng.random() < 0.4:
                    spare[i] = 5000.0 if a == len(ops[i]["alts"]) - 1 else -5000.0
                elif rng.random() < 0.5:
                    now[i] = max(now[i], now[j]) + float(rng.choice([1.0, 300.0, 1500.0]))
                else:
                    top = now[i]
                    stack = [j]
                    while stack:
                        x = stack.pop()
                        if now[x] >= top:
                            now[x] = top - 1.0
                            stack += [y for y, link in before[x]]
        new = spare
        for again in range(1 + (r < 10 or r % 12 == 0)):
            if again:
                st, en, alt = place(ops, after, before, [-x for x in en], spare, m, lat, False)
                now = [-x for x in en]
            st, en, alt = place(ops, before, after, now, spare, m, lat, True)
            if best is not None and max(en) > 1.02 * best[2][0]:
                continue
            order = [(j, alt[j]) for j in sorted(range(n), key=lambda j: (st[j], j))]
            t = [replay(b, before, order, x) for b, x in zip(builds, MODELS)]
            v = sum(math.log(x) for x in t)
            if best is None or v <= cur + HEAT * (1.0 - r / ROUNDS) * float(rng.random()):
                cur, rank, lean, held = v, now, new, []
                for b, x in zip(builds, MODELS):
                    replay(b, before, order, x, held=held)
            if best is None or v <= best[0]:
                best = (v, order, t)
    return polish(builds, before, after, best[1], rng, FIRSTS, GLOW)


def best_plan(builds):
    before = schedule(builds[0])[0]
    after = [[] for _ in before]
    for j, p in enumerate(before):
        for i, link in p:
            after[i].append((j, link))
    found = sorted((plan(builds, SEED + i) for i in range(STARTS)), key=lambda x: x[0])
    rng = np.random.default_rng(SEED)
    found = sorted((polish(builds, before, after, x[1], rng, SWEEPS // 4, GLOW2) for x in found[:2]), key=lambda x: x[0])
    return polish(builds, before, after, found[0][1], rng, SWEEPS, GLOW2)[1]


def refine(builds, before, after, order, rng):
    n = len(order)
    ops = builds[0]
    names = {}
    number = lambda x: names.setdefault(x, len(names))
    on = [[number(q) for q, call, c in o["alts"]] for o in ops]
    banks = [[number(b) for b in o["banks"]] for o in ops]
    pe = [o["alts"][0][0] == "P" for o in ops]
    cases, weight = [], np.full(n, 1.0 / n)
    for b, m in zip(builds, MODELS):
        cases.append(([[x[2] for x in o["alts"]] for o in b], [o["lat"] for o in b], [o["bytes"] / m["bpn"] for o in b],
                      [[(i, 0.0 if pe[i] and pe[j] else m["wake"]) for i, link in before[j] if not link] for j in range(n)],
                      m["wake"]))

    def times(seq, alt, first, last, old):
        out, v, state = [], 0.0, []
        for (price, lat, flow, need, wake), (was, past) in zip(cases, old):
            done, marks = list(was), past[:first // 16 + 1]
            free, who, df = list(marks[-1][0]), list(marks[-1][1]), marks[-1][2]
            for z in range(first // 16 * 16, n, 16):
                if z > last and marks[-1] == past[z // 16] and done == was:
                    marks = past
                    break
                for j in seq[z:z + 16]:
                    a = alt[j]
                    q = on[j][a]
                    s = free[q]
                    for i, d in need[j]:
                        d += done[i]
                        if d > s:
                            s = d
                    mine = banks[j]
                    if mine:
                        for b in mine:
                            if who[b] != q and free[b] > s:
                                s = free[b]
                        s += price[j][a]
                        free[q] = done[j] = s
                        for b in mine:
                            who[b], free[b] = q, s + wake
                    else:
                        s += price[j][a]
                        free[q] = s
                        if flow[j]:
                            df = max(df, s + 0.6 * DLAT) + flow[j]
                            done[j] = df + 0.4 * DLAT
                        else:
                            done[j] = s + lat[j]
                marks.append((list(free), list(who), df))
            end = max(done)
            out.append(end)
            state.append((done, marks))
            v += math.log(end) + MEAN * float(np.dot(weight, done)) / end
        return v, out, state

    def weigh(seq, alt, state):
        total = np.zeros(n)
        for (price, lat, flow, need, wake), (done, marks) in zip(cases, state):
            tail, rest, who = [0.0] * n, [0.0] * len(names), [-1] * len(names)
            for j in seq[::-1]:
                q = on[j][alt[j]]
                s = max(tail[j], rest[q] - lat[j])
                for b in banks[j]:
                    if who[b] != q and rest[b] > s:
                        s = rest[b]
                tail[j] = s
                s += lat[j] + price[j][alt[j]]
                rest[q] = s
                for b in banks[j]:
                    who[b], rest[b] = q, s + wake
                for i, d in need[j]:
                    if s + d > tail[i]:
                        tail[i] = s + d
            total += np.exp(np.minimum(np.array(done) + np.array(tail) - max(done), 0.0) / SLACK)
        weight[:] = total / total.sum()

    def chain(seq, alt, state):
        k = int(rng.integers(len(cases)))
        price, lat, flow, need, wake = cases[k]
        done, held = state[k][0], []
        p = seq.index(done.index(max(done)))
        while True:
            j = seq[p]
            q, s, by, z, left = on[j][alt[j]], 0.0, None, -1, set(banks[j])
            for i, d in need[j]:
                if done[i] + d > s:
                    s, by = done[i] + d, i
            mate = True
            for x in range(p - 1, -1, -1):
                i = seq[x]
                if on[i][alt[i]] == q:
                    if mate and not flow[i] and done[i] - lat[i] > s:
                        s, z = done[i] - lat[i], x
                    mate = False
                    left.difference_update(banks[i])
                elif left and not left.isdisjoint(banks[i]):
                    if done[i] + wake > s:
                        s, z = done[i] + wake, x
                    left.difference_update(banks[i])
                if not mate and not left:
                    break
            if z >= 0:
                if all(i != seq[z] for i, link in before[j]):
                    held.append((z, p))
                p = z
            elif by is None:
                return held
            else:
                p = seq.index(by)

    def ahead(seq, lo, hi, links):
        tied = {seq[hi - 1]}
        for x in range(hi - 2, lo - 1, -1):
            if any(i in tied for i, link in links[seq[x]]):
                tied.add(seq[x])
        return [x for x in seq[lo:hi] if x in tied], [x for x in seq[lo:hi] if x not in tied]

    seq, alt = [j for j, a in order], [0] * n
    for j, a in order:
        alt[j] = a
    either = [j for j in range(n) if len(on[j]) > 1]
    cur, t, state = times(seq, alt, 0, n, [([0.0] * n, [([0.0] * len(names), [-1] * len(names), 0.0)])] * len(cases))
    best, held, stale = (sum(math.log(x) for x in t), seq, alt, t), [], True
    for r in range(STEPS):
        move = float(rng.random())
        new, pick = seq, alt
        if r % SORT == 0:
            log, k = [], int(rng.integers(len(cases)))
            replay(builds[k], before, [(j, alt[j]) for j in seq], MODELS[k], log=log)
            new = seq = [seq[x] for x in sorted(range(n), key=lambda x: (log[x][0], x))]
            cur, t, state = times(seq, alt, 0, n, state)
            stale = True
        if move < 0.7 and (stale or r % 16 == 0):
            held, stale = chain(seq, alt, state), False
        if move < 0.7 and held:
            lo, hi = held[int(rng.integers(len(held)))]
            i, j, hi = seq[lo], seq[hi], hi + 1
        if r % TIDY == 0:
            k = int(rng.integers(len(cases)))
            d = float(rng.choice([100.0, 500.0, 5000.0]))
            spare, lat = [-d if alt[j] == len(on[j]) - 1 else d for j in range(n)], [0.0] * n
            st, en, pick = place(builds[k], before, after, state[k][0], spare, MODELS[k], lat, True)
            if move < 0.7:
                st, en, pick = place(builds[k], after, before, [-x for x in en], spare, MODELS[k], lat, False)
                st, en, pick = place(builds[k], before, after, [-x for x in en], spare, MODELS[k], lat, True)
            new, x = sorted(range(n), key=lambda j: (st[j], j)), None
        elif move < 0.7 and held:
            if move < 0.2:
                x = i if len(on[i]) > 1 and (move < 0.1 or len(on[j]) == 1) else j
                if len(on[x]) == 1:
                    continue
                pick = list(alt)
                pick[x] = (alt[x] + 1 + int(rng.integers(len(on[x]) - 1))) % len(on[x])
            elif move < 0.45:
                tied, rest = ahead(seq, lo, hi, after)
                new = seq[:lo] + tied + rest + seq[hi:]
            else:
                tied, rest = ahead(seq[lo:hi][::-1], 0, hi - lo, before)
                new = seq[:lo] + rest[::-1] + tied[::-1] + seq[hi:]
        elif move < 0.8:
            x = either[int(rng.integers(len(either)))]
            pick = list(alt)
            pick[x] = (alt[x] + 1 + int(rng.integers(len(on[x]) - 1))) % len(on[x])
        else:
            lo = int(rng.integers(n - 1))
            hi = min(n, lo + 2 + int(rng.integers(REACH)))
            if move < 0.9:
                tied, rest = ahead(seq, lo, hi, after)
                new = seq[:lo] + tied + rest + seq[hi:]
            else:
                tied, rest = ahead(seq[lo:hi][::-1], 0, hi - lo, before)
                new = seq[:lo] + rest[::-1] + tied[::-1] + seq[hi:]
        if new == seq and pick is alt:
            continue
        if pick is not alt:
            lo, hi = (0, n) if x is None else (seq.index(x),) * 2
        v, t, then = times(new, pick, lo, hi, state)
        if v <= cur - WARM * (1.0 - r / STEPS) * math.log(1.0 - float(rng.random())):
            stale = True
            cur, seq, alt, state = v, new, pick, then
            v = sum(math.log(x) for x in t)
            if v < best[0]:
                best = (v, seq, alt, t)
    SPAN[:] = best[3]
    return [(j, best[2][j]) for j in best[1]]


def polish(builds, before, after, order, rng, sweeps, glow):
    n = len(order)
    ops = builds[0]
    names = {}
    number = lambda x: names.setdefault(x, len(names))
    on = [[number(q) for q, call, c in o["alts"]] for o in ops]
    banks = [[number(b) for b in o["banks"]] for o in ops]
    pe = [o["alts"][0][0] == "P" for o in ops]
    busy = [names["V"], names["S"], names["P"]]
    width = len(names)
    cases = []
    for b, m in zip(builds, MODELS):
        cases.append(([[x[2] for x in o["alts"]] for o in b], [o["lat"] for o in b], [o["bytes"] / m["bpn"] for o in b],
                      [[(i, 0.0 if pe[i] and pe[j] else m["wake"]) for i, link in before[j] if not link] for j in range(n)],
                      m["wake"]))

    def run(case, part, alt, done, free, who, df):
        price, lat, flow, need, wake = case
        for j in part:
            a = alt[j]
            q = on[j][a]
            s = free[q]
            for i, d in need[j]:
                d += done[i]
                if d > s:
                    s = d
            mine = banks[j]
            if mine:
                for b in mine:
                    if who[b] != q and free[b] > s:
                        s = free[b]
                s += price[j][a]
                free[q] = done[j] = s
                for b in mine:
                    who[b], free[b] = q, s + wake
            else:
                s += price[j][a]
                free[q] = s
                if flow[j]:
                    df = max(df, s + 0.6 * DLAT) + flow[j]
                    done[j] = df + 0.4 * DLAT
                else:
                    done[j] = s + lat[j]
        return df

    def frame(case, seq, alt, a, b):
        price, lat, flow, need, wake = case
        done, free, who = [0.0] * n, [0.0] * width, [-1] * width
        df = run(case, seq[:a], alt, done, free, who, 0.0)
        tail, rest, next_, flows = [0.0] * n, [0.0] * width, [-1] * width, 0.0
        for j in seq[:b - 1:-1] if b < n else []:
            q = on[j][alt[j]]
            if flow[j]:
                flows = flow[j] + max(flows, 0.4 * DLAT + tail[j])
                s = max(0.6 * DLAT + flows, rest[q])
            else:
                s = max(tail[j] + lat[j], rest[q])
            for x in banks[j]:
                if next_[x] != q and next_[x] >= 0 and rest[x] + wake > s:
                    s = rest[x] + wake
            s += price[j][alt[j]]
            rest[q] = s
            for x in banks[j]:
                next_[x], rest[x] = q, s
            for i, d in need[j]:
                if s + d > tail[i]:
                    tail[i] = s + d
        return done, free, who, df, tail, rest, next_, flows, max([0.0] + [done[i] + tail[i] for i in seq[:a]])

    def value(part, alt, frames):
        v, ends = 0.0, []
        for case, (done, free, who, df, tail, rest, next_, flows, over) in zip(cases, frames):
            free, who = list(free), list(who)
            df = run(case, part, alt, done, free, who, df)
            end = max(over, df + flows, max([done[j] + tail[j] for j in part]),
                      max([free[x] + rest[x] for x in range(width) if who[x] != next_[x] or who[x] < 0]))
            ends.append(end)
            v += math.log(end) + (MEAN * sum([done[j] for j in part]) / len(part)
                                  + NEAR * sum([free[q] + rest[q] for q in busy])) / end
        return v, ends

    def chain(part, alt, k, frames):
        price, lat, flow, need, wake = cases[k]
        done, free, who, df, tail, rest, next_ = frames[k][:7]
        run(cases[k], part, alt, done, list(free), list(who), df)
        where, seen, top, held = {j: x for x, j in enumerate(part)}, set(), (0.0, 0), []
        for x in range(len(part) - 1, -1, -1):
            j = part[x]
            q = on[j][alt[j]]
            s = tail[j]
            for y in [q] + banks[j]:
                if y not in seen and (y == q or next_[y] != q):
                    s = max(s, rest[y] - lat[j])
                seen.add(y)
            top = max(top, (done[j] + s, x))
        p = top[1]
        while True:
            j = part[p]
            q, s, by, z, left = on[j][alt[j]], 0.0, None, -1, set(banks[j])
            for i, d in need[j]:
                if done[i] + d > s:
                    s, by = done[i] + d, i
            mate = True
            for x in range(p - 1, -1, -1):
                i = part[x]
                if on[i][alt[i]] == q:
                    if mate and not flow[i] and done[i] - lat[i] > s:
                        s, z = done[i] - lat[i], x
                    mate = False
                    left.difference_update(banks[i])
                elif left and not left.isdisjoint(banks[i]):
                    if done[i] + wake > s:
                        s, z = done[i] + wake, x
                    left.difference_update(banks[i])
                if not mate and not left:
                    break
            if z >= 0:
                if all(i != part[z] for i, link in before[j]):
                    held.append((z, p))
                p = z
            elif by in where:
                p = where[by]
            else:
                return held

    def tied(part, links):
        mine = {part[-1]}
        for x in part[-2::-1]:
            if any(i in mine for i, link in links[x]):
                mine.add(x)
        return [x for x in part if x in mine], [x for x in part if x not in mine]

    seq, alt = [j for j, a in order], [0] * n
    for j, a in order:
        alt[j] = a
    best = None
    for sweep in range(sweeps):
        log, k = [], sweep % len(cases)
        replay(builds[k], before, [(j, alt[j]) for j in seq], MODELS[k], log=log)
        seq = [seq[x] for x in sorted(range(n), key=lambda x: (log[x][0], x))]
        warm = glow * (1.0 - sweep / sweeps)
        for a in range(-int(rng.integers(WINDOW // 2)), n - WINDOW // 2, WINDOW // 2):
            a, b = max(a, 0), min(n, a + WINDOW)
            frames = [frame(case, seq, alt, a, b) for case in cases]
            part = seq[a:b]
            cur, ends = value(part, alt, frames)
            held, stale = [], True
            idle = all(max(f[8], f[3] + f[7]) > e - 1.0 for f, e in zip(frames, ends))
            for move, u1, u2, u3 in rng.random((TRIES // 5 if idle else TRIES, 4)).tolist():
                if move < 0.7 and stale:
                    held, stale = chain(part, alt, int(u3 * 997) % len(cases), frames), False
                if move < 0.7 and held:
                    lo, hi = held[int(u1 * len(held))]
                    turn, first = move < 0.2, move < 0.45
                    x = part[lo if (u2 < 0.5 or len(on[part[hi]]) == 1) and len(on[part[lo]]) > 1 else hi]
                else:
                    lo = int(u1 * (len(part) - 1))
                    hi = min(len(part) - 1, lo + 1 + int(u2 * REACH))
                    turn, first, x = move < 0.78, move < 0.89, part[lo]
                new, was = part, alt[x]
                if turn:
                    if len(on[x]) == 1:
                        continue
                    alt[x] = (was + 1 + int(u2 * 991) % (len(on[x]) - 1)) % len(on[x])
                elif first:
                    mine, others = tied(part[lo:hi + 1], after)
                    new = part[:lo] + mine + others + part[hi + 1:]
                else:
                    mine, others = tied(part[lo:hi + 1][::-1], before)
                    new = part[:lo] + others[::-1] + mine[::-1] + part[hi + 1:]
                if new == part and not turn:
                    continue
                v, t = value(new, alt, frames)
                if v <= cur - warm * math.log(1.0 - u3):
                    cur, part, ends, stale = v, new, t, True
                else:
                    alt[x] = was
            seq[a:b] = part
            v = sum(math.log(x) for x in ends)
            if best is None or v < best[0]:
                best = (v, [(j, alt[j]) for j in seq], ends)
    SPAN[:] = best[2]
    return best


def build(g, core, T, topo, m):
    rank = T.rank_of(core)
    cores = list(T.cores)
    ops = []
    step = ["constants", 0]
    CY, PEC, GA, SC, FAR, BPN = m["cy"], m["pe"], m["ga"], m["sc"], m["far"], m["bpn"]

    def R(name, lo=0, hi=None, step=1, at=None):
        if hi is None:
            hi = SCRATCH[name][1][1]
        a = lo if at is None else at
        ap = T[name][:, a:hi] if step == 1 else T[name][:, a:hi:step]
        return (ap, [(name, lo, hi)], [], len(range(a, hi, step)), name, False)

    def W(name, ap, n=256):
        return (ap, [(name, 0, 1 << 20)], [], n, name, False)

    def IND(win, off):
        return (win[0].indirect(off[0]), win[1], off[1], 16 * off[3], win[4], True)

    def put(alts, outs, ins, sem=None, cnt=1, lat=0.0, nbytes=0, keep=False):
        rd, wr = [], []
        for x in ins:
            if isinstance(x, tuple):
                rd += x[1] + x[2]
        for x in outs:
            wr += x[1]
            rd += x[2]
        ops.append({"alts": alts, "rd": rd, "wr": wr, "sem": sem, "cnt": cnt, "lat": lat, "bytes": nbytes, "keep": keep,
                    "step": tuple(step),
                    "banks": set(r[0] for r in rd + wr if psum(r[0]))})

    def ap(x):
        return x[0] if isinstance(x, tuple) else x

    def cost(o, i, per, fix=50.0):
        if o[5]:
            return fix + o[3] * SC * CY
        if i[5]:
            return fix + i[3] * max(GA, per) * CY
        return max(64.0, i[3] * per) * CY

    def half(*xs):
        return 0.5 if all(SCRATCH[x[4]][2] in ("bfloat16", "float16", "uint16") for x in xs) else 1.0

    def a_cp(o, i):
        return ("V", lambda: g.vector.tensor_copy(o[0], i[0]), cost(o, i, half(o, i)))

    def a_ts(o, a, s1, op0, s2=None, op1=None):
        if op1 is None:
            return ("V", lambda: g.vector.tensor_scalar(o[0], a[0], ap(s1), None, op0), cost(o, a, half(o, a)))
        return ("V", lambda: g.vector.tensor_scalar(o[0], a[0], ap(s1), ap(s2), op0, op1), cost(o, a, half(o, a)))

    def a_act(o, i, func, bias=0.0, scale=1.0):
        if o[5]:
            return ("S", lambda: g.scalar.activation(o[0], i[0], func), cost(o, i, 1.0, 65.0))
        return ("S", lambda: g.scalar.activation(o[0], i[0], func, bias=ap(bias), scale=ap(scale)), cost(o, i, 1.0, 65.0))

    def a_sel(o, i, pat, op, fill, base, ch):
        return ("G", lambda: g.affine_select(o[0], i[0], pat, op, fill, base, ch), 170.0 + 2 * o[3] * CY)

    def cp(o, i):
        put([a_cp(o, i)], [o], [i])

    def tt(o, a, b, op):
        put([("V", lambda: g.vector.tensor_tensor(o[0], a[0], b[0], op),
              cost(o, a, 1.0 if psum(a[4]) or psum(b[4]) else 2.0))], [o], [a, b])

    def ts(o, a, s1, op0, s2=None, op1=None):
        put([a_ts(o, a, s1, op0, s2, op1)], [o], [a, s1, s2])

    def scan(o, a, b, init, op0, op1):
        put([("V", lambda: g.vector.tensor_tensor_scan(o[0], a[0], b[0], ap(init), op0, op1), cost(o, a, 2 * half(o, a, b)))],
            [o], [a, b, init])

    def ms(o, c):
        put([("V", lambda: g.vector.memset(o[0], c), cost(o, o, half(o)))], [o], [])

    def act(o, i, func, bias=0.0, scale=1.0):
        put([a_act(o, i, func, bias, scale)], [o], [i, bias, scale])

    def lin(o, i, scale, bias):
        put([a_act(o, i, F.Identity, bias, scale), a_ts(o, i, scale, A.mult, bias, A.add)], [o], [i, scale, bias])

    def relu(o, i, bias):
        put([a_act(o, i, F.Relu, bias), a_ts(o, i, bias, A.add, 0.0, A.max)], [o], [i, bias])

    def both(o, i, s_form, v_form):
        put([a_act(o, i, *s_form), a_ts(o, i, *v_form)], [o], [i] + list(s_form[1:]) + list(v_form[0::2]))

    def row(name):
        ops[-1]["keep"] = name

    def gather(o, i):
        put([a_act(o, i, F.Copy), a_cp(o, i)], [o], [i])

    def add_list(o, via, a, b):
        if DIRECT:
            tt(o, a, b, A.add)
        else:
            tt(via, a, b, A.add)
            gather(o, via)

    def zone(p):
        return 256 * (p if p < 4 or LIFTED else p + 1)

    def only(q):
        ops[-1]["alts"] = [a for a in ops[-1]["alts"] if q in ("*", a[0])]

    def low(o, via, i, bits):
        if ANDU:
            ts(o, i, bits, A.bitwise_and)
        else:
            ts(via, i, bits, A.bitwise_and)
            gather(o, via)

    def join(n):
        part = ops[-n:]
        del ops[-n:]
        calls = [o["alts"][0][1] for o in part]
        ops.append(dict(part[0], rd=list(dict.fromkeys(x for o in part for x in o["rd"])),
                        wr=list(dict.fromkeys(x for o in part for x in o["wr"])),
                        banks=set(x for o in part for x in o["banks"]),
                        alts=[(part[0]["alts"][0][0], lambda: [c() for c in calls][-1], sum(o["alts"][0][2] for o in part))]))

    def mm(o, l, r, start, stop):
        slow = 4 if SCRATCH[r[4]][2] == "float32" else 1
        put([("P", lambda: g.tensor.matmul(o[0], l[0], r[0], start, stop), max(64, r[3]) * slow * PEC)], [o], [l, r])

    def iota(o, pat, base, ch, flt=True):
        if flt:
            call = lambda: g.iota(o[0], pat, base, ch, allow_small_or_imprecise_dtypes=True)
        else:
            call = lambda: g.iota(o[0], pat, base, ch)
        put([("G", call, 130.0 + 2 * o[3] * CY)], [o], [])

    def select(o, pat, op, fill, base, ch):
        put([a_sel(o, o, pat, op, fill, base, ch)], [o], [o])

    def dma(o, i, q, sem, nbytes):
        eng = g.sync if q == "Y" else g.scalar
        put([(q, lambda: eng.dma_start(o[0], i[0]), 60.0)], [o], [i], sem, 16, DLAT + nbytes / BPN, nbytes, q == "Y")

    def wrap(o, name, lo, hi, start=True, stop=True, base="WB"):
        for r in range(16):
            mm(o, R(base, 15 - r, 143 - r), R(name, lo, hi, 16, lo + r), start and r == 0, stop and r == 15)
            if r == 7 and name in CUT:
                join(8)
        join(8 if name in CUT else 16)

    def col(j):
        return R("col", j, j + 1)

    held = [0]

    def own(i):
        z = held[0] % 4 * 128
        held[0] += 1
        scan(R("s1", z, z + i[3]), R("SEL", 0, i[3]), i, 0.0, A.add, A.min)
        return R("s1", z, z + i[3], 16, z + 15)

    def ext(t, name="hbm"):
        return (t, [] if name == "hbm" else [(name, 0, S)], [], 0, name, False)

    PG, PI, PW15, M0, MH, M15, AB, ZI, ZJ, ZK, DW, AS, AO, M2, CB, ODD, AC, C2K, CRAW, ZC = range(20)
    U_C1, U_C, U_A, U_A9, U_S, U_AT, U_W, U_P, U_FB, U_E, U_H = [16 * i for i in range(11)]
    W_S, W_AT, W_D, W_Y, W_FB, W_K, W_NZ, W_D1, W_D2, W_E, W_A, W_N, W_AD = [16 * i for i in range(13)]

    def u(c, lo=0, hi=256):
        return R("u16", c + lo // 16, c + hi // 16)

    def w(c, lo=0, hi=256):
        return R("w32", c + lo // 16, c + hi // 16)

    def pl(b, c, lo, hi):
        return R(b, c + lo // 16, c + hi // 16)

    XS = R("xsb", 16)
    RAW = 7.0 * S
    bufi, buff, bufy = (W(x, T[x][:, :, :]) for x in ("bufi", "buff", "bufy"))
    for y in range(2):
        dma(W("bufi", T.bufi[:, y, :]), ext(T.board[y:8:2, :]), "Y", "dB", 65536)
    dma(R("xsb", 16, 16 + S), ext(T.xs[:, :]), "Y", "dX", 1 << 20)
    dma(R("dsb", 0, S), ext(T.ds[:, :]), "Y", "dD", 1 << 21)
    for y in range(2):
        dma(ext(T.hmb[y:128:2, :], "hmb"), ext(T.hm[:, :]), "Y", "dH", 131072)
    TB = W("TB", T.TB[:, :, :])
    iota(R("pci", 0, 1), [[0, 1]], 0, 1, False)
    iota(R("grp"), [[1, 8], [0, 16]], 0, 0)
    iota(R("i16"), [[1, 16]], 0, 0)
    iota(R("XP"), [[1, 144]], 0, -1)
    iota(R("j16"), [[0, 8], [1, 16]], 0, 0)
    iota(R("M1b"), [[1, 256]], 0, 0)
    iota(R("ba"), [[0, AW]], S, 0)
    for o in ops[-7:]:
        o["keep"] = "first"
    iota(R("bd", S), [[0, BW - S]], S, 0)
    iota(R("neg"), [[0, 256]], S, 0)
    iota(TB, [[0, 256]], 4096, 0)
    select(TB, [[0, 8], [1, 32]], A.is_gt, -4096.0, -15, 0)
    select(TB, [[0, 8], [1, 32]], A.is_ge, 0.0, -15, 0)
    select(TB, [[-16, 8], [0, 32]], A.is_equal, 0.0, 0, 1)
    for k in range(16):
        o, i = R("TR", 128 * k, 128 * k + 128), W("TB", T.TB[:, :, 15 - k:31 - k], 128)
        put([a_sel(o, i, [[0, 128]], A.is_ge, 0.0, 0, 0), a_act(o, i, F.Copy), a_cp(o, i)], [o], [i])
    iota(R("NBM"), [[0, 128]], 0, 0)
    select(R("NBM"), [[-1, 128]], A.not_equal, 32.0, 0, 1)
    select(R("NBM"), [[-1, 128]], A.not_equal, -32.0, -1, 1)
    ms(R("ones"), 1.0)
    ms(R("rc", 0, 16), 0.0)
    ms(R("f", 256, 272), 1.0)
    ms(R("Bo", 256, 272), 2048.0)
    ms(R("xsb", 0, 16), 1e29)
    ms(R("xsb", 16 + S), 1e29)
    ms(R("dsb", S, S + 8), 0)
    ms(R("dwr"), 0.0)
    ts(R("pci", 2, 3), R("pci", 0, 1), 4, A.arith_shift_right)
    ts(R("pci", 4, 5), R("pci", 0, 1), 15, A.bitwise_and)
    cp(col(PG), R("pci", 2, 3))
    cp(col(PI), R("pci", 4, 5))
    ts(R("BLK"), R("grp"), col(PG), A.is_equal)
    ts(R("ID"), R("XP", 0, 128), 0.0, A.is_equal)
    ts(R("tm"), R("XP", 0, 128), 0.0, A.is_gt)
    tt(R("tm"), R("tm"), R("BLK"), A.mult)
    lin(R("UP"), R("ID"), float(S), 0.0)
    tt(R("UP"), R("UP"), R("tm"), A.add)
    lin(col(PW15), col(PI), -1.0, 15.0)
    ts(R("WB"), R("XP"), col(PW15), A.is_equal)
    ts(R("MK"), R("j16"), col(PI), A.is_equal, 0.5, A.subtract)
    lin(R("SEL"), R("MK"), 33.0 * BIG, 15.5 * BIG)
    ts(R("SE2"), R("MK"), -2.0 ** 21, A.mult, float(S), A.min)
    lin(col(C2K), col(PW15), -float(S), 0.0)
    for c, add in ((CB, 0.0), (CRAW, -RAW)):
        lin(col(c), col(PW15), BIG, add)
    lin(R("M1"), R("M1b"), 1.0, 0.0)
    put([("S", lambda: g.scalar.activation(T.L2[:, 16:24], T.rc[:, 0:8], F.Silu), 1400.0)], [R("L2", 16, 24)], [R("rc", 0, 8)])
    ts(R("keep"), R("j16"), 1.0, A.min)
    ts(col(M0), col(PI), 0.0, A.is_equal)
    ts(col(MH), col(PI), float(2 * rank + 1), A.is_equal)
    ts(col(M15), col(PI), 15.0, A.is_equal, -1.0, A.mult)
    ts(R("pci", 6, 7), R("pci", 0, 1), 1, A.bitwise_and)
    cp(col(ODD), R("pci", 6, 7))
    lin(col(M2), col(ODD), -1.0, 1.0)
    for name, src, scale in (("I16", "ID", 16.0), ("NI", "ID", -1.0), ("ID32", "ID", 1.0),
                             ("B16", "BLK", 16.0), ("B256", "BLK", 256.0), ("B2K", "BLK", 2048.0),
                             ("N4K", "BLK", -4096.0), ("NB", "BLK", -1.0), ("DW", "BLK", col(PI)), ("N15", "BLK", col(M15)),
                             ("B15", "BLK", -15.0 / 16), ("WB2", "WB", 2.0), ("WBI", "WB", col(PI)), ("WB0", "WB", col(M0)),
                             ("IE", "ID", col(M2)), ("IO", "ID", col(ODD))):
        lin(R(name), R(src), scale, 0.0)
    if "h" in SCAN[0]:
        lin(R("WBH", 0, 128), R("BLK"), col(MH), 0.0)
    else:
        lin(R("WBH"), R("WB"), col(MH), 0.0)
    tt(R("TRI"), R("tm"), R("ID"), A.subtract)
    lin(R("TRI"), R("TRI"), 2048.0, 0.0)
    lin(col(AB), col(PI), -512.0, 2048.5)
    lin(col(AC), col(AB), -1.0, 0.0)
    lin(col(ZK), col(PI), 2048.0, 2048.0)
    ts(R("clt"), R("i16"), col(PI), A.is_gt)
    for r in range(1, 16):
        o, i, c = R("LL", 128 * r, 128 * r + 128), R("NB"), R("clt", r, r + 1)
        put([a_sel(o, i, [[16, 8], [0, 16]], A.is_gt, 0.0, r, -1), a_act(o, i, F.Identity, 0.0, c), a_ts(o, i, c, A.mult)],
            [o], [i, c])
    if LEAST:
        lin(R("BRAW"), R("BLK"), -RAW / 16, 0.0)
    if LIFTED:
        lin(col(ZI), col(PI), 256.0, -896.0)
        lin(R("N4I"), R("ID"), -4096.0, 0.0)
    else:
        ts(col(ZI), col(PI), 3.5, A.is_gt, 256.0, A.mult)
        lin(col(ZJ), col(PI), 256.0, -1024.0)
        tt(col(ZI), col(ZI), col(ZJ), A.add)
    if PLAIN:
        ts(R("TI32"), R("UP"), 0.5, A.min)
        lin(col(ZJ), col(PI), 128.0, 128.0)
    lin(col(DW), col(PI), 1.0, 1024.0)
    for split in set(SPLIT):
        for lo, hi in HALVES if split else [(0, 256)]:
            z = 32 * split
            ts(R("dwr", z + lo // 8, z + (lo + hi) // 16), R("i16", lo // 16, hi // 16), 16.0, A.mult, col(DW), A.add)
    if "p" in SCAN[0]:
        lin(w(W_E, 0, 128), R("dwr", 48, 56), 1.0, col(CB))
    ts(col(AS), col(PI), 2.0, A.not_equal)
    lin(col(AO), col(AS), 2048.0 - 2 * S, 2.0 * S)
    step[0] = "fold"
    ts(R("X"), bufi, S + 1, A.bitwise_and)
    both(R("p7", 0, 256), R("X"), (F.Relu, 2.0 * S, -2.0 * S), (0.0, A.is_equal, 2.0 * S, A.mult))
    tt(buff, bufi, R("p7", 0, 256), A.add)
    gather(bufy, bufi)
    for y in range(2):
        dma(ext(T.ba[16 * y:128:32, 0:S], "ba"), W("bufy", T.bufy[:, y, :]), "Y", "dR", 65536)
        dma(ext(T.ba[16 * y + 2:128:32, 0:S], "ba"), W("buff", T.buff[:, y, :]), "Y", "dR", 65536)
    dma(R("bd", 0, S), R("ba", 0, S), "Y", "dC", 1 << 21)

    bdw, baw = R("bd"), R("ba")

    def targets(lst, base, lo, hi, o):
        tt(R("t", o + lo, o + hi), IND(R("dsb"), u(lst, lo, hi)), R(base, lo, hi), A.add)
        low(R("q16", o + lo, o + hi), R("q", o + lo, o + hi), R("t", o + lo, o + hi), S - 1)
        lin(R("qo", o + lo, o + hi), R("q16", o + lo, o + hi), 1.0, -2048.0)

    def square(o, lo, hi, stop):
        for i, (mat, name) in enumerate((("B256", "T1"), ("B16", "T2"), ("DW", "OH"))):
            mm(o, R(mat), R(name, lo, hi), i == 0, stop and i == 2)
        join(3)

    def dedupe(pb, kw, o, after):
        def equal(b, first, last, cross, hi, stop=False):
            for z in range(first, last, PAIR):
                step[0] = "equal %d %d %d" % (o, z // 8, hi)
                cs = range(z, min(z + PAIR, last))
                for c in cs:
                    a = 128 if cross else 16 * c
                    ts(R("E", 256 * c + a, 256 * c + hi), R("key", o + a, o + hi), R("w32", kw + c, kw + c + 1), A.is_equal)
                join(len(cs))
                row("equal")
                cs = [(c, 128 if cross else 16 * c + 16) for c in cs if cross or 16 * c + 16 < hi]
                for c, a in cs:
                    mm(R(b, a, hi), R("NB"), R("E", 256 * c + a, 256 * c + hi), False, stop and c == last - 1)
                if cs:
                    join(len(cs))

        for b, (lo, hi) in zip(pb, HALVES if len(pb) > 1 else [(0, 256)]):
            mm(R(b, lo, hi), R("N15"), R("T1", lo, hi), True, False)
            if o == 0:
                mm(R(b, lo, lo + 128), R("ID"), R("A1", lo, lo + 128), False, False)
            else:
                for i in range(2 if lo else 0):
                    mm(R(b, lo, hi), R("ID"), R("MK"), False, False)
                both(R("E", S + lo, S + hi), R("key", o + lo, o + hi), (F.Relu, 1.0 - S, 1.0), (float(S), A.is_equal))
                mm(R(b, lo, hi), R("NB"), R("E", S + lo, S + hi), False, False)
            early = LEAD if hi == 256 else 0
            if WIDE and hi - lo == 256:
                mm(R(b, 128, 256), R("ID"), R("A1", 128, 256), False, False)
                equal(b, 8, 16, False, 256)
                equal(b, 0, 8, False, 256)
                for r in range(1, 16):
                    diag = (T.E[:, r:17 * 256:272], [("E", 272 * i, 272 * i + 16) for i in range(16)], [], 16, "E", False)
                    mm(R(b, 0, 256, 16, r), R("LL", 128 * r, 128 * r + 128), diag, False, r == 15)
                join(15)
                after(lo, hi)
                continue
            equal(b, lo // 16, 8, False, 128)
            if o == 0 and hi - lo == 256:
                mm(R(b, 128, 256), R("ID"), R("A1", 128, 256), False, False)
            equal(b, 0, early, True, 256)
            equal(b, 8, hi // 16, False, 256)
            for r in range(1, 16):
                diag = (T.E[:, 17 * lo + r:17 * hi:272], [("E", 272 * i, 272 * i + 16) for i in range(lo // 16, hi // 16)],
                        [], 16, "E", False)
                mm(R(b, lo, hi, 16, lo + r), R("LL", 128 * r, 128 * r + 128), diag, False, r == 15 and hi < 256)
            join(15)
            if hi == 256:
                equal(b, early, 8, True, 256, True)
            after(lo, hi)

    table = []
    for t in range(RO):
        PW = "PW%d" % t
        land = "land%d" % t
        step[:] = ["search", t]
        for b in range(8):
            put([("V", (lambda b: lambda: g.vector.transpose(T.Bw[:, b:256:8], T.buff[:, :, 16 * b:16 * b + 16]))(b), 64 * CY)],
                [R("Bw", 32 * b, 32 * b + 32)], [W("buff", None)])
        join(8)
        ops[-1]["behind"] = table
        ts(R("f", 0, 256), R("Bw"), float(S), A.is_lt if t else A.is_gt)
        scan(R("rc", 16, 288), R("f"), R("ones"), 0.0, A.add, A.mult)
        lin(R("Bo", 0, 256), R("Bw"), 1.0, -2048.0 if t else -2048.0 - 2 * S)
        if t and PLAIN:
            put([("S", lambda: g.scalar.activation(T.fx[:, :], T.nat[:, :], F.Sign, bias=S - 0.5, scale=-1.0,
                                                   accum_out=T.col[:, ZC:ZC + 1]), 256 * CY + 25.0)],
                [R("fx"), col(ZC)], [R("nat")])
            mm(R("p0", 0, 1), R("TI32"), col(ZC), True, True)
            ts(R("T1"), R("M1b"), R("p0", 0, 1), A.subtract, col(ZJ), A.is_ge)
        else:
            mm(R("p0", 0, 16), R("BLK"), R("rc", 16, 272, 16, 31), True, True)
            ts(R("T1"), R("M1b"), own(R("p0", 0, 16)), A.subtract, col(CB), A.is_ge)
        wrap(R("p4", 0, 17), "rc", 16, 288)
        mm(R("p1", 0, 272), R("UP"), R("f"), True, False)
        mm(R("p1", 0, 272), R("BLK"), R("rc", 15, 287), False, True)
        first = 128 if "a" in SCAN[t] else 0
        if first:
            mm(R("p5", 0, 128), R("BLK"), R("T1", 0, 128), True, True)
            lin(u(U_C1, 0, 128), own(R("p5", 0, 128)), 1.0, col(CB))
        wrap(pl("p3", 0, first, 256), "T1", first, 256)
        lin(R("L2", 0, 17), R("p4", 0, 17), 1.0, 0.0)
        lin(R("G"), R("p1", 0, 272), 1.0, -float(S))
        gather(u(U_C1, first, 256), pl("p3", 0, first, 256))
        if t == 0:
            step[0] = "table 0"
            ts(R("xo", 0, 256), R("Bw"), float(S), A.min)
            for c in range(0, 256, CX[0]):
                gather(R("XB0", 16 * c, 16 * (c + CX[0])), IND(XS, R("xo", c, c + CX[0])))
            step[0] = "table 1"
            both(R("fx"), R("G", 0, 256), (F.Relu, 256.0 * 4 * S, -4.0 * S), (256.0, A.is_lt, 4.0 * S, A.mult))
            mm(R("p7", 0, 256), R("ID32"), R("Bo", 0, 256), True, False)
            mm(R("p7", 0, 256), R("NI"), R("fx"), False, True)
            relu(R("xo", 256, 512), R("p7", 0, 256), 2048.0 + 16)
            for c in range(0, 256, CX[1]):
                gather(R("XB1", 16 * c, 16 * (c + CX[1])), IND(R("xsb"), R("xo", 256 + c, 256 + c + CX[1])))
        for lo, hi in SEARCH[t]:
            step[0] = "level %d" % lo
            tt(R("T2", lo, hi), IND(R("L2"), u(U_C1, lo, hi)), R("M1", lo, hi), A.is_le)
            pb = "p4" if lo == 0 else "p0"
            if "bB"[lo > 0] in SCAN[t]:
                mm(R(pb, 256 + lo, 256 + hi), R("B16"), R("T1", lo, hi), True, False)
                mm(R(pb, 256 + lo, 256 + hi), R("BLK"), R("T2", lo, hi), False, True)
                lin(u(U_C, lo, hi), own(R(pb, 256 + lo, 256 + hi)), 1.0, col(CB))
            else:
                gather(R("C1", lo // 16, hi // 16), u(U_C1, lo, hi))
                mm(pl(pb, 32, lo, hi), R("I16"), R("C1", lo // 16, hi // 16), True, False)
                wrap(pl(pb, 32, lo, hi), "T2", lo, hi, False)
                gather(u(U_C, lo, hi), pl(pb, 32, lo, hi))
            gather(R("C2", lo // 16, hi // 16), u(U_C, lo, hi))
        for lo, hi in SEARCH[t]:
            step[0] = "row %d" % lo
            pa = "p3" if lo == 0 else "p2"
            tt(R("OH", lo, hi), IND(R("G"), u(U_C, lo, hi)), R("M1", lo, hi), A.is_equal)
            tt(R("Zu", lo, hi), IND(R("Bo"), u(U_C, lo, hi)), R("OH", lo, hi), A.mult)
            square(R("p5", lo, hi), lo, hi, True)
            lin(R("srep", lo, hi), R("p5", lo, hi), 1.0, 0.0)
            if "cC"[lo > 0] in SCAN[t]:
                mm(R("p6", lo, hi), R("BLK"), R("Zu", lo, hi), True, True)
                lin(u(U_A, lo, hi), own(R("p6", lo, hi)), 1.0, col(C2K))
            else:
                wrap(pl(pa, 32, lo, hi), "Zu", lo, hi)
                lin(u(U_A, lo, hi), pl(pa, 32, lo, hi), 1.0, 2048.0)
                step[0] = "aside"
                mm(R("p6", lo, hi), R("BLK"), R("Zu", lo, hi), True, True)
        step[0] = "aside"
        mm(R("p0", 64, 80), R("I16"), R("C2"), True, False)
        wrap(R("p0", 64, 80), "OH", 0, 256, False, True, "WBI")
        gather(w(W_S), R("p0", 64, 80))
        gather(u(U_S), w(W_S))
        lin(R("arep"), R("p6", 0, 256), col(AS), col(AO))
        both(R("ge"), R("p6", 0, 256), (F.Sign, col(AB), 1.0), (col(AC), A.is_gt, 2.0, A.mult))
        cp(R("wi", 0, 16), u(U_A))
        low(u(U_A9), R("wi", 16, 32), R("wi", 0, 16), 511)
        lin(R("hg"), IND(R("hmb"), u(U_A9)), 1.0, -2048.0)
        act(IND(bdw, u(U_S)), R("neg"), F.Silu)
        for lo, hi in FIRST[t]:
            step[0] = "targets %d" % lo
            targets(U_A, "srep", lo, hi, 0)
        for lo, hi in HALVES:
            gather(R("xa", lo, hi), IND(XS, u(U_A, lo, hi)))
            mm(R("p2", lo, hi), R("ID"), R("xa", lo, hi), True, True)
        def compare(b):
            step[0] = "compare %d" % b
            lo, hi = 64 * b, 64 * b + 64
            pc = R(PC[b], 128 + lo, 128 + hi)
            for c in range(lo, hi, CV[b]):
                gather(R("xv", 16 * c, 16 * (c + CV[b])), IND(R("XB%d" % t, 0, S), R("q16", c, c + CV[b])))
            for ks in GROUPS:
                outs = [(k, R("cmp", 16 * lo + 64 * k, 16 * lo + 64 * k + 64)) for k in ks]
                for k, o in outs:
                    tt(o, R("xv", 16 * lo, 16 * hi, 16, 16 * lo + k), R("p2", lo, hi), A.is_lt)
                join(len(ks))
                row("compare")
                ops[-1]["behind"] = [mark[x] for x in AHEAD if AHEAD[x] == (b, ks[0])]
                if ks[0] == 0:
                    mm(pc, R("B15"), R("ones", 0, 64), True, False)
                for k, o in outs:
                    mm(pc, R("WB2", 15 - k, 143 - k), o, False, k == 15)
                join(len(ks))
            both(R("good", lo, hi), pc, (F.Sign, 0.0, 1.0), (1.0, A.min, -1.0, A.max))

        mark = {}
        for h, (lo, hi) in enumerate(HALVES):
            compare(2 * h)
            compare(2 * h + 1)
            pb, pw = ("p5", "p4") if h == 0 else ("p6", "p3")
            good = R("good", lo, hi)
            step[0] = "claim %d" % h
            mm(R(pb, 256, 384), R("ID"), R("qo", lo, hi), True, False)
            mm(R(pb, 256, 384), R("TRI"), good, False, True)
            square(R("p7", lo, hi), lo, hi, False)
            mm(R("p7", lo, hi), R("B2K"), good, False, True)
            mm(R("p7", 256 + lo, 256 + hi), R("NBM"), R("ge", lo, hi), True, False)
            mm(R("p7", 256 + lo, 256 + hi), R("BLK"), good, False, True)
            ts(R("Z", lo, hi), R(pb, 256, 384), col(ZK), A.add, 2048.0, A.min)
            mark["pick"] = len(ops) - 1
            if LEAST:
                lin(R("back", lo, hi), R("p7", lo, hi), 1.0, 32768.0)
            else:
                relu(R("back", lo, hi), R("p7", lo, hi), S - 32768.0)
            act(R("A1", lo, hi), R("p7", 256 + lo, 256 + hi), F.Sign, bias=-49.0)
            at = R(pb, lo, hi)
            if LEAST:
                mm(at, R("BRAW"), R("ones", 0, 128), True, False)
                mm(at, R("BLK"), R("Z", lo, hi), False, True)
                tt(R("key", lo, hi), at, R("back", lo, hi), A.min)
                scan(R("s2", lo, hi), R("SE2"), R("key", lo, hi), 0.0, A.add, A.max)
                aw = R("s2", lo, hi, 16, lo + 15)
            else:
                mm(at, R("NI32"), R("back", lo, hi), True, False)
                mm(at, R("BLK"), R("Z", lo, hi), False, True)
                aw = own(at)
                lin(R("key", lo, hi), at, 1.0, -RAW)
            mark["own"] = len(ops) - 1
            lin(u(U_AT, lo, hi), aw, 1.0, col(C2K))
            lin(w(W_AT, lo, hi), aw, 1.0, col(C2K))
            step[0] = "victim %d" % h
            lin(R("whom", lo, hi), IND(baw, u(U_AT, lo, hi)), 1.0, -2048.0)
            if "vw"[h] in SCAN[t]:
                mm(R(pw, 0, 128), R("B0"), R("whom", lo, hi), True, True)
                lin(u(U_W, lo, hi), own(R(pw, 0, 128)), 1.0, col(C2K))
            else:
                wrap(R(pw, 0, 8), "whom", lo, hi, True, True, "WB0")
                lin(u(U_W, lo, hi), R(pw, 0, 8), 1.0, 2048.0)
            mark["targets"] = len(ops)
            targets(U_W, "key", lo, hi, 256)
            step[0] = "payload"
            mm(R(pb, 384, 512), R("IO"), R("hg", lo, hi), True, False)
            mm(R(pb, 384, 512), R("IE"), R("whom", lo, hi), False, True)
            lin(R("pay", lo, hi), R(pb, 384, 512), 1.0, LIFT + 2048.0)
            step[0] = "free %d" % h
            for c in range(lo, hi, CF):
                both(R("fr", 16 * c, 16 * (c + CF)), IND(baw, R("q16", 256 + c, 256 + c + CF)),
                     (F.Relu, 1.0 - S, 1.0), (float(S), A.is_equal))
                only(FR[c // CF])
        step[0] = "payload"
        for p in range(N):
            z = zone(p)
            iota(R(PW, z, z + 16), [[2, 16]], REB0 + int(LIFT) + 32 * rank, 0)
        for lo, hi in HALVES if SPLIT[t] else [(0, 256)]:
            tt(w(W_D, lo, hi), w(W_AT, lo, hi), w(W_S, lo, hi), A.subtract)
        for h, (lo, hi) in enumerate(HALVES):
            pb = "p1" if h == 0 else "p2"
            step[0] = "weigh %d" % h
            mm(R(pb, 0, 128), R("ID"), R("qo", 256 + lo, 256 + hi), True, False)
            mm(R(pb, 0, 128), R("B2K"), R("A1", lo, hi), False, False)
            for c in range(0, 128, 64):
                for k in range(16):
                    z = 16 * (lo + c)
                    mm(R(pb, c, c + 64), R("TR", 128 * k, 128 * k + 128), R("fr", z, z + 1024, 16, z + k), False, False)
                join(16)
        def send(lo, hi):
            step[0] = "send %d" % lo
            n, pp = hi - lo, 32 + lo // 8
            fl = R("Zp", 2 * lo + n, 2 * hi)
            won = R("p5" if lo else "p0", lo, hi)
            relu(fl, won, 0.0)
            if LIFTED:
                mm(R("p7", lo, hi), R("N4I"), fl, True, False)
            else:
                relu(R("p7", lo, hi), won, 0.0)
            if lo:
                gather(col(ZC), R("sc", lo - 1, lo))
            scan(R("sc", lo, hi), fl, R("ones", lo, hi), col(ZC if lo else ZI), A.add, A.subtract)
            if LIFTED:
                mm(R("p7", lo, hi), R("ID"), R("sc", lo, hi), False, True)
                ts(R("Zp", 2 * lo, 2 * lo + n), R("p7", lo, hi), float(S), A.add, 1152.0, A.min)
            else:
                tt(R("Zp", 2 * lo, 2 * lo + n), R("sc", lo, hi), R("p7", lo, hi), A.mult)
            if lo and "p" in SCAN[0]:
                mm(R("p3", 256, 384), R("BLK"), R("Zp", 2 * lo, 2 * lo + n), True, True)
                tt(u(U_P, lo, hi), own(R("p3", 256, 384)), w(W_E, 0, n), A.add)
                wrap(R("p4", pp + n // 16, pp + n // 8), "Zp", 2 * lo + n, 2 * hi)
            else:
                mm(R("p4", pp, pp + n // 8), R("ID"), R("dwr", 32 * SPLIT[t] + lo // 8, 32 * SPLIT[t] + hi // 8), True, False)
                wrap(R("p4", pp, pp + n // 8), "Zp", 2 * lo, 2 * hi, False)
                lin(u(U_P, lo, hi), R("p4", pp, pp + n // 16), 1.0, 1024.0 - 16 * 1152 if LIFTED else 0.0)
            act(IND(R(PW), u(U_P, lo, hi)), R("pay", lo, hi), F.Silu)
            tt(w(W_Y, lo, hi), R("p4", pp + n // 16, pp + n // 8), w(W_D, lo, hi), A.mult)
            tt(w(W_FB, lo, hi), w(W_Y, lo, hi), w(W_S, lo, hi), A.add)

        dedupe(["p0", "p5"] if SPLIT[t] else ["p0"], W_AT, 0, send)
        gather(u(U_FB), w(W_FB))
        act(IND(bdw, u(U_FB)), R("neg"), F.Silu)
        z = zone(rank)
        o, i = R(land, 16 * rank, 16 * rank + 16), R(PW, z, z + 16)
        put([a_sel(o, i, [[0, 16]], A.is_ge, 0.0, 0, 0), a_act(o, i, F.Copy), a_cp(o, i)], [o], [i])
        sent = ext(None, "sent%d" % t)
        calls, used = [], 0
        for mine in masks_from(core, cores, topo):
            trs = []
            for c in mine:
                z = zone(cores.index(c))
                rid, pid, _e = topo.addr(c)
                trs.append(RemoteDMATransfer(dst_ids=[DstId(rid=rid, pnc=pid)], dma_engine_mask=sum(1 << e for e in mine[c]),
                                             remote_sem=T.sem["arr%d" % t], src=T[PW][:, z:z + 16],
                                             dst=T[land][:, 16 * rank:16 * rank + 16]))
                used += len(mine[c])
            calls.append(trs)
        put([("G", (lambda calls, t: lambda: [g.remote_dma_fused(x, local_sem=T.sem["snt%d" % t]) for x in calls])(calls, t),
              300.0)], [sent], [R(PW)], "snt%d" % t, -used, FAR - 300.0)
        arrivals = sum(len(call[core]) for c in cores if c != core for call in masks_from(c, cores, topo) if core in call)
        put([("X", None, 0.0)], [(None, [(land, 16 * p, 16 * p + 16) for p in range(N) if p != rank], [])], [sent],
            "arr%d" % t, -arrivals)
        for h, (lo, hi) in enumerate(HALVES):
            step[0] = "name %d" % h
            pb = R("p1" if h == 0 else "p2", 0, 128)
            z = 2 * lo + 128 if SPLIT[t] else 256 + lo
            mm(pb, R("N4K"), R("Zp", z, z + 128), False, True)
            ts(R("Z", 256 + lo, 256 + hi), pb, 9.0 * S, A.add, 2048.0, A.min)
            mm(R("p6", lo, hi), R("BLK"), R("Z", 256 + lo, 256 + hi), True, True)
            lin(R("key", 256 + lo, 256 + hi), R("p6", lo, hi), 1.0, -RAW)
            if "nm"[h] in SCAN[t]:
                lin(w(W_K, lo, hi), own(R("p6", lo, hi)), 1.0, col(CRAW))
            else:
                wrap(pl("p5", 384, lo, hi), "Z", 256 + lo, 256 + hi)
                lin(w(W_K, lo, hi), pl("p5", 384, lo, hi), 1.0, -RAW)
            tt(w(W_D2, lo, hi), w(W_K, lo, hi), w(W_FB, lo, hi), A.subtract)

        def reborn():
            step[0] = "reborn"
            ts(R("l16"), R(land), ROUND, A.add, ROUND + LIFT + 2048.0, A.subtract)
            if "h" in SCAN[0]:
                mm(R("p4", 0, 128), R("WBH", 0, 128), R("l16"), True, True)
                lin(u(U_H, 0, 128), own(R("p4", 0, 128)), 1.0, col(C2K))
            else:
                wrap(R("p4", 0, 8), "l16", 0, 128, True, True, "WBH")
                lin(u(U_H, 0, 128), R("p4", 0, 8), 1.0, 2048.0)
            at = IND(bdw, u(U_H, 0, 128))
            both(R("zz"), at, (F.Abs, -2.0 * S * S, 2.0 * S), (float(S), A.not_equal, 2.0 * S, A.mult))
            gather(R("old"), at)
            mm(R("p3", 0, 128), R("NI"), R("l16"), True, False)
            mm(R("p3", 0, 128), R("NI"), R("zz"), False, True)
            relu(R("dd"), R("p3", 0, 128), 2048.0)
            tt(at, R("old"), R("dd"), A.subtract)

        def ends(lo, hi):
            if REB[t] == lo // 128:
                reborn()
            step[0] = "ends %d" % lo
            if lo:
                relu(R("ge", 0, 128), R("p7", lo, hi), 0.0)
                scan(R("sg"), R("keep"), R("ge", 0, 128), 0.0, A.mult, A.max)
                go = R("sg", 0, 128, 16, 15)
            else:
                relu(R("gl"), R("p0", 0, 128), 1.0)
                go = R("p1", 128, 136)
                wrap(go, "gl", 0, 128, True, True, "WB0")
            tt(w(W_Y, lo, hi), go, w(W_D2, lo, hi), A.mult)
            add_list(u(U_E, lo, hi), w(W_E, lo, hi), w(W_Y, lo, hi), w(W_FB, lo, hi))
            cp(IND(bdw, u(U_E, lo, hi)), R("arep", lo, hi))
            if lo and REB[t] == 2:
                reborn()

        dedupe(["p0", "p7"], W_K, 256, ends)
        step[0] = "next"
        if t + 1 < RO:
            dma(W("buff", T.buff[:, 0, :]), ext(T.bd[2:128:32, 0:S], "bd"), "Y", "dF", 65536)
            dma(W("buff", T.buff[:, 1, :]), ext(T.bd[18:128:32, 0:S], "bd"), "Y", "dF", 65536)
            if PLAIN:
                dma(R("nat"), ext(T.bd[2:128:16, 0:S], "bd"), "Y", "dN", 131072)
            dma(ext(T.ba[0:128:16, 0:S], "ba"), ext(T.bd[0:128:16, 0:S], "bd"), "Y", "dA", 131072)
            for lo in range(0, 256, CE):
                cp(IND(R("XB1"), u(U_E, lo, lo + CE)), R("xa", lo, lo + CE))
            table = [len(ops) - 1] * TABLE
        else:
            dma(ext(T.y[:, :], "y"), ext(T.bd[0:128:16, 0:S], "bd"), "Y", "dY", 131072)

    return ops


def rank_program(g, core, T, topo):
    if T.rank_of(core) is None:
        return
    if not ORDER:
        ORDER.extend(best_plan([build(g, core, T, topo, m) for m in MODELS]))
    calls = build(g, core, T, topo, MODELS[0])
    ops = [calls[j]["alts"][a][:2] + (calls[j]["rd"], calls[j]["wr"], calls[j]["sem"], calls[j]["cnt"]) for j, a in ORDER]
    queue = {"V": g.vector, "S": g.scalar, "P": g.tensor, "G": g, "Y": g.sync}
    hist = {}
    known = {q: {} for q in queue}
    waits = []
    marked = set()
    for j, (q, call, rd, wr, sem, cnt) in enumerate(ops):
        need = {}
        for regs, writes in ((rd, False), (wr, True)):
            for (name, lo, hi) in regs:
                bank = psum(name)
                for (i, l2, h2, w2) in hist.get(name, []):
                    qi, semi = ops[i][0], ops[i][4]
                    meet = l2 < hi and lo < h2
                    if semi is None and sem is None and qi == q:
                        hit = meet and (w2 or writes) and q != "P"
                    else:
                        hit = (meet and (w2 or writes)) or bank
                    if hit and not (sem is not None and semi == sem):
                        k = semi if semi is not None else qi
                        need[k] = max(need.get(k, -1), i)
        mine_w = []
        if q != "X":
            for k, i in need.items():
                if known[q].get(k, -1) < i:
                    known[q][k] = i
                    mine_w.append((k, i))
                    marked.add(i)
        waits.append(mine_w)
        for regs, writes in ((rd, False), (wr, True)):
            for (name, lo, hi) in regs:
                hist.setdefault(name, []).append((j, lo, hi, writes))
    count = {}
    value = {}
    for j, (q, call, rd, wr, sem, cnt) in enumerate(ops):
        if sem is not None:
            count[sem] = count.get(sem, 0) + abs(cnt)
        elif j in marked:
            count[q] = count.get(q, 0) + 1
            value[j] = count[q]
    for j, (q, call, rd, wr, sem, cnt) in enumerate(ops):
        for (k, i) in waits[j]:
            queue[q].wait_ge(T.sem[k], value[i] if i in value else count[k])
        if call is None:
            continue
        ins = call()
        if sem is not None:
            if cnt > 0:
                ins.then_inc(T.sem[sem], cnt)
        elif j in marked:
            ins.then_inc(T.sem[q], 1)
    for k, v in count.items():
        g.wait_ge(T.sem[k], v)
